import numpy as np
import ml_dtypes


def mxq(x, axis, fmt="e4m3"):
    dtype, down = {"e4m3": (ml_dtypes.float8_e4m3fn, 7), "e5m2": (ml_dtypes.float8_e5m2, 14)}[fmt]
    v = np.moveaxis(np.asarray(x, np.float32).astype(ml_dtypes.bfloat16).astype(np.float64), axis, -1)
    blocks = v.reshape(v.shape[:-1] + (-1, 32))
    amax = np.abs(blocks).max(-1, keepdims=True)
    byte = np.maximum(np.where(amax > 0, np.frexp(amax)[1] - 1 + 127, 0) - down, 1)
    scale = np.exp2(byte - 127.0)
    codes = (blocks / scale).astype(np.float32).astype(dtype).astype(np.float64)
    return np.moveaxis((codes * scale).reshape(v.shape), -1, axis)


WIDE = False


def mx_kscale(k):
    if not WIDE:
        return np.ones(k)
    levels = np.array([10, -10, 5, -5, 0])
    if k % 512:
        return np.exp2(np.random.permutation(np.resize(levels, k // 32))).repeat(32)
    a = np.empty((k // 512, 16))
    for p in range(k // 512):
        a[p, :8] = np.random.permutation(np.resize(levels, 8))
        for g in range(8):
            far = levels[np.abs(levels - a[p, g]) >= 10]
            a[p, g + 8] = far[np.random.randint(len(far))]
    return np.exp2(a.ravel()).repeat(32)


def f64(x):
    return np.asarray(x).astype(np.float64)


def striped(idx):
    return np.tile(np.asarray(idx).reshape(-1, 16).T, (8, 1)).astype(np.uint16)


def unstriped(offs):
    return offs[:16].T.reshape(-1).astype(np.int64)


B, N, T, D, DV, NQ = 2, 512, 2048, 512, 256, 128
PAGE = 64
CAP = 2.0
NEW = 256


def setup_inputs():
    n = np.random.standard_normal
    pages = np.random.permutation(T // PAGE)[:B * N // PAGE]
    idx = (pages[:, None] * PAGE + np.arange(PAGE)[None, :]).reshape(-1)
    s = mx_kscale(D)[:, None]
    u = np.ones(T)
    u[idx] = mx_kscale(B * N)
    r = np.random.uniform(0.5, 2.0, T)
    k = n((D, T)) / s
    v = n((DV, T)) / (u * r)
    new = np.random.permutation(idx.reshape(B, N)[:, -NEW // B:].reshape(-1))
    return {
        "qT": (n((B, D, NQ)) * s * (0.60 / np.sqrt(D))).astype(np.float32),
        "kT": np.where(np.isin(np.arange(T), new)[None, :], n((D, T)), k).astype(np.float32),
        "vT": np.where(np.isin(np.arange(T), new)[None, :], n((DV, T)), v).astype(np.float32),
        "new_kT": k[:, new].astype(np.float32),
        "new_vT": v[:, new].astype(np.float32),
        "vs": np.tile(u * r, (128, 1)).astype(np.float32),
        "offs": striped(idx),
        "slots": striped(new),
    }


def reference(qT, kT, vT, new_kT, new_vT, vs, offs, slots):
    idx = unstriped(offs)
    k = f64(kT)
    k[:, unstriped(slots)] = f64(new_kT)
    v = f64(vT)
    v[:, unstriped(slots)] = f64(new_vT)
    pick = lambda x: x[:, idx].reshape(x.shape[0], B, N).transpose(1, 0, 2)
    q = f64(qT)
    score = mxq(q, 1, "e4m3").transpose(0, 2, 1) @ mxq(pick(k), 1, "e4m3")
    score = CAP * np.tanh(score / CAP)
    m = score.max(-1, keepdims=True)
    p = np.exp(score - m)
    total = p.sum(-1, keepdims=True)
    w = p * pick(f64(vs))[:, :1, :]
    y = mxq(w, 2, "e4m3") @ mxq(pick(v).transpose(0, 2, 1), 1, "e4m3")
    y = y / total
    return y

@@ -1,0 +1,211 @@
+from contextlib import ExitStack
+
+import concourse.mybir as mybir
+from concourse.masks import make_identity
+
+B, N, T, D, DV, NQ, NEW = 2, 512, 2048, 512, 256, 128, 256
+P = 128
+PACK = 4
+FLOPS = 2 * B * NQ * N * (D + DV)
+BYTES = 4 * (B * D * NQ + D * T + DV * T + D * NEW + DV * NEW + T + B * NQ * DV) + 2 * P * (B * N + NEW) // 16
+
+F32 = mybir.dt.float32
+BF16 = mybir.dt.bfloat16
+U32 = mybir.dt.uint32
+U16 = mybir.dt.uint16
+U8 = mybir.dt.uint8
+FP8X4 = mybir.dt.float8_e4m3fn_x4
+ACT = mybir.ActivationFunctionType
+ALU = mybir.AluOpType
+
+PAD = 16
+HALF = N // 2
+IL_SHARES = (("vector", 0, 0, HALF), ("scalar", 1, 32, HALF), ("vector", 1, 0, 32))
+
+
+def tile_attend_x_append256_cap_kernel(tc, qT, kT, vT, new_kT, new_vT, vs, offs, slots, out):
+    nc = tc.nc
+    with ExitStack() as ctx:
+        keep = ctx.enter_context(tc.tile_pool(name="keep", bufs=1))
+        psum = ctx.enter_context(tc.psum_pool(name="psum", bufs=1))
+
+        offs_t = keep.tile([P, B * N // 16], U16, name="offs_t")
+        slots_t = keep.tile([P, NEW // 16], U16, name="slots_t")
+        new_k = keep.tile([P, PACK, NEW], F32, name="new_k")
+        new_v = keep.tile([P, 2, NEW], F32, name="new_v")
+        q_raw = keep.tile([P, B, PACK, NQ], F32, name="q_raw")
+        vs_t = keep.tile([P, T], F32, name="vs_t")
+        kp = [keep.tile([P, T], F32, name=f"kp{t}") for t in range(PACK)]
+        vp = [keep.tile([P, T], F32, name=f"vp{h}") for h in range(2)]
+
+        warm = keep.tile([P, 1], F32, name="warm")
+        nc.gpsimd.memset(warm[:], 0.0)
+        nc.scalar.activation(warm[:], warm[:], ACT.Exp)
+        k_hbm = kT.rearrange("(p j) w -> p j w", j=PACK)
+        nk_hbm = new_kT.rearrange("(p j) w -> p j w", j=PACK)
+        nc.vector.memset(vs_t[:], 0.0)
+        nc.sync.dma_start(slots_t[:], slots)
+        nc.sync.dma_start(new_k[:, 0, :], nk_hbm[:, 0, :])
+        nc.sync.dma_start(kp[0][:], k_hbm[:, 0, :])
+        nc.sync.dma_start(offs_t[:], offs)
+        nc.sync.dma_start(vs_t[0:1, :], vs[0:1, :])
+        nc.sync.dma_start(new_k[:, 1:PACK, :], nk_hbm[:, 1:PACK, :])
+        nc.sync.dma_start(kp[1][:], k_hbm[:, 1, :])
+        nc.sync.dma_start(kp[2][:], k_hbm[:, 2, :])
+        nc.sync.dma_start(new_v[:], new_vT.rearrange("(h p) w -> p h w", p=P))
+        nc.sync.dma_start(vp[0][:], vT[0:P, :])
+        nc.sync.dma_start(kp[3][:], k_hbm[:, 3, :])
+        nc.sync.dma_start(q_raw[:], qT.rearrange("b (p j) w -> p b j w", j=PACK))
+        nc.sync.dma_start(vp[1][:], vT[P : 2 * P, :])
+
+        ident = keep.tile([P, P], F32, name="ident")
+        make_identity(nc, ident[:])
+
+        gk = keep.tile([P, PACK, B, 2, HALF + PAD], BF16, name="gk", align_bytes=64)
+        gv = [keep.tile([P, B, N + PAD], BF16, name=f"gv{h}", align_bytes=64) for h in range(2)]
+
+        def append_k(t):
+            nc.vector.tensor_copy(kp[t][:].indirect(slots_t[:]), new_k[:, t, :])
+
+        def append_v(h):
+            nc.vector.tensor_copy(vp[h][:].indirect(slots_t[:]), new_v[:, h, :])
+
+        vc, vsc = [], []
+
+        def turn_v(h):
+            turned = psum.tile([P, B, 2, P], F32, name=f"v_ps{h}")
+            for b in range(B):
+                words = gv[h][:, b, 0:N].bitcast(F32)
+                for u in range(2):
+                    nc.tensor.transpose(turned[:, b, u, :], words[:, u : N // 2 : 2], ident[:])
+            x = keep.tile([P, B * P * PACK], BF16, name=f"vx{h}", align_bytes=64)
+            nc.scalar.copy(
+                x[:].bitcast(F32).rearrange("p (b e u) -> p b e u", b=B, u=2),
+                turned[:].rearrange("p b u e -> p b e u"),
+            )
+            return x
+
+        def quantise_v(h, x):
+            codes = keep.tile([P, B * P], U32, name=f"vc{h}", align_bytes=64)
+            scale = keep.tile([P, B * P], U8, name=f"vsc{h}", align_bytes=64)
+            nc.vector.quantize_mx(out=codes[:].bitcast(FP8X4), scales=scale[:], in_=x[:])
+            vc.append(codes)
+            vsc.append(scale)
+
+        def gather_k_scalar(t):
+            k16 = keep.tile([P, T], BF16, name=f"k16_{t}")
+            nc.scalar.copy(k16[:], kp[t][:])
+            nc.scalar.activation(gk[:, t, :, :, 0:HALF], k16[:].indirect(offs_t[:]), ACT.Copy)
+
+        append_k(0)
+        gather_k_scalar(0)
+
+        vsg = keep.tile([P, B * N], F32, name="vsg")
+        nc.vector.tensor_copy(vsg[:], vs_t[:].indirect(offs_t[:]))
+        vsT = []
+        for b in range(B):
+            turned = psum.tile([P, PACK, P], F32, name=f"vs_ps{b}", tag=f"y{b}")
+            for t in range(PACK):
+                nc.tensor.transpose(turned[:, t, :], vsg[:, b * N + t : (b + 1) * N : PACK], ident[:])
+            one = keep.tile([P, PACK], F32, name=f"vsT{b}")
+            nc.scalar.copy(one[:], turned[:, :, 0])
+            vsT.append(one)
+
+        append_k(1)
+        gather_k_scalar(1)
+        append_k(2)
+        nc.vector.tensor_copy(gk[:, 2, :, :, 0:HALF], kp[2][:].indirect(offs_t[:]))
+
+        append_v(0)
+        v16 = keep.tile([P, T], BF16, name="v16")
+        nc.scalar.copy(v16[:], vp[0][:])
+        nc.scalar.activation(gv[0][:, :, 0:N], v16[:].indirect(offs_t[:]), ACT.Copy)
+
+        append_k(3)
+        for b in range(B):
+            nc.vector.tensor_copy(gk[:, 3, b, :, 0:HALF], kp[3][:].indirect(offs_t[:, b * N // 16 : (b + 1) * N // 16]))
+
+        qx = keep.tile([P, B, NQ, PACK], BF16, name="qx", align_bytes=64)
+        nc.gpsimd.tensor_scalar(qx[:], q_raw[:].rearrange("p b j w -> p b w j"), 1.0, 0.0, ALU.mult, ALU.add)
+
+        kx = [keep.tile([P, N * PACK], BF16, name=f"kx{b}", align_bytes=64) for b in range(B)]
+        for b in range(B):
+            kx_cols = kx[b][:].rearrange("p (c i t) -> p c t i", i=4, t=PACK)
+            for engine, half, lo, hi in IL_SHARES:
+                engine = nc.vector.tensor_copy if engine == "vector" else nc.scalar.copy
+                engine(
+                    kx_cols[:, (half * HALF + lo) // 4 : (half * HALF + hi) // 4],
+                    gk[:, :, b, half, lo:hi].rearrange("p t (c i) -> p c t i", i=4),
+                )
+        qc = keep.tile([P, B * NQ], U32, name="qc", align_bytes=64)
+        qs = keep.tile([P, B * NQ], U8, name="qs", align_bytes=64)
+        nc.vector.quantize_mx(out=qc[:].bitcast(FP8X4), scales=qs[:], in_=qx[:].rearrange("p b w j -> p (b w j)"))
+
+        scores = []
+        for b in range(B):
+            codes = keep.tile([P, N], U32, name=f"kc{b}", align_bytes=64)
+            scale = keep.tile([P, N], U8, name=f"ksc{b}", align_bytes=64)
+            nc.vector.quantize_mx(out=codes[:].bitcast(FP8X4), scales=scale[:], in_=kx[b][:])
+            acc = psum.tile([P, N], F32, name=f"s_ps{b}")
+            nc.tensor.matmul_mx(
+                out=acc[:],
+                lhsT=qc[:, b * NQ : (b + 1) * NQ].bitcast(FP8X4),
+                lhsT_scale=qs[:, b * NQ : (b + 1) * NQ],
+                rhs=codes[:].bitcast(FP8X4),
+                rhs_scale=scale[:],
+                start=True,
+                stop=True,
+            )
+            scores.append(acc)
+
+        vx0 = turn_v(0)
+        quantise_v(0, vx0)
+        append_v(1)
+
+        th, prob, total = [], [], []
+        for b in range(B):
+            tanh = keep.tile([P, PACK, P], F32, name=f"th{b}")
+            nc.scalar.activation(tanh[:], scores[b][:].rearrange("q (s t) -> q t s", t=PACK), ACT.Tanh, scale=0.5)
+            minus_m = keep.tile([P, 1], F32, name=f"nm{b}")
+            scaled = keep.tile([P, N], F32, name=f"scaled{b}")
+            nc.vector.tensor_scalar(scaled[:], tanh[:].rearrange("q t s -> q (t s)"), -2.0, None, ALU.mult, ALU.min, accum_out=minus_m[:])
+            p = keep.tile([P, PACK, P], F32, name=f"p{b}")
+            row_sum = keep.tile([P, 1], F32, name=f"l{b}")
+            nc.scalar.activation(p[:], tanh[:], ACT.Exp, bias=minus_m[:], scale=2.0, accum_out=row_sum[:])
+            prob.append(p)
+            total.append(row_sum)
+        nc.vector.tensor_copy(gv[1][:, :, 0:N], vp[1][:].indirect(offs_t[:]))
+        vx1 = turn_v(1)
+
+        for b in range(B):
+            turned = psum.tile([P, PACK, P], F32, name=f"w_ps{b}")
+            for t in range(PACK):
+                nc.tensor.transpose(turned[:, t, :], prob[b][:, t, :], ident[:])
+            wx = keep.tile([P, NQ, PACK], BF16, name=f"wx{b}", align_bytes=64)
+            nc.vector.tensor_tensor(
+                wx[:],
+                turned[:].rearrange("p t q -> p q t"),
+                vsT[b][:].unsqueeze(1).to_broadcast([P, NQ, PACK]),
+                ALU.mult,
+            )
+            codes = keep.tile([P, NQ], U32, name=f"wc{b}", align_bytes=64)
+            scale = keep.tile([P, NQ], U8, name=f"wsc{b}", align_bytes=64)
+            nc.vector.quantize_mx(out=codes[:].bitcast(FP8X4), scales=scale[:], in_=wx[:].rearrange("p q t -> p (q t)"))
+            inv = keep.tile([P, 1], F32, name=f"inv{b}")
+            nc.vector.reciprocal(inv[:], total[b][:])
+            if b == 0:
+                quantise_v(1, vx1)
+            y = psum.tile([P, DV], F32, name=f"y_ps{b}", tag=f"y{b}")
+            for h in range(2):
+                nc.tensor.matmul_mx(
+                    out=y[:, h * P : (h + 1) * P],
+                    lhsT=codes[:].bitcast(FP8X4),
+                    lhsT_scale=scale[:],
+                    rhs=vc[h][:, b * P : (b + 1) * P].bitcast(FP8X4),
+                    rhs_scale=vsc[h][:, b * P : (b + 1) * P],
+                    start=True,
+                    stop=True,
+                )
+            y_sb = keep.tile([P, DV], F32, name=f"y{b}")
+            nc.scalar.activation(y_sb[:], y[:], ACT.Copy, scale=inv[:])
+            nc.sync.dma_start(out[b], y_sb[:])

@@ -19,8 +19,6 @@ ACT = mybir.ActivationFunctionType
 ALU = mybir.AluOpType
 
 PAD = 16
-HALF = N // 2
-IL_SHARES = (("vector", 0, 0, HALF), ("scalar", 1, 32, HALF), ("vector", 1, 0, 32))
 
 
 def tile_attend_x_append256_cap_kernel(tc, qT, kT, vT, new_kT, new_vT, vs, offs, slots, out):
@@ -61,7 +59,11 @@ def tile_attend_x_append256_cap_kernel(tc, qT, kT, vT, new_kT, new_vT, vs, offs,
         ident = keep.tile([P, P], F32, name="ident")
         make_identity(nc, ident[:])
 
-        gk = keep.tile([P, PACK, B, 2, HALF + PAD], BF16, name="gk", align_bytes=64)
+        gk = [keep.tile([P, 2, N, 2], BF16, name=f"gk{b}", align_bytes=64) for b in range(B)]
+
+        def seq_offs(b):
+            return offs_t[:, b * N // 16 : (b + 1) * N // 16]
+
         gv = [keep.tile([P, B, N + PAD], BF16, name=f"gv{h}", align_bytes=64) for h in range(2)]
 
         def append_k(t):
@@ -95,7 +97,12 @@ def tile_attend_x_append256_cap_kernel(tc, qT, kT, vT, new_kT, new_vT, vs, offs,
         def gather_k_scalar(t):
             k16 = keep.tile([P, T], BF16, name=f"k16_{t}")
             nc.scalar.copy(k16[:], kp[t][:])
-            nc.scalar.activation(gk[:, t, :, :, 0:HALF], k16[:].indirect(offs_t[:]), ACT.Copy)
+            for b in range(B):
+                nc.scalar.activation(gk[b][:, t // 2, :, t % 2], k16[:].indirect(seq_offs(b)), ACT.Copy)
+
+        def gather_k_vector(t):
+            for b in range(B):
+                nc.vector.tensor_copy(gk[b][:, t // 2, :, t % 2], kp[t][:].indirect(seq_offs(b)))
 
         append_k(0)
         gather_k_scalar(0)
@@ -114,7 +121,7 @@ def tile_attend_x_append256_cap_kernel(tc, qT, kT, vT, new_kT, new_vT, vs, offs,
         append_k(1)
         gather_k_scalar(1)
         append_k(2)
-        nc.vector.tensor_copy(gk[:, 2, :, :, 0:HALF], kp[2][:].indirect(offs_t[:]))
+        gather_k_vector(2)
 
         append_v(0)
         v16 = keep.tile([P, T], BF16, name="v16")
@@ -122,21 +129,17 @@ def tile_attend_x_append256_cap_kernel(tc, qT, kT, vT, new_kT, new_vT, vs, offs,
         nc.scalar.activation(gv[0][:, :, 0:N], v16[:].indirect(offs_t[:]), ACT.Copy)
 
         append_k(3)
-        for b in range(B):
-            nc.vector.tensor_copy(gk[:, 3, b, :, 0:HALF], kp[3][:].indirect(offs_t[:, b * N // 16 : (b + 1) * N // 16]))
+        gather_k_vector(3)
 
         qx = keep.tile([P, B, NQ, PACK], BF16, name="qx", align_bytes=64)
         nc.gpsimd.tensor_scalar(qx[:], q_raw[:].rearrange("p b j w -> p b w j"), 1.0, 0.0, ALU.mult, ALU.add)
 
         kx = [keep.tile([P, N * PACK], BF16, name=f"kx{b}", align_bytes=64) for b in range(B)]
         for b in range(B):
-            kx_cols = kx[b][:].rearrange("p (c i t) -> p c t i", i=4, t=PACK)
-            for engine, half, lo, hi in IL_SHARES:
-                engine = nc.vector.tensor_copy if engine == "vector" else nc.scalar.copy
-                engine(
-                    kx_cols[:, (half * HALF + lo) // 4 : (half * HALF + hi) // 4],
-                    gk[:, :, b, half, lo:hi].rearrange("p t (c i) -> p c t i", i=4),
-                )
+            nc.scalar.copy(
+                kx[b][:].bitcast(F32).rearrange("p (s u) -> p s u", u=2),
+                gk[b][:].rearrange("p u s t -> p (u s t)").bitcast(F32).rearrange("p (u s) -> p s u", u=2),
+            )
         qc = keep.tile([P, B * NQ], U32, name="qc", align_bytes=64)
         qs = keep.tile([P, B * NQ], U8, name="qs", align_bytes=64)
         nc.vector.quantize_mx(out=qc[:].bitcast(FP8X4), scales=qs[:], in_=qx[:].rearrange("p b w j -> p (b w j)"))

@@ -29,7 +29,8 @@ def tile_attend_x_append256_cap_kernel(tc, qT, kT, vT, new_kT, new_vT, vs, offs,
 
         offs_t = keep.tile([P, B * N // 16], U16, name="offs_t")
         slots_t = keep.tile([P, NEW // 16], U16, name="slots_t")
-        new_k = keep.tile([P, PACK, NEW], F32, name="new_k")
+        new_k0 = keep.tile([P, NEW], F32, name="new_k0")
+        new_k = keep.tile([P, PACK - 1, NEW], F32, name="new_k", tag="new_k", align_bytes=64)
         new_v = keep.tile([P, 2, NEW], F32, name="new_v")
         q_raw = keep.tile([P, B, PACK, NQ], F32, name="q_raw")
         vs_t = keep.tile([P, T], F32, name="vs_t")
@@ -43,18 +44,18 @@ def tile_attend_x_append256_cap_kernel(tc, qT, kT, vT, new_kT, new_vT, vs, offs,
         nk_hbm = new_kT.rearrange("(p j) w -> p j w", j=PACK)
         nc.vector.memset(vs_t[:], 0.0)
         nc.sync.dma_start(slots_t[:], slots)
-        nc.sync.dma_start(new_k[:, 0, :], nk_hbm[:, 0, :])
+        nc.sync.dma_start(new_k0[:], nk_hbm[:, 0, :])
         nc.sync.dma_start(kp[0][:], k_hbm[:, 0, :])
         nc.sync.dma_start(offs_t[:], offs)
         nc.sync.dma_start(vs_t[0:1, :], vs[0:1, :])
-        nc.sync.dma_start(new_k[:, 1:PACK, :], nk_hbm[:, 1:PACK, :])
+        nc.sync.dma_start(new_k[:], nk_hbm[:, 1:PACK, :])
         nc.sync.dma_start(kp[1][:], k_hbm[:, 1, :])
         nc.sync.dma_start(kp[2][:], k_hbm[:, 2, :])
         nc.sync.dma_start(new_v[:], new_vT.rearrange("(h p) w -> p h w", p=P))
         nc.sync.dma_start(vp[0][:], vT[0:P, :])
+        nc.sync.dma_start(vp[1][:], vT[P : 2 * P, :])
         nc.sync.dma_start(kp[3][:], k_hbm[:, 3, :])
         nc.sync.dma_start(q_raw[:], qT.rearrange("b (p j) w -> p b j w", j=PACK))
-        nc.sync.dma_start(vp[1][:], vT[P : 2 * P, :])
 
         ident = keep.tile([P, P], F32, name="ident")
         make_identity(nc, ident[:])
@@ -64,10 +65,10 @@ def tile_attend_x_append256_cap_kernel(tc, qT, kT, vT, new_kT, new_vT, vs, offs,
         def seq_offs(b):
             return offs_t[:, b * N // 16 : (b + 1) * N // 16]
 
-        gv = [keep.tile([P, B, N + PAD], BF16, name=f"gv{h}", align_bytes=64) for h in range(2)]
+        gv = [keep.tile([P, B, N + PAD], BF16, name="gv0", align_bytes=64)]
 
         def append_k(t):
-            nc.vector.tensor_copy(kp[t][:].indirect(slots_t[:]), new_k[:, t, :])
+            nc.vector.tensor_copy(kp[t][:].indirect(slots_t[:]), new_k0[:] if t == 0 else new_k[:, t - 1, :])
 
         def append_v(h):
             nc.vector.tensor_copy(vp[h][:].indirect(slots_t[:]), new_v[:, h, :])
@@ -87,8 +88,8 @@ def tile_attend_x_append256_cap_kernel(tc, qT, kT, vT, new_kT, new_vT, vs, offs,
             )
             return x
 
-        def quantise_v(h, x):
-            codes = keep.tile([P, B * P], U32, name=f"vc{h}", align_bytes=64)
+        def quantise_v(h, x, tag):
+            codes = keep.tile([P, B * P], U32, name=f"vc{h}", tag=tag, align_bytes=64)
             scale = keep.tile([P, B * P], U8, name=f"vsc{h}", align_bytes=64)
             nc.vector.quantize_mx(out=codes[:].bitcast(FP8X4), scales=scale[:], in_=x[:])
             vc.append(codes)
@@ -128,8 +129,12 @@ def tile_attend_x_append256_cap_kernel(tc, qT, kT, vT, new_kT, new_vT, vs, offs,
         nc.scalar.copy(v16[:], vp[0][:])
         nc.scalar.activation(gv[0][:, :, 0:N], v16[:].indirect(offs_t[:]), ACT.Copy)
 
+        append_v(1)
+        vx0 = turn_v(0)
         append_k(3)
         gather_k_vector(3)
+        gv.append(keep.tile([P, B, N + PAD], BF16, name="gv1", tag="new_k", align_bytes=64))
+        nc.vector.tensor_copy(gv[1][:, :, 0:N], vp[1][:].indirect(offs_t[:]))
 
         qx = keep.tile([P, B, NQ, PACK], BF16, name="qx", align_bytes=64)
         nc.gpsimd.tensor_scalar(qx[:], q_raw[:].rearrange("p b j w -> p b w j"), 1.0, 0.0, ALU.mult, ALU.add)
@@ -146,7 +151,7 @@ def tile_attend_x_append256_cap_kernel(tc, qT, kT, vT, new_kT, new_vT, vs, offs,
 
         scores = []
         for b in range(B):
-            codes = keep.tile([P, N], U32, name=f"kc{b}", align_bytes=64)
+            codes = keep.tile([P, N], U32, name=f"kc{b}", tag=f"kc{b}", align_bytes=64)
             scale = keep.tile([P, N], U8, name=f"ksc{b}", align_bytes=64)
             nc.vector.quantize_mx(out=codes[:].bitcast(FP8X4), scales=scale[:], in_=kx[b][:])
             acc = psum.tile([P, N], F32, name=f"s_ps{b}")
@@ -161,24 +166,22 @@ def tile_attend_x_append256_cap_kernel(tc, qT, kT, vT, new_kT, new_vT, vs, offs,
             )
             scores.append(acc)
 
-        vx0 = turn_v(0)
-        quantise_v(0, vx0)
-        append_v(1)
+        vx1 = turn_v(1)
+        quantise_v(0, vx0, "kc0")
 
         th, prob, total = [], [], []
         for b in range(B):
             tanh = keep.tile([P, PACK, P], F32, name=f"th{b}")
             nc.scalar.activation(tanh[:], scores[b][:].rearrange("q (s t) -> q t s", t=PACK), ACT.Tanh, scale=0.5)
             minus_m = keep.tile([P, 1], F32, name=f"nm{b}")
-            scaled = keep.tile([P, N], F32, name=f"scaled{b}")
+            scaled = keep.tile([P, N], F32, name=f"scaled{b}", tag=f"scaled{b}", align_bytes=64)
             nc.vector.tensor_scalar(scaled[:], tanh[:].rearrange("q t s -> q (t s)"), -2.0, None, ALU.mult, ALU.min, accum_out=minus_m[:])
             p = keep.tile([P, PACK, P], F32, name=f"p{b}")
             row_sum = keep.tile([P, 1], F32, name=f"l{b}")
             nc.scalar.activation(p[:], tanh[:], ACT.Exp, bias=minus_m[:], scale=2.0, accum_out=row_sum[:])
             prob.append(p)
             total.append(row_sum)
-        nc.vector.tensor_copy(gv[1][:, :, 0:N], vp[1][:].indirect(offs_t[:]))
-        vx1 = turn_v(1)
+        quantise_v(1, vx1, "scaled1")
 
         for b in range(B):
             turned = psum.tile([P, PACK, P], F32, name=f"w_ps{b}")
@@ -196,8 +199,6 @@ def tile_attend_x_append256_cap_kernel(tc, qT, kT, vT, new_kT, new_vT, vs, offs,
             nc.vector.quantize_mx(out=codes[:].bitcast(FP8X4), scales=scale[:], in_=wx[:].rearrange("p q t -> p (q t)"))
             inv = keep.tile([P, 1], F32, name=f"inv{b}")
             nc.vector.reciprocal(inv[:], total[b][:])
-            if b == 0:
-                quantise_v(1, vx1)
             y = psum.tile([P, DV], F32, name=f"y_ps{b}", tag=f"y{b}")
             for h in range(2):
                 nc.tensor.matmul_mx(

@@ -19,6 +19,7 @@ ACT = mybir.ActivationFunctionType
 ALU = mybir.AluOpType
 
 PAD = 16
+SPLIT = 256
 
 
 def tile_attend_x_append256_cap_kernel(tc, qT, kT, vT, new_kT, new_vT, vs, offs, slots, out):
@@ -60,7 +61,7 @@ def tile_attend_x_append256_cap_kernel(tc, qT, kT, vT, new_kT, new_vT, vs, offs,
         ident = keep.tile([P, P], F32, name="ident")
         make_identity(nc, ident[:])
 
-        gk = [keep.tile([P, 2, N, 2], BF16, name=f"gk{b}", align_bytes=64) for b in range(B)]
+        gk = keep.tile([P, PACK, B, N + PAD], BF16, name="gk", tag="gk", align_bytes=64)
 
         def seq_offs(b):
             return offs_t[:, b * N // 16 : (b + 1) * N // 16]
@@ -75,13 +76,13 @@ def tile_attend_x_append256_cap_kernel(tc, qT, kT, vT, new_kT, new_vT, vs, offs,
 
         vc, vsc = [], []
 
-        def turn_v(h):
+        def turn_v(h, tag):
             turned = psum.tile([P, B, 2, P], F32, name=f"v_ps{h}")
             for b in range(B):
                 words = gv[h][:, b, 0:N].bitcast(F32)
                 for u in range(2):
                     nc.tensor.transpose(turned[:, b, u, :], words[:, u : N // 2 : 2], ident[:])
-            x = keep.tile([P, B * P * PACK], BF16, name=f"vx{h}", align_bytes=64)
+            x = keep.tile([P, B * P * PACK], BF16, name=f"vx{h}", tag=tag, align_bytes=64)
             nc.scalar.copy(
                 x[:].bitcast(F32).rearrange("p (b e u) -> p b e u", b=B, u=2),
                 turned[:].rearrange("p b u e -> p b e u"),
@@ -98,12 +99,8 @@ def tile_attend_x_append256_cap_kernel(tc, qT, kT, vT, new_kT, new_vT, vs, offs,
         def gather_k_scalar(t):
             k16 = keep.tile([P, T], BF16, name=f"k16_{t}")
             nc.scalar.copy(k16[:], kp[t][:])
-            for b in range(B):
-                nc.scalar.activation(gk[b][:, t // 2, :, t % 2], k16[:].indirect(seq_offs(b)), ACT.Copy)
+            nc.scalar.activation(gk[:, t, :, 0:N], k16[:].indirect(offs_t[:]), ACT.Copy)
 
-        def gather_k_vector(t):
-            for b in range(B):
-                nc.vector.tensor_copy(gk[b][:, t // 2, :, t % 2], kp[t][:].indirect(seq_offs(b)))
 
         append_k(0)
         gather_k_scalar(0)
@@ -122,7 +119,7 @@ def tile_attend_x_append256_cap_kernel(tc, qT, kT, vT, new_kT, new_vT, vs, offs,
         append_k(1)
         gather_k_scalar(1)
         append_k(2)
-        gather_k_vector(2)
+        nc.vector.tensor_copy(gk[:, 2, :, 0:N], kp[2][:].indirect(offs_t[:]))
 
         append_v(0)
         v16 = keep.tile([P, T], BF16, name="v16")
@@ -130,9 +127,9 @@ def tile_attend_x_append256_cap_kernel(tc, qT, kT, vT, new_kT, new_vT, vs, offs,
         nc.scalar.activation(gv[0][:, :, 0:N], v16[:].indirect(offs_t[:]), ACT.Copy)
 
         append_v(1)
-        vx0 = turn_v(0)
         append_k(3)
-        gather_k_vector(3)
+        for b in range(B):
+            nc.vector.tensor_copy(gk[:, 3, b, 0:N], kp[3][:].indirect(seq_offs(b)))
         gv.append(keep.tile([P, B, N + PAD], BF16, name="gv1", tag="new_k", align_bytes=64))
         nc.vector.tensor_copy(gv[1][:, :, 0:N], vp[1][:].indirect(offs_t[:]))
 
@@ -140,10 +137,10 @@ def tile_attend_x_append256_cap_kernel(tc, qT, kT, vT, new_kT, new_vT, vs, offs,
         nc.gpsimd.tensor_scalar(qx[:], q_raw[:].rearrange("p b j w -> p b w j"), 1.0, 0.0, ALU.mult, ALU.add)
 
         kx = [keep.tile([P, N * PACK], BF16, name=f"kx{b}", align_bytes=64) for b in range(B)]
-        for b in range(B):
-            nc.scalar.copy(
-                kx[b][:].bitcast(F32).rearrange("p (s u) -> p s u", u=2),
-                gk[b][:].rearrange("p u s t -> p (u s t)").bitcast(F32).rearrange("p (u s) -> p s u", u=2),
+        for engine, b, lo, hi in ((nc.scalar.copy, 0, 0, N), (nc.scalar.copy, 1, 0, SPLIT), (nc.vector.tensor_copy, 1, SPLIT, N)):
+            engine(
+                kx[b][:].rearrange("p (c i t) -> p c t i", i=4, t=PACK)[:, lo // 4 : hi // 4],
+                gk[:, :, b, lo:hi].rearrange("p t (c i) -> p c t i", i=4),
             )
         qc = keep.tile([P, B * NQ], U32, name="qc", align_bytes=64)
         qs = keep.tile([P, B * NQ], U8, name="qs", align_bytes=64)
@@ -166,7 +163,8 @@ def tile_attend_x_append256_cap_kernel(tc, qT, kT, vT, new_kT, new_vT, vs, offs,
             )
             scores.append(acc)
 
-        vx1 = turn_v(1)
+        vx0 = turn_v(0, "gk")
+        vx1 = turn_v(1, "vx1")
         quantise_v(0, vx0, "kc0")
 
         th, prob, total = [], [], []

@@ -134,7 +134,10 @@ def tile_attend_x_append256_cap_kernel(tc, qT, kT, vT, new_kT, new_vT, vs, offs,
         nc.vector.tensor_copy(gv[1][:, :, 0:N], vp[1][:].indirect(offs_t[:]))
 
         qx = keep.tile([P, B, NQ, PACK], BF16, name="qx", align_bytes=64)
-        nc.gpsimd.tensor_scalar(qx[:], q_raw[:].rearrange("p b j w -> p b w j"), 1.0, 0.0, ALU.mult, ALU.add)
+        nc.vector.tensor_copy(
+            qx[:].rearrange("p b (c i) j -> p b c j i", i=4),
+            q_raw[:].rearrange("p b j (c i) -> p b c j i", i=4),
+        )
 
         kx = [keep.tile([P, N * PACK], BF16, name=f"kx{b}", align_bytes=64) for b in range(B)]
         for engine, b, lo, hi in ((nc.scalar.copy, 0, 0, N), (nc.scalar.copy, 1, 0, SPLIT), (nc.vector.tensor_copy, 1, SPLIT, N)):

@@ -19,7 +19,6 @@ ACT = mybir.ActivationFunctionType
 ALU = mybir.AluOpType
 
 PAD = 16
-SPLIT = 256
 
 
 def tile_attend_x_append256_cap_kernel(tc, qT, kT, vT, new_kT, new_vT, vs, offs, slots, out):
@@ -30,13 +29,12 @@ def tile_attend_x_append256_cap_kernel(tc, qT, kT, vT, new_kT, new_vT, vs, offs,
 
         offs_t = keep.tile([P, B * N // 16], U16, name="offs_t")
         slots_t = keep.tile([P, NEW // 16], U16, name="slots_t")
-        new_k0 = keep.tile([P, NEW], F32, name="new_k0")
-        new_k = keep.tile([P, PACK - 1, NEW], F32, name="new_k", tag="new_k", align_bytes=64)
-        new_v = keep.tile([P, 2, NEW], F32, name="new_v")
-        q_raw = keep.tile([P, B, PACK, NQ], F32, name="q_raw")
+        new_k = [keep.tile([P, NEW], F32, name=f"new_k{t}") for t in range(PACK)]
+        new_v = [keep.tile([P, NEW], F32, name=f"new_v{h}", tag=f"after_v{h}", align_bytes=64) for h in range(2)]
+        q_raw = keep.tile([P, B, PACK, NQ], F32, name="q_raw", tag="after_q", align_bytes=64)
         vs_t = keep.tile([P, T], F32, name="vs_t")
         kp = [keep.tile([P, T], F32, name=f"kp{t}") for t in range(PACK)]
-        vp = [keep.tile([P, T], F32, name=f"vp{h}") for h in range(2)]
+        vp = [keep.tile([P, T], F32, name=f"vp{h}", tag=f"after_gather{h}", align_bytes=64) for h in range(2)]
 
         warm = keep.tile([P, 1], F32, name="warm")
         nc.gpsimd.memset(warm[:], 0.0)
@@ -45,44 +43,41 @@ def tile_attend_x_append256_cap_kernel(tc, qT, kT, vT, new_kT, new_vT, vs, offs,
         nk_hbm = new_kT.rearrange("(p j) w -> p j w", j=PACK)
         nc.vector.memset(vs_t[:], 0.0)
         nc.sync.dma_start(slots_t[:], slots)
-        nc.sync.dma_start(new_k0[:], nk_hbm[:, 0, :])
-        nc.sync.dma_start(kp[0][:], k_hbm[:, 0, :])
-        nc.sync.dma_start(offs_t[:], offs)
-        nc.sync.dma_start(vs_t[0:1, :], vs[0:1, :])
-        nc.sync.dma_start(new_k[:], nk_hbm[:, 1:PACK, :])
-        nc.sync.dma_start(kp[1][:], k_hbm[:, 1, :])
-        nc.sync.dma_start(kp[2][:], k_hbm[:, 2, :])
-        nc.sync.dma_start(new_v[:], new_vT.rearrange("(h p) w -> p h w", p=P))
-        nc.sync.dma_start(vp[0][:], vT[0:P, :])
-        nc.sync.dma_start(vp[1][:], vT[P : 2 * P, :])
-        nc.sync.dma_start(kp[3][:], k_hbm[:, 3, :])
+        for t in range(PACK):
+            nc.sync.dma_start(new_k[t][:], nk_hbm[:, t, :])
+            nc.sync.dma_start(kp[t][:], k_hbm[:, t, :])
+            if t == 0:
+                nc.sync.dma_start(offs_t[:], offs)
+                nc.sync.dma_start(vs_t[0:1, :], vs[0:1, :])
         nc.sync.dma_start(q_raw[:], qT.rearrange("b (p j) w -> p b j w", j=PACK))
+        for h in range(2):
+            nc.sync.dma_start(new_v[h][:], new_vT[h * P : (h + 1) * P, :])
+            nc.sync.dma_start(vp[h][:], vT[h * P : (h + 1) * P, :])
 
         ident = keep.tile([P, P], F32, name="ident")
         make_identity(nc, ident[:])
 
-        gk = keep.tile([P, PACK, B, N + PAD], BF16, name="gk", tag="gk", align_bytes=64)
+        gk = keep.tile([P, PACK, B, N + PAD], BF16, name="gk", align_bytes=64)
+        gv = [keep.tile([P, B, N + PAD], BF16, name=f"gv{h}", align_bytes=64) for h in range(2)]
 
         def seq_offs(b):
             return offs_t[:, b * N // 16 : (b + 1) * N // 16]
 
-        gv = [keep.tile([P, B, N + PAD], BF16, name="gv0", align_bytes=64)]
-
         def append_k(t):
-            nc.vector.tensor_copy(kp[t][:].indirect(slots_t[:]), new_k0[:] if t == 0 else new_k[:, t - 1, :])
+            nc.vector.tensor_copy(kp[t][:].indirect(slots_t[:]), new_k[t][:])
 
         def append_v(h):
-            nc.vector.tensor_copy(vp[h][:].indirect(slots_t[:]), new_v[:, h, :])
+            nc.vector.tensor_copy(vp[h][:].indirect(slots_t[:]), new_v[h][:])
 
         vc, vsc = [], []
 
-        def turn_v(h, tag):
+        def turn_v(h):
             turned = psum.tile([P, B, 2, P], F32, name=f"v_ps{h}")
             for b in range(B):
                 words = gv[h][:, b, 0:N].bitcast(F32)
                 for u in range(2):
                     nc.tensor.transpose(turned[:, b, u, :], words[:, u : N // 2 : 2], ident[:])
-            x = keep.tile([P, B * P * PACK], BF16, name=f"vx{h}", tag=tag, align_bytes=64)
+            x = keep.tile([P, B * P * PACK], BF16, name=f"vx{h}", align_bytes=64)
             nc.scalar.copy(
                 x[:].bitcast(F32).rearrange("p (b e u) -> p b e u", b=B, u=2),
                 turned[:].rearrange("p b u e -> p b e u"),
@@ -100,7 +95,6 @@ def tile_attend_x_append256_cap_kernel(tc, qT, kT, vT, new_kT, new_vT, vs, offs,
             k16 = keep.tile([P, T], BF16, name=f"k16_{t}")
             nc.scalar.copy(k16[:], kp[t][:])
             nc.scalar.activation(gk[:, t, :, 0:N], k16[:].indirect(offs_t[:]), ACT.Copy)
-
 
         append_k(0)
         gather_k_scalar(0)
@@ -120,40 +114,30 @@ def tile_attend_x_append256_cap_kernel(tc, qT, kT, vT, new_kT, new_vT, vs, offs,
         gather_k_scalar(1)
         append_k(2)
         nc.vector.tensor_copy(gk[:, 2, :, 0:N], kp[2][:].indirect(offs_t[:]))
-
-        append_v(0)
-        v16 = keep.tile([P, T], BF16, name="v16")
-        nc.scalar.copy(v16[:], vp[0][:])
-        nc.scalar.activation(gv[0][:, :, 0:N], v16[:].indirect(offs_t[:]), ACT.Copy)
-
-        append_v(1)
         append_k(3)
         for b in range(B):
             nc.vector.tensor_copy(gk[:, 3, b, 0:N], kp[3][:].indirect(seq_offs(b)))
-        gv.append(keep.tile([P, B, N + PAD], BF16, name="gv1", tag="new_k", align_bytes=64))
-        nc.vector.tensor_copy(gv[1][:, :, 0:N], vp[1][:].indirect(offs_t[:]))
 
         qx = keep.tile([P, B, NQ, PACK], BF16, name="qx", align_bytes=64)
-        nc.vector.tensor_copy(
+        nc.scalar.copy(
             qx[:].rearrange("p b (c i) j -> p b c j i", i=4),
             q_raw[:].rearrange("p b j (c i) -> p b c j i", i=4),
         )
-
-        kx = [keep.tile([P, N * PACK], BF16, name=f"kx{b}", align_bytes=64) for b in range(B)]
-        for engine, b, lo, hi in ((nc.scalar.copy, 0, 0, N), (nc.scalar.copy, 1, 0, SPLIT), (nc.vector.tensor_copy, 1, SPLIT, N)):
-            engine(
-                kx[b][:].rearrange("p (c i t) -> p c t i", i=4, t=PACK)[:, lo // 4 : hi // 4],
-                gk[:, :, b, lo:hi].rearrange("p t (c i) -> p c t i", i=4),
-            )
         qc = keep.tile([P, B * NQ], U32, name="qc", align_bytes=64)
         qs = keep.tile([P, B * NQ], U8, name="qs", align_bytes=64)
         nc.vector.quantize_mx(out=qc[:].bitcast(FP8X4), scales=qs[:], in_=qx[:].rearrange("p b w j -> p (b w j)"))
 
-        scores = []
+        kx = keep.tile([P, B, N * PACK], BF16, name="kx", tag="after_q", align_bytes=64)
         for b in range(B):
-            codes = keep.tile([P, N], U32, name=f"kc{b}", tag=f"kc{b}", align_bytes=64)
+            nc.scalar.copy(
+                kx[:, b, :].rearrange("p (c i t) -> p c t i", i=4, t=PACK),
+                gk[:, :, b, 0:N].rearrange("p t (c i) -> p c t i", i=4),
+            )
+
+        def score(b, tag):
+            codes = keep.tile([P, N], U32, name=f"kc{b}", tag=tag, align_bytes=64)
             scale = keep.tile([P, N], U8, name=f"ksc{b}", align_bytes=64)
-            nc.vector.quantize_mx(out=codes[:].bitcast(FP8X4), scales=scale[:], in_=kx[b][:])
+            nc.vector.quantize_mx(out=codes[:].bitcast(FP8X4), scales=scale[:], in_=kx[:, b, :])
             acc = psum.tile([P, N], F32, name=f"s_ps{b}")
             nc.tensor.matmul_mx(
                 out=acc[:],
@@ -164,25 +148,30 @@ def tile_attend_x_append256_cap_kernel(tc, qT, kT, vT, new_kT, new_vT, vs, offs,
                 start=True,
                 stop=True,
             )
-            scores.append(acc)
+            return acc
 
-        vx0 = turn_v(0, "gk")
-        vx1 = turn_v(1, "vx1")
-        quantise_v(0, vx0, "kc0")
+        append_v(0)
+        scores = [score(0, "after_v0")]
+        nc.vector.tensor_copy(gv[0][:, :, 0:N], vp[0][:].indirect(offs_t[:]))
+        scores.append(score(1, "after_gather0"))
+        vx0 = turn_v(0)
+        append_v(1)
 
-        th, prob, total = [], [], []
+        prob, total = [], []
         for b in range(B):
             tanh = keep.tile([P, PACK, P], F32, name=f"th{b}")
             nc.scalar.activation(tanh[:], scores[b][:].rearrange("q (s t) -> q t s", t=PACK), ACT.Tanh, scale=0.5)
             minus_m = keep.tile([P, 1], F32, name=f"nm{b}")
-            scaled = keep.tile([P, N], F32, name=f"scaled{b}", tag=f"scaled{b}", align_bytes=64)
+            scaled = keep.tile([P, N], F32, name=f"scaled{b}", tag="after_v1", align_bytes=64)
             nc.vector.tensor_scalar(scaled[:], tanh[:].rearrange("q t s -> q (t s)"), -2.0, None, ALU.mult, ALU.min, accum_out=minus_m[:])
             p = keep.tile([P, PACK, P], F32, name=f"p{b}")
             row_sum = keep.tile([P, 1], F32, name=f"l{b}")
             nc.scalar.activation(p[:], tanh[:], ACT.Exp, bias=minus_m[:], scale=2.0, accum_out=row_sum[:])
             prob.append(p)
             total.append(row_sum)
-        quantise_v(1, vx1, "scaled1")
+            nc.vector.tensor_copy(gv[1][:, b, 0:N], vp[1][:].indirect(seq_offs(b)))
+        quantise_v(0, vx0, "after_v1")
+        vx1 = turn_v(1)
 
         for b in range(B):
             turned = psum.tile([P, PACK, P], F32, name=f"w_ps{b}")
@@ -200,6 +189,8 @@ def tile_attend_x_append256_cap_kernel(tc, qT, kT, vT, new_kT, new_vT, vs, offs,
             nc.vector.quantize_mx(out=codes[:].bitcast(FP8X4), scales=scale[:], in_=wx[:].rearrange("p q t -> p (q t)"))
             inv = keep.tile([P, 1], F32, name=f"inv{b}")
             nc.vector.reciprocal(inv[:], total[b][:])
+            if b == 0:
+                quantise_v(1, vx1, "vc1")
             y = psum.tile([P, DV], F32, name=f"y_ps{b}", tag=f"y{b}")
             for h in range(2):
                 nc.tensor.matmul_mx(

@@ -19,6 +19,7 @@ ACT = mybir.ActivationFunctionType
 ALU = mybir.AluOpType
 
 PAD = 16
+SPLIT = 288
 
 
 def tile_attend_x_append256_cap_kernel(tc, qT, kT, vT, new_kT, new_vT, vs, offs, slots, out):
@@ -34,7 +35,7 @@ def tile_attend_x_append256_cap_kernel(tc, qT, kT, vT, new_kT, new_vT, vs, offs,
         q_raw = keep.tile([P, B, PACK, NQ], F32, name="q_raw", tag="after_q", align_bytes=64)
         vs_t = keep.tile([P, T], F32, name="vs_t")
         kp = [keep.tile([P, T], F32, name=f"kp{t}") for t in range(PACK)]
-        vp = [keep.tile([P, T], F32, name=f"vp{h}", tag=f"after_gather{h}", align_bytes=64) for h in range(2)]
+        vp = [keep.tile([P, T], F32, name=f"vp{h}") for h in range(2)]
 
         warm = keep.tile([P, 1], F32, name="warm")
         nc.gpsimd.memset(warm[:], 0.0)
@@ -69,27 +70,13 @@ def tile_attend_x_append256_cap_kernel(tc, qT, kT, vT, new_kT, new_vT, vs, offs,
         def append_v(h):
             nc.vector.tensor_copy(vp[h][:].indirect(slots_t[:]), new_v[h][:])
 
-        vc, vsc = [], []
-
         def turn_v(h):
             turned = psum.tile([P, B, 2, P], F32, name=f"v_ps{h}")
             for b in range(B):
                 words = gv[h][:, b, 0:N].bitcast(F32)
                 for u in range(2):
                     nc.tensor.transpose(turned[:, b, u, :], words[:, u : N // 2 : 2], ident[:])
-            x = keep.tile([P, B * P * PACK], BF16, name=f"vx{h}", align_bytes=64)
-            nc.scalar.copy(
-                x[:].bitcast(F32).rearrange("p (b e u) -> p b e u", b=B, u=2),
-                turned[:].rearrange("p b u e -> p b e u"),
-            )
-            return x
-
-        def quantise_v(h, x, tag):
-            codes = keep.tile([P, B * P], U32, name=f"vc{h}", tag=tag, align_bytes=64)
-            scale = keep.tile([P, B * P], U8, name=f"vsc{h}", align_bytes=64)
-            nc.vector.quantize_mx(out=codes[:].bitcast(FP8X4), scales=scale[:], in_=x[:])
-            vc.append(codes)
-            vsc.append(scale)
+            return turned
 
         def gather_k_scalar(t):
             k16 = keep.tile([P, T], BF16, name=f"k16_{t}")
@@ -123,27 +110,32 @@ def tile_attend_x_append256_cap_kernel(tc, qT, kT, vT, new_kT, new_vT, vs, offs,
             qx[:].rearrange("p b (c i) j -> p b c j i", i=4),
             q_raw[:].rearrange("p b j (c i) -> p b c j i", i=4),
         )
-        qc = keep.tile([P, B * NQ], U32, name="qc", align_bytes=64)
-        qs = keep.tile([P, B * NQ], U8, name="qs", align_bytes=64)
-        nc.vector.quantize_mx(out=qc[:].bitcast(FP8X4), scales=qs[:], in_=qx[:].rearrange("p b w j -> p (b w j)"))
 
         kx = keep.tile([P, B, N * PACK], BF16, name="kx", tag="after_q", align_bytes=64)
         for b in range(B):
             nc.scalar.copy(
-                kx[:, b, :].rearrange("p (c i t) -> p c t i", i=4, t=PACK),
-                gk[:, :, b, 0:N].rearrange("p t (c i) -> p c t i", i=4),
+                kx[:, b, 0 : SPLIT * PACK].rearrange("p (c i t) -> p c t i", i=4, t=PACK),
+                gk[:, :, b, 0:SPLIT].rearrange("p t (c i) -> p c t i", i=4),
+            )
+            nc.gpsimd.tensor_scalar(
+                kx[:, b, SPLIT * PACK :].rearrange("p (s t) -> p s t", t=PACK),
+                gk[:, :, b, SPLIT:N].rearrange("p t s -> p s t"),
+                1.0,
+                0.0,
+                ALU.mult,
+                ALU.add,
             )
 
-        def score(b, tag):
-            codes = keep.tile([P, N], U32, name=f"kc{b}", tag=tag, align_bytes=64)
+        def score(b):
+            codes = qk_codes[:, B * NQ + b * N : B * NQ + (b + 1) * N]
             scale = keep.tile([P, N], U8, name=f"ksc{b}", align_bytes=64)
-            nc.vector.quantize_mx(out=codes[:].bitcast(FP8X4), scales=scale[:], in_=kx[:, b, :])
+            nc.vector.quantize_mx(out=codes.bitcast(FP8X4), scales=scale[:], in_=kx[:, b, :])
             acc = psum.tile([P, N], F32, name=f"s_ps{b}")
             nc.tensor.matmul_mx(
                 out=acc[:],
-                lhsT=qc[:, b * NQ : (b + 1) * NQ].bitcast(FP8X4),
+                lhsT=qk_codes[:, b * NQ : (b + 1) * NQ].bitcast(FP8X4),
                 lhsT_scale=qs[:, b * NQ : (b + 1) * NQ],
-                rhs=codes[:].bitcast(FP8X4),
+                rhs=codes.bitcast(FP8X4),
                 rhs_scale=scale[:],
                 start=True,
                 stop=True,
@@ -151,28 +143,38 @@ def tile_attend_x_append256_cap_kernel(tc, qT, kT, vT, new_kT, new_vT, vs, offs,
             return acc
 
         append_v(0)
-        scores = [score(0, "after_v0")]
-        nc.vector.tensor_copy(gv[0][:, :, 0:N], vp[0][:].indirect(offs_t[:]))
-        scores.append(score(1, "after_gather0"))
-        vx0 = turn_v(0)
-        append_v(1)
-
-        prob, total = [], []
+        v16 = keep.tile([P, T], BF16, name="v16")
+        nc.scalar.copy(v16[:], vp[0][:])
+        qk_codes = keep.tile([P, B * (NQ + N)], U32, name="qk_codes", tag="after_v0", align_bytes=64)
+        qs = keep.tile([P, B * NQ], U8, name="qs", align_bytes=64)
+        nc.vector.quantize_mx(out=qk_codes[:, 0 : B * NQ].bitcast(FP8X4), scales=qs[:], in_=qx[:].rearrange("p b w j -> p (b w j)"))
+        scores = [score(b) for b in range(B)]
+        capped = []
         for b in range(B):
-            tanh = keep.tile([P, PACK, P], F32, name=f"th{b}")
+            tanh = keep.tile([P, PACK, P], F32, name=f"th{b}", tag=f"after_exp{b}", align_bytes=64)
             nc.scalar.activation(tanh[:], scores[b][:].rearrange("q (s t) -> q t s", t=PACK), ACT.Tanh, scale=0.5)
-            minus_m = keep.tile([P, 1], F32, name=f"nm{b}")
-            scaled = keep.tile([P, N], F32, name=f"scaled{b}", tag="after_v1", align_bytes=64)
-            nc.vector.tensor_scalar(scaled[:], tanh[:].rearrange("q t s -> q (t s)"), -2.0, None, ALU.mult, ALU.min, accum_out=minus_m[:])
-            p = keep.tile([P, PACK, P], F32, name=f"p{b}")
-            row_sum = keep.tile([P, 1], F32, name=f"l{b}")
-            nc.scalar.activation(p[:], tanh[:], ACT.Exp, bias=minus_m[:], scale=2.0, accum_out=row_sum[:])
-            prob.append(p)
-            total.append(row_sum)
-            nc.vector.tensor_copy(gv[1][:, b, 0:N], vp[1][:].indirect(seq_offs(b)))
-        quantise_v(0, vx0, "after_v1")
-        vx1 = turn_v(1)
+            capped.append(tanh)
+        nc.scalar.activation(gv[0][:, :, 0:N], v16[:].indirect(offs_t[:]), ACT.Copy)
+        append_v(1)
+        nc.vector.tensor_copy(gv[1][:, :, 0:N], vp[1][:].indirect(offs_t[:]))
+        v_turned = {h: turn_v(h) for h in (1, 0)}
 
+        scaled = keep.tile([P, B, N], F32, name="scaled", tag="after_v1", align_bytes=64)
+        total = keep.tile([P, B], F32, name="total")
+        prob = []
+        for b in range(B):
+            minus_m = keep.tile([P, 1], F32, name=f"nm{b}")
+            nc.vector.tensor_scalar(scaled[:, b, :], capped[b][:].rearrange("q t s -> q (t s)"), -2.0, None, ALU.mult, ALU.min, accum_out=minus_m[:])
+            p = keep.tile([P, PACK, P], F32, name=f"p{b}")
+            nc.scalar.activation(p[:], capped[b][:], ACT.Exp, bias=minus_m[:], scale=2.0, accum_out=total[:, b : b + 1])
+            prob.append(p)
+
+        vx = keep.tile([P, B, DV * PACK], BF16, name="vx", tag="after_exp1", align_bytes=64)
+        vx_words = vx[:].rearrange("p b x -> p (b x)").bitcast(F32).rearrange("p (b h e u) -> p b h e u", b=B, h=2, u=2)
+        for h in (1, 0):
+            nc.scalar.copy(vx_words[:, :, h], v_turned[h][:].rearrange("p b u e -> p b e u"))
+
+        wc, wsc = [], []
         for b in range(B):
             turned = psum.tile([P, PACK, P], F32, name=f"w_ps{b}")
             for t in range(PACK):
@@ -187,21 +189,28 @@ def tile_attend_x_append256_cap_kernel(tc, qT, kT, vT, new_kT, new_vT, vs, offs,
             codes = keep.tile([P, NQ], U32, name=f"wc{b}", align_bytes=64)
             scale = keep.tile([P, NQ], U8, name=f"wsc{b}", align_bytes=64)
             nc.vector.quantize_mx(out=codes[:].bitcast(FP8X4), scales=scale[:], in_=wx[:].rearrange("p q t -> p (q t)"))
-            inv = keep.tile([P, 1], F32, name=f"inv{b}")
-            nc.vector.reciprocal(inv[:], total[b][:])
-            if b == 0:
-                quantise_v(1, vx1, "vc1")
+            wc.append(codes)
+            wsc.append(scale)
+        inv = keep.tile([P, B], F32, name="inv")
+        nc.vector.reciprocal(inv[:], total[:])
+        vc = keep.tile([P, B * DV], U32, name="vc", align_bytes=64)
+        vsc = keep.tile([P, B * DV], U8, name="vsc", align_bytes=64)
+        nc.vector.quantize_mx(out=vc[:].bitcast(FP8X4), scales=vsc[:], in_=vx[:].rearrange("p b x -> p (b x)"))
+
+        for b in range(B):
             y = psum.tile([P, DV], F32, name=f"y_ps{b}", tag=f"y{b}")
-            for h in range(2):
-                nc.tensor.matmul_mx(
-                    out=y[:, h * P : (h + 1) * P],
-                    lhsT=codes[:].bitcast(FP8X4),
-                    lhsT_scale=scale[:],
-                    rhs=vc[h][:, b * P : (b + 1) * P].bitcast(FP8X4),
-                    rhs_scale=vsc[h][:, b * P : (b + 1) * P],
-                    start=True,
-                    stop=True,
-                )
+            nc.tensor.matmul_mx(
+                out=y[:],
+                lhsT=wc[b][:].bitcast(FP8X4),
+                lhsT_scale=wsc[b][:],
+                rhs=vc[:, b * DV : (b + 1) * DV].bitcast(FP8X4),
+                rhs_scale=vsc[:, b * DV : (b + 1) * DV],
+                start=True,
+                stop=True,
+            )
             y_sb = keep.tile([P, DV], F32, name=f"y{b}")
-            nc.scalar.activation(y_sb[:], y[:], ACT.Copy, scale=inv[:])
+            if b == 0:
+                nc.scalar.activation(y_sb[:], y[:], ACT.Copy, scale=inv[:, b : b + 1])
+            else:
+                nc.vector.tensor_scalar(y_sb[:], y[:], inv[:, b : b + 1], None, ALU.mult)
             nc.sync.dma_start(out[b], y_sb[:])

@@ -30,7 +30,10 @@ def tile_attend_x_append256_cap_kernel(tc, qT, kT, vT, new_kT, new_vT, vs, offs,
 
         offs_t = keep.tile([P, B * N // 16], U16, name="offs_t")
         slots_t = keep.tile([P, NEW // 16], U16, name="slots_t")
-        new_k = [keep.tile([P, NEW], F32, name=f"new_k{t}") for t in range(PACK)]
+        gk = keep.tile([P, PACK * B * (N + PAD)], BF16, name="gk", align_bytes=64)
+        planes = gk[:].rearrange("p (t b s) -> p t b s", t=PACK, b=B)
+        new_k = [keep.tile([P, NEW], F32, name=f"new_k{t}") for t in range(PACK - 1)]
+        new_k = [tile[:] for tile in new_k] + [planes[:, 2, 1, 0:N].bitcast(F32)]
         new_v = [keep.tile([P, NEW], F32, name=f"new_v{h}", tag=f"after_v{h}", align_bytes=64) for h in range(2)]
         q_raw = keep.tile([P, B, PACK, NQ], F32, name="q_raw", tag="after_q", align_bytes=64)
         vs_t = keep.tile([P, T], F32, name="vs_t")
@@ -45,7 +48,7 @@ def tile_attend_x_append256_cap_kernel(tc, qT, kT, vT, new_kT, new_vT, vs, offs,
         nc.vector.memset(vs_t[:], 0.0)
         nc.sync.dma_start(slots_t[:], slots)
         for t in range(PACK):
-            nc.sync.dma_start(new_k[t][:], nk_hbm[:, t, :])
+            nc.sync.dma_start(new_k[t], nk_hbm[:, t, :])
             nc.sync.dma_start(kp[t][:], k_hbm[:, t, :])
             if t == 0:
                 nc.sync.dma_start(offs_t[:], offs)
@@ -58,30 +61,29 @@ def tile_attend_x_append256_cap_kernel(tc, qT, kT, vT, new_kT, new_vT, vs, offs,
         ident = keep.tile([P, P], F32, name="ident")
         make_identity(nc, ident[:])
 
-        gk = keep.tile([P, PACK, B, N + PAD], BF16, name="gk", align_bytes=64)
         gv = [keep.tile([P, B, N + PAD], BF16, name=f"gv{h}", align_bytes=64) for h in range(2)]
 
         def seq_offs(b):
             return offs_t[:, b * N // 16 : (b + 1) * N // 16]
 
         def append_k(t):
-            nc.vector.tensor_copy(kp[t][:].indirect(slots_t[:]), new_k[t][:])
+            nc.vector.tensor_copy(kp[t][:].indirect(slots_t[:]), new_k[t])
 
         def append_v(h):
             nc.vector.tensor_copy(vp[h][:].indirect(slots_t[:]), new_v[h][:])
 
-        def turn_v(h):
-            turned = psum.tile([P, B, 2, P], F32, name=f"v_ps{h}")
-            for b in range(B):
+        def turn_v(b):
+            turned = psum.tile([P, 2, 2, P], F32, name=f"v_ps{b}")
+            for h in range(2):
                 words = gv[h][:, b, 0:N].bitcast(F32)
                 for u in range(2):
-                    nc.tensor.transpose(turned[:, b, u, :], words[:, u : N // 2 : 2], ident[:])
+                    nc.tensor.transpose(turned[:, h, u, :], words[:, u : N // 2 : 2], ident[:])
             return turned
 
         def gather_k_scalar(t):
             k16 = keep.tile([P, T], BF16, name=f"k16_{t}")
             nc.scalar.copy(k16[:], kp[t][:])
-            nc.scalar.activation(gk[:, t, :, 0:N], k16[:].indirect(offs_t[:]), ACT.Copy)
+            nc.scalar.activation(planes[:, t, :, 0:N], k16[:].indirect(offs_t[:]), ACT.Copy)
 
         append_k(0)
         gather_k_scalar(0)
@@ -100,26 +102,23 @@ def tile_attend_x_append256_cap_kernel(tc, qT, kT, vT, new_kT, new_vT, vs, offs,
         append_k(1)
         gather_k_scalar(1)
         append_k(2)
-        nc.vector.tensor_copy(gk[:, 2, :, 0:N], kp[2][:].indirect(offs_t[:]))
+        nc.vector.tensor_copy(planes[:, 2, 0, 0:N], kp[2][:].indirect(seq_offs(0)))
         append_k(3)
-        for b in range(B):
-            nc.vector.tensor_copy(gk[:, 3, b, 0:N], kp[3][:].indirect(seq_offs(b)))
+        for t, b in ((3, 0), (2, 1), (3, 1)):
+            nc.vector.tensor_copy(planes[:, t, b, 0:N], kp[t][:].indirect(seq_offs(b)))
 
         qx = keep.tile([P, B, NQ, PACK], BF16, name="qx", align_bytes=64)
-        nc.scalar.copy(
-            qx[:].rearrange("p b (c i) j -> p b c j i", i=4),
-            q_raw[:].rearrange("p b j (c i) -> p b c j i", i=4),
-        )
+        nc.gpsimd.tensor_scalar(qx[:], q_raw[:].rearrange("p b j w -> p b w j"), 1.0, 0.0, ALU.mult, ALU.add)
 
         kx = keep.tile([P, B, N * PACK], BF16, name="kx", tag="after_q", align_bytes=64)
         for b in range(B):
             nc.scalar.copy(
                 kx[:, b, 0 : SPLIT * PACK].rearrange("p (c i t) -> p c t i", i=4, t=PACK),
-                gk[:, :, b, 0:SPLIT].rearrange("p t (c i) -> p c t i", i=4),
+                planes[:, :, b, 0:SPLIT].rearrange("p t (c i) -> p c t i", i=4),
             )
             nc.gpsimd.tensor_scalar(
                 kx[:, b, SPLIT * PACK :].rearrange("p (s t) -> p s t", t=PACK),
-                gk[:, :, b, SPLIT:N].rearrange("p t s -> p s t"),
+                planes[:, :, b, SPLIT:N].rearrange("p t s -> p s t"),
                 1.0,
                 0.0,
                 ALU.mult,
@@ -156,8 +155,8 @@ def tile_attend_x_append256_cap_kernel(tc, qT, kT, vT, new_kT, new_vT, vs, offs,
             capped.append(tanh)
         nc.scalar.activation(gv[0][:, :, 0:N], v16[:].indirect(offs_t[:]), ACT.Copy)
         append_v(1)
-        nc.vector.tensor_copy(gv[1][:, :, 0:N], vp[1][:].indirect(offs_t[:]))
-        v_turned = {h: turn_v(h) for h in (1, 0)}
+        nc.vector.tensor_copy(gv[1][:, 0, 0:N], vp[1][:].indirect(seq_offs(0)))
+        v_turned = [turn_v(0)]
 
         scaled = keep.tile([P, B, N], F32, name="scaled", tag="after_v1", align_bytes=64)
         total = keep.tile([P, B], F32, name="total")
@@ -168,49 +167,47 @@ def tile_attend_x_append256_cap_kernel(tc, qT, kT, vT, new_kT, new_vT, vs, offs,
             p = keep.tile([P, PACK, P], F32, name=f"p{b}")
             nc.scalar.activation(p[:], capped[b][:], ACT.Exp, bias=minus_m[:], scale=2.0, accum_out=total[:, b : b + 1])
             prob.append(p)
+        nc.vector.tensor_copy(gv[1][:, 1, 0:N], vp[1][:].indirect(seq_offs(1)))
 
-        vx = keep.tile([P, B, DV * PACK], BF16, name="vx", tag="after_exp1", align_bytes=64)
-        vx_words = vx[:].rearrange("p b x -> p (b x)").bitcast(F32).rearrange("p (b h e u) -> p b h e u", b=B, h=2, u=2)
-        for h in (1, 0):
-            nc.scalar.copy(vx_words[:, :, h], v_turned[h][:].rearrange("p b u e -> p b e u"))
-
-        wc, wsc = [], []
+        wx = []
         for b in range(B):
             turned = psum.tile([P, PACK, P], F32, name=f"w_ps{b}")
             for t in range(PACK):
                 nc.tensor.transpose(turned[:, t, :], prob[b][:, t, :], ident[:])
-            wx = keep.tile([P, NQ, PACK], BF16, name=f"wx{b}", align_bytes=64)
+            weights = keep.tile([P, NQ, PACK], BF16, name=f"wx{b}", align_bytes=64)
             nc.vector.tensor_tensor(
-                wx[:],
+                weights[:],
                 turned[:].rearrange("p t q -> p q t"),
                 vsT[b][:].unsqueeze(1).to_broadcast([P, NQ, PACK]),
                 ALU.mult,
             )
-            codes = keep.tile([P, NQ], U32, name=f"wc{b}", align_bytes=64)
-            scale = keep.tile([P, NQ], U8, name=f"wsc{b}", align_bytes=64)
-            nc.vector.quantize_mx(out=codes[:].bitcast(FP8X4), scales=scale[:], in_=wx[:].rearrange("p q t -> p (q t)"))
-            wc.append(codes)
-            wsc.append(scale)
+            wx.append(weights)
+        v_turned.append(turn_v(1))
+        vx = keep.tile([P, B, DV * PACK], BF16, name="vx", tag="after_exp1", align_bytes=64)
         inv = keep.tile([P, B], F32, name="inv")
         nc.vector.reciprocal(inv[:], total[:])
-        vc = keep.tile([P, B * DV], U32, name="vc", align_bytes=64)
-        vsc = keep.tile([P, B * DV], U8, name="vsc", align_bytes=64)
-        nc.vector.quantize_mx(out=vc[:].bitcast(FP8X4), scales=vsc[:], in_=vx[:].rearrange("p b x -> p (b x)"))
 
         for b in range(B):
+            nc.scalar.copy(
+                vx[:, b, :].bitcast(F32).rearrange("p (h e u) -> p h e u", h=2, u=2),
+                v_turned[b][:].rearrange("p h u e -> p h e u"),
+            )
+            wc = keep.tile([P, NQ], U32, name=f"wc{b}", align_bytes=64)
+            wsc = keep.tile([P, NQ], U8, name=f"wsc{b}", align_bytes=64)
+            nc.vector.quantize_mx(out=wc[:].bitcast(FP8X4), scales=wsc[:], in_=wx[b][:].rearrange("p q t -> p (q t)"))
+            vc = keep.tile([P, DV], U32, name=f"vc{b}", align_bytes=64)
+            vsc = keep.tile([P, DV], U8, name=f"vsc{b}", align_bytes=64)
+            nc.vector.quantize_mx(out=vc[:].bitcast(FP8X4), scales=vsc[:], in_=vx[:, b, :])
             y = psum.tile([P, DV], F32, name=f"y_ps{b}", tag=f"y{b}")
             nc.tensor.matmul_mx(
                 out=y[:],
-                lhsT=wc[b][:].bitcast(FP8X4),
-                lhsT_scale=wsc[b][:],
-                rhs=vc[:, b * DV : (b + 1) * DV].bitcast(FP8X4),
-                rhs_scale=vsc[:, b * DV : (b + 1) * DV],
+                lhsT=wc[:].bitcast(FP8X4),
+                lhsT_scale=wsc[:],
+                rhs=vc[:].bitcast(FP8X4),
+                rhs_scale=vsc[:],
                 start=True,
                 stop=True,
             )
             y_sb = keep.tile([P, DV], F32, name=f"y{b}")
-            if b == 0:
-                nc.scalar.activation(y_sb[:], y[:], ACT.Copy, scale=inv[:, b : b + 1])
-            else:
-                nc.vector.tensor_scalar(y_sb[:], y[:], inv[:, b : b + 1], None, ALU.mult)
+            nc.scalar.activation(y_sb[:], y[:], ACT.Copy, scale=inv[:, b : b + 1])
             nc.sync.dma_start(out[b], y_sb[:])

@@ -108,7 +108,11 @@ def tile_attend_x_append256_cap_kernel(tc, qT, kT, vT, new_kT, new_vT, vs, offs,
             nc.vector.tensor_copy(planes[:, t, b, 0:N], kp[t][:].indirect(seq_offs(b)))
 
         qx = keep.tile([P, B, NQ, PACK], BF16, name="qx", align_bytes=64)
-        nc.gpsimd.tensor_scalar(qx[:], q_raw[:].rearrange("p b j w -> p b w j"), 1.0, 0.0, ALU.mult, ALU.add)
+        nc.gpsimd.tensor_scalar(qx[:, 0], q_raw[:, 0].rearrange("p j w -> p w j"), 1.0, 0.0, ALU.mult, ALU.add)
+        nc.scalar.copy(
+            qx[:, 1].rearrange("p (c i) j -> p c j i", i=4),
+            q_raw[:, 1].rearrange("p j (c i) -> p c j i", i=4),
+        )
 
         kx = keep.tile([P, B, N * PACK], BF16, name="kx", tag="after_q", align_bytes=64)
         for b in range(B):

@@ -61,7 +61,11 @@ def tile_attend_x_append256_cap_kernel(tc, qT, kT, vT, new_kT, new_vT, vs, offs,
         ident = keep.tile([P, P], F32, name="ident")
         make_identity(nc, ident[:])
 
-        gv = [keep.tile([P, B, N + PAD], BF16, name=f"gv{h}", align_bytes=64) for h in range(2)]
+        gv0 = keep.tile([P, 2, B * N // 2], BF16, name="gv0", align_bytes=64)
+        gv1 = keep.tile([P, B, N + PAD], BF16, name="gv1", align_bytes=64)
+
+        def dealt_v1(b):
+            return gv1[:, b, 0:N].rearrange("p (u s e) -> p s u e", u=2, e=2)
 
         def seq_offs(b):
             return offs_t[:, b * N // 16 : (b + 1) * N // 16]
@@ -74,10 +78,10 @@ def tile_attend_x_append256_cap_kernel(tc, qT, kT, vT, new_kT, new_vT, vs, offs,
 
         def turn_v(b):
             turned = psum.tile([P, 2, 2, P], F32, name=f"v_ps{b}")
-            for h in range(2):
-                words = gv[h][:, b, 0:N].bitcast(F32)
-                for u in range(2):
-                    nc.tensor.transpose(turned[:, h, u, :], words[:, u : N // 2 : 2], ident[:])
+            for u in range(2):
+                nc.tensor.transpose(turned[:, 0, u, :], gv0[:, u, b * N // 2 : (b + 1) * N // 2].bitcast(F32), ident[:])
+            for u in range(2):
+                nc.tensor.transpose(turned[:, 1, u, :], gv1[:, b, u * N // 2 : (u + 1) * N // 2].bitcast(F32), ident[:])
             return turned
 
         def gather_k_scalar(t):
@@ -155,11 +159,11 @@ def tile_attend_x_append256_cap_kernel(tc, qT, kT, vT, new_kT, new_vT, vs, offs,
         capped = []
         for b in range(B):
             tanh = keep.tile([P, PACK, P], F32, name=f"th{b}", tag=f"after_exp{b}", align_bytes=64)
-            nc.scalar.activation(tanh[:], scores[b][:].rearrange("q (s t) -> q t s", t=PACK), ACT.Tanh, scale=0.5)
+            nc.scalar.activation(tanh[:].rearrange("q t s -> q s t"), scores[b][:].rearrange("q (s t) -> q s t", t=PACK), ACT.Tanh, scale=0.5)
             capped.append(tanh)
-        nc.scalar.activation(gv[0][:, :, 0:N], v16[:].indirect(offs_t[:]), ACT.Copy)
+        nc.scalar.activation(gv0[:].rearrange("p u (s e) -> p s u e", e=2), v16[:].indirect(offs_t[:]), ACT.Copy)
         append_v(1)
-        nc.vector.tensor_copy(gv[1][:, 0, 0:N], vp[1][:].indirect(seq_offs(0)))
+        nc.vector.tensor_copy(dealt_v1(0), vp[1][:].indirect(seq_offs(0)))
         v_turned = [turn_v(0)]
 
         scaled = keep.tile([P, B, N], F32, name="scaled", tag="after_v1", align_bytes=64)
@@ -171,7 +175,7 @@ def tile_attend_x_append256_cap_kernel(tc, qT, kT, vT, new_kT, new_vT, vs, offs,
             p = keep.tile([P, PACK, P], F32, name=f"p{b}")
             nc.scalar.activation(p[:], capped[b][:], ACT.Exp, bias=minus_m[:], scale=2.0, accum_out=total[:, b : b + 1])
             prob.append(p)
-        nc.vector.tensor_copy(gv[1][:, 1, 0:N], vp[1][:].indirect(seq_offs(1)))
+        nc.vector.tensor_copy(dealt_v1(1), vp[1][:].indirect(seq_offs(1)))
 
         wx = []
         for b in range(B):

@@ -62,10 +62,11 @@ def tile_attend_x_append256_cap_kernel(tc, qT, kT, vT, new_kT, new_vT, vs, offs,
         make_identity(nc, ident[:])
 
         gv0 = keep.tile([P, 2, B * N // 2], BF16, name="gv0", align_bytes=64)
-        gv1 = keep.tile([P, B, N + PAD], BF16, name="gv1", align_bytes=64)
+        gv1 = []
 
-        def dealt_v1(b):
-            return gv1[:, b, 0:N].rearrange("p (u s e) -> p s u e", u=2, e=2)
+        def gather_v1(b, tag):
+            gv1.append(keep.tile([P, N], BF16, name=f"gv1_{b}", tag=tag, align_bytes=64))
+            nc.vector.tensor_copy(gv1[b][:].rearrange("p (u s e) -> p s u e", u=2, e=2), vp[1][:].indirect(seq_offs(b)))
 
         def seq_offs(b):
             return offs_t[:, b * N // 16 : (b + 1) * N // 16]
@@ -76,13 +77,10 @@ def tile_attend_x_append256_cap_kernel(tc, qT, kT, vT, new_kT, new_vT, vs, offs,
         def append_v(h):
             nc.vector.tensor_copy(vp[h][:].indirect(slots_t[:]), new_v[h][:])
 
-        def turn_v(b):
-            turned = psum.tile([P, 2, 2, P], F32, name=f"v_ps{b}")
+        def turn_v(turned, b, h):
             for u in range(2):
-                nc.tensor.transpose(turned[:, 0, u, :], gv0[:, u, b * N // 2 : (b + 1) * N // 2].bitcast(F32), ident[:])
-            for u in range(2):
-                nc.tensor.transpose(turned[:, 1, u, :], gv1[:, b, u * N // 2 : (u + 1) * N // 2].bitcast(F32), ident[:])
-            return turned
+                run = gv0[:, u, b * N // 2 : (b + 1) * N // 2] if h == 0 else gv1[b][:, u * N // 2 : (u + 1) * N // 2]
+                nc.tensor.transpose(turned[:, u, :], run.bitcast(F32), ident[:])
 
         def gather_k_scalar(t):
             k16 = keep.tile([P, T], BF16, name=f"k16_{t}")
@@ -137,7 +135,7 @@ def tile_attend_x_append256_cap_kernel(tc, qT, kT, vT, new_kT, new_vT, vs, offs,
             codes = qk_codes[:, B * NQ + b * N : B * NQ + (b + 1) * N]
             scale = keep.tile([P, N], U8, name=f"ksc{b}", align_bytes=64)
             nc.vector.quantize_mx(out=codes.bitcast(FP8X4), scales=scale[:], in_=kx[:, b, :])
-            acc = psum.tile([P, N], F32, name=f"s_ps{b}")
+            acc = psum.tile([P, N], F32, name=f"s_ps{b}", tag=f"s{b}")
             nc.tensor.matmul_mx(
                 out=acc[:],
                 lhsT=qk_codes[:, b * NQ : (b + 1) * NQ].bitcast(FP8X4),
@@ -159,12 +157,14 @@ def tile_attend_x_append256_cap_kernel(tc, qT, kT, vT, new_kT, new_vT, vs, offs,
         capped = []
         for b in range(B):
             tanh = keep.tile([P, PACK, P], F32, name=f"th{b}", tag=f"after_exp{b}", align_bytes=64)
-            nc.scalar.activation(tanh[:].rearrange("q t s -> q s t"), scores[b][:].rearrange("q (s t) -> q s t", t=PACK), ACT.Tanh, scale=0.5)
+            nc.scalar.activation(tanh[:], scores[b][:].rearrange("q (s t) -> q t s", t=PACK), ACT.Tanh, scale=0.5)
             capped.append(tanh)
         nc.scalar.activation(gv0[:].rearrange("p u (s e) -> p s u e", e=2), v16[:].indirect(offs_t[:]), ACT.Copy)
         append_v(1)
-        nc.vector.tensor_copy(dealt_v1(0), vp[1][:].indirect(seq_offs(0)))
-        v_turned = [turn_v(0)]
+        gather_v1(0, "gv1_0")
+        v_first = psum.tile([P, 2, 2, P], F32, name="v_first", tag="v_first")
+        for h in range(2):
+            turn_v(v_first[:, h], 0, h)
 
         scaled = keep.tile([P, B, N], F32, name="scaled", tag="after_v1", align_bytes=64)
         total = keep.tile([P, B], F32, name="total")
@@ -175,7 +175,7 @@ def tile_attend_x_append256_cap_kernel(tc, qT, kT, vT, new_kT, new_vT, vs, offs,
             p = keep.tile([P, PACK, P], F32, name=f"p{b}")
             nc.scalar.activation(p[:], capped[b][:], ACT.Exp, bias=minus_m[:], scale=2.0, accum_out=total[:, b : b + 1])
             prob.append(p)
-        nc.vector.tensor_copy(dealt_v1(1), vp[1][:].indirect(seq_offs(1)))
+        gather_v1(1, "after_exp0")
 
         wx = []
         for b in range(B):
@@ -190,32 +190,52 @@ def tile_attend_x_append256_cap_kernel(tc, qT, kT, vT, new_kT, new_vT, vs, offs,
                 ALU.mult,
             )
             wx.append(weights)
-        v_turned.append(turn_v(1))
         vx = keep.tile([P, B, DV * PACK], BF16, name="vx", tag="after_exp1", align_bytes=64)
         inv = keep.tile([P, B], F32, name="inv")
         nc.vector.reciprocal(inv[:], total[:])
 
-        for b in range(B):
-            nc.scalar.copy(
-                vx[:, b, :].bitcast(F32).rearrange("p (h e u) -> p h e u", h=2, u=2),
-                v_turned[b][:].rearrange("p h u e -> p h e u"),
-            )
-            wc = keep.tile([P, NQ], U32, name=f"wc{b}", align_bytes=64)
-            wsc = keep.tile([P, NQ], U8, name=f"wsc{b}", align_bytes=64)
-            nc.vector.quantize_mx(out=wc[:].bitcast(FP8X4), scales=wsc[:], in_=wx[b][:].rearrange("p q t -> p (q t)"))
-            vc = keep.tile([P, DV], U32, name=f"vc{b}", align_bytes=64)
-            vsc = keep.tile([P, DV], U8, name=f"vsc{b}", align_bytes=64)
-            nc.vector.quantize_mx(out=vc[:].bitcast(FP8X4), scales=vsc[:], in_=vx[:, b, :])
-            y = psum.tile([P, DV], F32, name=f"y_ps{b}", tag=f"y{b}")
+        def quantise(name, src, width):
+            codes = keep.tile([P, width], U32, name=f"{name}_c", align_bytes=64)
+            scale = keep.tile([P, width], U8, name=f"{name}_s", align_bytes=64)
+            nc.vector.quantize_mx(out=codes[:].bitcast(FP8X4), scales=scale[:], in_=src)
+            return codes, scale
+
+        def product(y, w, v):
             nc.tensor.matmul_mx(
                 out=y[:],
-                lhsT=wc[:].bitcast(FP8X4),
-                lhsT_scale=wsc[:],
-                rhs=vc[:].bitcast(FP8X4),
-                rhs_scale=vsc[:],
+                lhsT=w[0][:].bitcast(FP8X4),
+                lhsT_scale=w[1][:],
+                rhs=v[0][:].bitcast(FP8X4),
+                rhs_scale=v[1][:],
                 start=True,
                 stop=True,
             )
-            y_sb = keep.tile([P, DV], F32, name=f"y{b}")
-            nc.scalar.activation(y_sb[:], y[:], ACT.Copy, scale=inv[:, b : b + 1])
-            nc.sync.dma_start(out[b], y_sb[:])
+
+        nc.scalar.copy(
+            vx[:, 0, :].bitcast(F32).rearrange("p (h e u) -> p h e u", h=2, u=2),
+            v_first[:].rearrange("p h u e -> p h e u"),
+        )
+        v_last = [psum.tile([P, 2, P], F32, name=f"v_last{h}", tag=("v_first", "s0")[h]) for h in range(2)]
+        for h in range(2):
+            turn_v(v_last[h][:], 1, h)
+        for h in range(2):
+            nc.scalar.copy(
+                vx[:, 1, h * P * PACK : (h + 1) * P * PACK].bitcast(F32).rearrange("p (e u) -> p e u", u=2),
+                v_last[h][:].rearrange("p u e -> p e u"),
+            )
+        w0 = quantise("w0", wx[0][:].rearrange("p q t -> p (q t)"), NQ)
+        v0 = quantise("v0", vx[:, 0, :], DV)
+        y0 = psum.tile([P, DV], F32, name="y0_ps", tag="y0")
+        product(y0, w0, v0)
+        y0_sb = keep.tile([P, DV], F32, name="y0_sb")
+        nc.scalar.activation(y0_sb[:], y0[:], ACT.Copy, scale=inv[:, 0:1])
+        nc.sync.dma_start(out[0], y0_sb[:])
+
+        w1 = quantise("w1", wx[1][:].rearrange("p q t -> p (q t)"), NQ)
+        y1 = [psum.tile([P, P], F32, name=f"y1_ps{h}", tag=("y1", "s1")[h]) for h in range(2)]
+        for h in range(2):
+            product(y1[h], w1, quantise(f"v1{h}", vx[:, 1, h * P * PACK : (h + 1) * P * PACK], P))
+        y1_sb = keep.tile([P, DV], F32, name="y1_sb")
+        nc.scalar.activation(y1_sb[:, 0:P], y1[0][:], ACT.Copy, scale=inv[:, 1:2])
+        nc.vector.tensor_scalar(y1_sb[:, P:DV], y1[1][:], inv[:, 1:2], None, ALU.mult)
+        nc.sync.dma_start(out[1], y1_sb[:])

@@ -19,111 +19,110 @@ ACT = mybir.ActivationFunctionType
 ALU = mybir.AluOpType
 
 PAD = 16
-SPLIT = 288
+SPLIT = 256
+HALF = T // 2
+V_CUT = 960
 
 
 def tile_attend_x_append256_cap_kernel(tc, qT, kT, vT, new_kT, new_vT, vs, offs, slots, out):
     nc = tc.nc
     with ExitStack() as ctx:
         keep = ctx.enter_context(tc.tile_pool(name="keep", bufs=1))
+        shared = ctx.enter_context(tc.tile_pool(name="shared", bufs=1))
         psum = ctx.enter_context(tc.psum_pool(name="psum", bufs=1))
 
         offs_t = keep.tile([P, B * N // 16], U16, name="offs_t")
         slots_t = keep.tile([P, NEW // 16], U16, name="slots_t")
         gk = keep.tile([P, PACK * B * (N + PAD)], BF16, name="gk", align_bytes=64)
         planes = gk[:].rearrange("p (t b s) -> p t b s", t=PACK, b=B)
-        new_k = [keep.tile([P, NEW], F32, name=f"new_k{t}") for t in range(PACK - 1)]
-        new_k = [tile[:] for tile in new_k] + [planes[:, 2, 1, 0:N].bitcast(F32)]
-        new_v = [keep.tile([P, NEW], F32, name=f"new_v{h}", tag=f"after_v{h}", align_bytes=64) for h in range(2)]
+        new_k0 = keep.tile([P, NEW], F32, name="new_k0")
+        new_k1 = keep.tile([P, NEW], F32, name="new_k1")
+        new_k2 = gk[:, B * (N + PAD) : B * (N + PAD) + N].bitcast(F32)
+        new_k3 = keep.tile([P, NEW], F32, name="new_k3")
+        new_v = keep.tile([P, 2, NEW], F32, name="new_v", tag="after_v0", align_bytes=64)
         q_raw = keep.tile([P, B, PACK, NQ], F32, name="q_raw", tag="after_q", align_bytes=64)
         vs_t = keep.tile([P, T], F32, name="vs_t")
-        kp = [keep.tile([P, T], F32, name=f"kp{t}") for t in range(PACK)]
-        vp = [keep.tile([P, T], F32, name=f"vp{h}") for h in range(2)]
+        k_whole = {t: keep.tile([P, T], F32, name=f"k{t}") for t in (0, 3)}
+        k_half = {t: [keep.tile([P, HALF], F32, name=f"k{t}_{a}") for a in range(2)] for t in (1, 2)}
+        v0 = keep.tile([P, T], F32, name="v0")
+        v1_half = [keep.tile([P, V_CUT], F32, name="v1_0"), shared.tile([P, T - V_CUT], F32, name="v1_1", offset=0)]
 
-        warm = keep.tile([P, 1], F32, name="warm")
-        nc.gpsimd.memset(warm[:], 0.0)
-        nc.scalar.activation(warm[:], warm[:], ACT.Exp)
         k_hbm = kT.rearrange("(p j) w -> p j w", j=PACK)
         nk_hbm = new_kT.rearrange("(p j) w -> p j w", j=PACK)
-        nc.vector.memset(vs_t[:], 0.0)
+        nc.gpsimd.memset(vs_t[0 : P - 1, :], 0.0)
+        nc.scalar.dma_start(vs_t[P - 1 : P, :], vs[0:1, :])
+        nc.sync.dma_start(offs_t[:], offs)
         nc.sync.dma_start(slots_t[:], slots)
-        for t in range(PACK):
-            nc.sync.dma_start(new_k[t], nk_hbm[:, t, :])
-            nc.sync.dma_start(kp[t][:], k_hbm[:, t, :])
-            if t == 0:
-                nc.sync.dma_start(offs_t[:], offs)
-                nc.sync.dma_start(vs_t[0:1, :], vs[0:1, :])
+        nc.sync.dma_start(new_k0[:], nk_hbm[:, 0, :])
+        nc.sync.dma_start(k_whole[0][:], k_hbm[:, 0, :])
+        for a in range(2):
+            nc.sync.dma_start(k_half[1][a][:], k_hbm[:, 1, a * HALF : (a + 1) * HALF])
+        nc.sync.dma_start(new_k1[:], nk_hbm[:, 1, :])
+        for a in range(2):
+            nc.sync.dma_start(k_half[2][a][:], k_hbm[:, 2, a * HALF : (a + 1) * HALF])
+        nc.sync.dma_start(new_k2, nk_hbm[:, 2, :])
+        nc.sync.dma_start(new_k3[:], nk_hbm[:, 3, :])
+        nc.sync.dma_start(k_whole[3][:], k_hbm[:, 3, :])
         nc.sync.dma_start(q_raw[:], qT.rearrange("b (p j) w -> p b j w", j=PACK))
-        for h in range(2):
-            nc.sync.dma_start(new_v[h][:], new_vT[h * P : (h + 1) * P, :])
-            nc.sync.dma_start(vp[h][:], vT[h * P : (h + 1) * P, :])
+        nc.sync.dma_start(new_v[:], new_vT.rearrange("(h p) w -> p h w", h=2))
+        nc.sync.dma_start(v0[:], vT[0:P, :])
+        nc.sync.dma_start(v1_half[0][:], vT[P : 2 * P, 0:V_CUT])
+        nc.sync.dma_start(v1_half[1][:], vT[P : 2 * P, V_CUT:T])
 
         ident = keep.tile([P, P], F32, name="ident")
         make_identity(nc, ident[:])
 
-        gv0 = keep.tile([P, 2, B * N // 2], BF16, name="gv0", align_bytes=64)
-        gv1 = []
-
-        def gather_v1(b, tag):
-            gv1.append(keep.tile([P, N], BF16, name=f"gv1_{b}", tag=tag, align_bytes=64))
-            nc.vector.tensor_copy(gv1[b][:].rearrange("p (u s e) -> p s u e", u=2, e=2), vp[1][:].indirect(seq_offs(b)))
-
         def seq_offs(b):
             return offs_t[:, b * N // 16 : (b + 1) * N // 16]
 
-        def append_k(t):
-            nc.vector.tensor_copy(kp[t][:].indirect(slots_t[:]), new_k[t])
+        def append(window, new):
+            nc.vector.tensor_copy(window[:].indirect(slots_t[:]), new)
 
-        def append_v(h):
-            nc.vector.tensor_copy(vp[h][:].indirect(slots_t[:]), new_v[h][:])
+        def rounded(name, new):
+            tile = keep.tile([P, NEW], BF16, name=name)
+            nc.gpsimd.tensor_scalar(tile[:], new, 1.0, 0.0, ALU.mult, ALU.add)
+            return tile[:]
 
-        def turn_v(turned, b, h):
-            for u in range(2):
-                run = gv0[:, u, b * N // 2 : (b + 1) * N // 2] if h == 0 else gv1[b][:, u * N // 2 : (u + 1) * N // 2]
-                nc.tensor.transpose(turned[:, u, :], run.bitcast(F32), ident[:])
-
-        def gather_k_scalar(t):
-            k16 = keep.tile([P, T], BF16, name=f"k16_{t}")
-            nc.scalar.copy(k16[:], kp[t][:])
-            nc.scalar.activation(planes[:, t, :, 0:N], k16[:].indirect(offs_t[:]), ACT.Copy)
-
-        append_k(0)
-        gather_k_scalar(0)
+        def cast(name, halves, cut):
+            tile = keep.tile([P, T], BF16, name=name)
+            nc.scalar.copy(tile[:, 0:cut], halves[0][:])
+            nc.scalar.copy(tile[:, cut:T], halves[1][:])
+            return tile
 
         vsg = keep.tile([P, B * N], F32, name="vsg")
         nc.vector.tensor_copy(vsg[:], vs_t[:].indirect(offs_t[:]))
-        vsT = []
+        vs_ps = []
         for b in range(B):
             turned = psum.tile([P, PACK, P], F32, name=f"vs_ps{b}", tag=f"y{b}")
             for t in range(PACK):
                 nc.tensor.transpose(turned[:, t, :], vsg[:, b * N + t : (b + 1) * N : PACK], ident[:])
-            one = keep.tile([P, PACK], F32, name=f"vsT{b}")
-            nc.scalar.copy(one[:], turned[:, :, 0])
-            vsT.append(one)
+            vs_ps.append(turned)
 
-        append_k(1)
-        gather_k_scalar(1)
-        append_k(2)
-        nc.vector.tensor_copy(planes[:, 2, 0, 0:N], kp[2][:].indirect(seq_offs(0)))
-        append_k(3)
-        for t, b in ((3, 0), (2, 1), (3, 1)):
-            nc.vector.tensor_copy(planes[:, t, b, 0:N], kp[t][:].indirect(seq_offs(b)))
+        append(k_whole[0], new_k0[:])
+        nc.vector.tensor_copy(planes[:, 0, :, 0:N], k_whole[0][:].indirect(offs_t[:]))
+        k16 = {t: cast(f"k16_{t}", k_half[t], HALF) for t in (1, 2)}
+        append(k16[1], rounded("new_k1_16", new_k1[:]))
+        append(k16[2], rounded("new_k2_16", new_k2))
+        append(k_whole[3], new_k3[:])
+        for t in (1, 2):
+            nc.scalar.activation(planes[:, t, :, 0:N], k16[t][:].indirect(offs_t[:]), ACT.Copy)
+        for b in range(B):
+            nc.vector.tensor_copy(planes[:, 3, b, 0:N], k_whole[3][:].indirect(seq_offs(b)))
 
         qx = keep.tile([P, B, NQ, PACK], BF16, name="qx", align_bytes=64)
-        nc.gpsimd.tensor_scalar(qx[:, 0], q_raw[:, 0].rearrange("p j w -> p w j"), 1.0, 0.0, ALU.mult, ALU.add)
-        nc.scalar.copy(
-            qx[:, 1].rearrange("p (c i) j -> p c j i", i=4),
-            q_raw[:, 1].rearrange("p j (c i) -> p c j i", i=4),
-        )
+        for b in range(B):
+            nc.gpsimd.tensor_scalar(qx[:, b], q_raw[:, b].rearrange("p j w -> p w j"), 1.0, 0.0, ALU.mult, ALU.add)
+        new_v1 = rounded("new_v1_16", new_v[:, 1, :])
 
-        kx = keep.tile([P, B, N * PACK], BF16, name="kx", tag="after_q", align_bytes=64)
+        kx_both = keep.tile([P, B * N * PACK], BF16, name="kx", tag="after_q", align_bytes=64)
+        kx = [kx_both[:, b * N * PACK : (b + 1) * N * PACK] for b in range(B)]
         for b in range(B):
             nc.scalar.copy(
-                kx[:, b, 0 : SPLIT * PACK].rearrange("p (c i t) -> p c t i", i=4, t=PACK),
+                kx[b][:, 0 : SPLIT * PACK].rearrange("p (c i t) -> p c t i", i=4, t=PACK),
                 planes[:, :, b, 0:SPLIT].rearrange("p t (c i) -> p c t i", i=4),
             )
             nc.gpsimd.tensor_scalar(
-                kx[:, b, SPLIT * PACK :].rearrange("p (s t) -> p s t", t=PACK),
+                kx[b][:, SPLIT * PACK :].rearrange("p (s t) -> p s t", t=PACK),
                 planes[:, :, b, SPLIT:N].rearrange("p t s -> p s t"),
                 1.0,
                 0.0,
@@ -131,111 +130,101 @@ def tile_attend_x_append256_cap_kernel(tc, qT, kT, vT, new_kT, new_vT, vs, offs,
                 ALU.add,
             )
 
-        def score(b):
-            codes = qk_codes[:, B * NQ + b * N : B * NQ + (b + 1) * N]
-            scale = keep.tile([P, N], U8, name=f"ksc{b}", align_bytes=64)
-            nc.vector.quantize_mx(out=codes.bitcast(FP8X4), scales=scale[:], in_=kx[:, b, :])
-            acc = psum.tile([P, N], F32, name=f"s_ps{b}", tag=f"s{b}")
+        def quantise(name, src, width, codes=None):
+            if codes is None:
+                codes = keep.tile([P, width], U32, name=f"{name}_c", align_bytes=64)[:]
+            scale = keep.tile([P, width], U8, name=f"{name}_s", align_bytes=64)
+            nc.vector.quantize_mx(out=codes.bitcast(FP8X4), scales=scale[:], in_=src)
+            return codes, scale
+
+        def product(acc, lhs, cols, rhs):
             nc.tensor.matmul_mx(
                 out=acc[:],
-                lhsT=qk_codes[:, b * NQ : (b + 1) * NQ].bitcast(FP8X4),
-                lhsT_scale=qs[:, b * NQ : (b + 1) * NQ],
-                rhs=codes.bitcast(FP8X4),
-                rhs_scale=scale[:],
+                lhsT=lhs[0][:, cols].bitcast(FP8X4),
+                lhsT_scale=lhs[1][:, cols],
+                rhs=rhs[0].bitcast(FP8X4),
+                rhs_scale=rhs[1][:],
                 start=True,
                 stop=True,
             )
-            return acc
 
-        append_v(0)
-        v16 = keep.tile([P, T], BF16, name="v16")
-        nc.scalar.copy(v16[:], vp[0][:])
-        qk_codes = keep.tile([P, B * (NQ + N)], U32, name="qk_codes", tag="after_v0", align_bytes=64)
-        qs = keep.tile([P, B * NQ], U8, name="qs", align_bytes=64)
-        nc.vector.quantize_mx(out=qk_codes[:, 0 : B * NQ].bitcast(FP8X4), scales=qs[:], in_=qx[:].rearrange("p b w j -> p (b w j)"))
-        scores = [score(b) for b in range(B)]
-        capped = []
+        q8 = quantise("q", qx[:].rearrange("p b w j -> p (b w j)"), B * NQ)
+        append(v0, new_v[:, 0, :])
+        k_codes = keep.tile([P, B * N], U32, name="k_codes", tag="after_v0", align_bytes=64)
+        scores = []
         for b in range(B):
-            tanh = keep.tile([P, PACK, P], F32, name=f"th{b}", tag=f"after_exp{b}", align_bytes=64)
-            nc.scalar.activation(tanh[:], scores[b][:].rearrange("q (s t) -> q t s", t=PACK), ACT.Tanh, scale=0.5)
-            capped.append(tanh)
-        nc.scalar.activation(gv0[:].rearrange("p u (s e) -> p s u e", e=2), v16[:].indirect(offs_t[:]), ACT.Copy)
-        append_v(1)
-        gather_v1(0, "gv1_0")
-        v_first = psum.tile([P, 2, 2, P], F32, name="v_first", tag="v_first")
-        for h in range(2):
-            turn_v(v_first[:, h], 0, h)
+            acc = psum.tile([P, N], F32, name=f"s_ps{b}", tag=f"s{b}")
+            product(acc, q8, slice(b * NQ, (b + 1) * NQ), quantise(f"k{b}", kx[b], N, k_codes[:, b * N : (b + 1) * N]))
+            scores.append(acc)
+        v16 = cast("v16", v1_half, V_CUT)
+        append(v16, new_v1)
 
-        scaled = keep.tile([P, B, N], F32, name="scaled", tag="after_v1", align_bytes=64)
+        capped = [shared.tile([P, PACK, P], F32, name=f"th{b}", offset=b * N * 4) for b in range(B)]
+        for b in range(B):
+            nc.scalar.activation(capped[b][:], scores[b][:].rearrange("q (s t) -> q t s", t=PACK), ACT.Tanh, scale=0.5)
+        vsT = shared.tile([P, B, 8], F32, name="vsT", offset=B * N * 4)
+        for b in range(B):
+            nc.scalar.copy(vsT[:, b, 0:PACK], vs_ps[b][:, :, P - 1])
+
+        minus_m = []
+        for b in range(B):
+            scaled = keep.tile([P, N], F32, name=f"scaled{b}", tag=f"after_max{b}", align_bytes=64)
+            one = keep.tile([P, 1], F32, name=f"nm{b}")
+            nc.vector.tensor_scalar(scaled[:], capped[b][:].rearrange("q t s -> q (t s)"), -2.0, None, ALU.mult, ALU.min, accum_out=one[:])
+            minus_m.append(one)
+
+        gv0 = keep.tile([P, B, N], BF16, name="gv0", tag="after_max0", align_bytes=64)
+        gv1 = [keep.tile([P, N], BF16, name=f"gv1_{b}", align_bytes=64) for b in range(B)]
+        dealt = "p (u s e) -> p s u e"
+        for b in range(B):
+            nc.vector.tensor_copy(gv0[:, b, :].rearrange(dealt, u=2, e=2), v0[:].indirect(seq_offs(b)))
+
+        def gather_v1(b):
+            nc.scalar.activation(gv1[b][:].rearrange(dealt, u=2, e=2), v16[:].indirect(seq_offs(b)), ACT.Copy)
+
         total = keep.tile([P, B], F32, name="total")
+        gather_v1(0)
         prob = []
         for b in range(B):
-            minus_m = keep.tile([P, 1], F32, name=f"nm{b}")
-            nc.vector.tensor_scalar(scaled[:, b, :], capped[b][:].rearrange("q t s -> q (t s)"), -2.0, None, ALU.mult, ALU.min, accum_out=minus_m[:])
             p = keep.tile([P, PACK, P], F32, name=f"p{b}")
-            nc.scalar.activation(p[:], capped[b][:], ACT.Exp, bias=minus_m[:], scale=2.0, accum_out=total[:, b : b + 1])
+            nc.scalar.activation(p[:], capped[b][:], ACT.Exp, bias=minus_m[b][:], scale=2.0, accum_out=total[:, b : b + 1])
             prob.append(p)
-        gather_v1(1, "after_exp0")
+        gather_v1(1)
 
         wx = []
         for b in range(B):
-            turned = psum.tile([P, PACK, P], F32, name=f"w_ps{b}")
+            turned = psum.tile([P, PACK, P], F32, name=f"w_ps{b}", tag=f"w{b}")
             for t in range(PACK):
                 nc.tensor.transpose(turned[:, t, :], prob[b][:, t, :], ident[:])
             weights = keep.tile([P, NQ, PACK], BF16, name=f"wx{b}", align_bytes=64)
             nc.vector.tensor_tensor(
                 weights[:],
                 turned[:].rearrange("p t q -> p q t"),
-                vsT[b][:].unsqueeze(1).to_broadcast([P, NQ, PACK]),
+                vsT[:, b, 0:PACK].unsqueeze(1).to_broadcast([P, NQ, PACK]),
                 ALU.mult,
             )
             wx.append(weights)
-        vx = keep.tile([P, B, DV * PACK], BF16, name="vx", tag="after_exp1", align_bytes=64)
         inv = keep.tile([P, B], F32, name="inv")
         nc.vector.reciprocal(inv[:], total[:])
 
-        def quantise(name, src, width):
-            codes = keep.tile([P, width], U32, name=f"{name}_c", align_bytes=64)
-            scale = keep.tile([P, width], U8, name=f"{name}_s", align_bytes=64)
-            nc.vector.quantize_mx(out=codes[:].bitcast(FP8X4), scales=scale[:], in_=src)
-            return codes, scale
-
-        def product(y, w, v):
-            nc.tensor.matmul_mx(
-                out=y[:],
-                lhsT=w[0][:].bitcast(FP8X4),
-                lhsT_scale=w[1][:],
-                rhs=v[0][:].bitcast(FP8X4),
-                rhs_scale=v[1][:],
-                start=True,
-                stop=True,
-            )
-
-        nc.scalar.copy(
-            vx[:, 0, :].bitcast(F32).rearrange("p (h e u) -> p h e u", h=2, u=2),
-            v_first[:].rearrange("p h u e -> p h e u"),
-        )
-        v_last = [psum.tile([P, 2, P], F32, name=f"v_last{h}", tag=("v_first", "s0")[h]) for h in range(2)]
-        for h in range(2):
-            turn_v(v_last[h][:], 1, h)
-        for h in range(2):
+        vx = []
+        for b in range(B):
+            turned = psum.tile([P, 2, 2, P], F32, name=f"v_ps{b}", tag=("v", "w0")[b])
+            for h, runs in ((1, gv1[b][:]), (0, gv0[:, b, :])):
+                for u in range(2):
+                    nc.tensor.transpose(turned[:, h, u, :], runs[:, u * N // 2 : (u + 1) * N // 2].bitcast(F32), ident[:])
+            values = keep.tile([P, DV * PACK], BF16, name=f"vx{b}", align_bytes=64)
             nc.scalar.copy(
-                vx[:, 1, h * P * PACK : (h + 1) * P * PACK].bitcast(F32).rearrange("p (e u) -> p e u", u=2),
-                v_last[h][:].rearrange("p u e -> p e u"),
+                values[:].bitcast(F32).rearrange("p (h e u) -> p h e u", h=2, u=2),
+                turned[:].rearrange("p h u e -> p h e u"),
             )
-        w0 = quantise("w0", wx[0][:].rearrange("p q t -> p (q t)"), NQ)
-        v0 = quantise("v0", vx[:, 0, :], DV)
-        y0 = psum.tile([P, DV], F32, name="y0_ps", tag="y0")
-        product(y0, w0, v0)
-        y0_sb = keep.tile([P, DV], F32, name="y0_sb")
-        nc.scalar.activation(y0_sb[:], y0[:], ACT.Copy, scale=inv[:, 0:1])
-        nc.sync.dma_start(out[0], y0_sb[:])
+            vx.append(values)
 
-        w1 = quantise("w1", wx[1][:].rearrange("p q t -> p (q t)"), NQ)
-        y1 = [psum.tile([P, P], F32, name=f"y1_ps{h}", tag=("y1", "s1")[h]) for h in range(2)]
-        for h in range(2):
-            product(y1[h], w1, quantise(f"v1{h}", vx[:, 1, h * P * PACK : (h + 1) * P * PACK], P))
-        y1_sb = keep.tile([P, DV], F32, name="y1_sb")
-        nc.scalar.activation(y1_sb[:, 0:P], y1[0][:], ACT.Copy, scale=inv[:, 1:2])
-        nc.vector.tensor_scalar(y1_sb[:, P:DV], y1[1][:], inv[:, 1:2], None, ALU.mult)
-        nc.sync.dma_start(out[1], y1_sb[:])
+        for b in range(B):
+            w8 = quantise(f"w{b}", wx[b][:].rearrange("p q t -> p (q t)"), NQ)
+            v8 = quantise(f"v{b}", vx[b][:], DV)
+            y = psum.tile([P, DV], F32, name=f"y_ps{b}", tag=f"y{b}")
+            product(y, w8, slice(0, NQ), v8)
+            y_sb = keep.tile([P, DV], F32, name=f"y_sb{b}")
+            nc.scalar.activation(y_sb[:], y[:], ACT.Copy, scale=inv[:, b : b + 1])
+            nc.sync.dma_start(out[b], y_sb[:])

@@ -19,7 +19,7 @@ ACT = mybir.ActivationFunctionType
 ALU = mybir.AluOpType
 
 PAD = 16
-SPLIT = 256
+SPLIT = 384
 HALF = T // 2
 V_CUT = 960
 
@@ -55,9 +55,9 @@ def tile_attend_x_append256_cap_kernel(tc, qT, kT, vT, new_kT, new_vT, vs, offs,
         nc.sync.dma_start(slots_t[:], slots)
         nc.sync.dma_start(new_k0[:], nk_hbm[:, 0, :])
         nc.sync.dma_start(k_whole[0][:], k_hbm[:, 0, :])
+        nc.sync.dma_start(new_k1[:], nk_hbm[:, 1, :])
         for a in range(2):
             nc.sync.dma_start(k_half[1][a][:], k_hbm[:, 1, a * HALF : (a + 1) * HALF])
-        nc.sync.dma_start(new_k1[:], nk_hbm[:, 1, :])
         for a in range(2):
             nc.sync.dma_start(k_half[2][a][:], k_hbm[:, 2, a * HALF : (a + 1) * HALF])
         nc.sync.dma_start(new_k2, nk_hbm[:, 2, :])
@@ -78,9 +78,9 @@ def tile_attend_x_append256_cap_kernel(tc, qT, kT, vT, new_kT, new_vT, vs, offs,
         def append(window, new):
             nc.vector.tensor_copy(window[:].indirect(slots_t[:]), new)
 
-        def rounded(name, new):
+        def rounded(name, new, copy):
             tile = keep.tile([P, NEW], BF16, name=name)
-            nc.gpsimd.tensor_scalar(tile[:], new, 1.0, 0.0, ALU.mult, ALU.add)
+            copy(tile[:], new)
             return tile[:]
 
         def cast(name, halves, cut):
@@ -100,9 +100,10 @@ def tile_attend_x_append256_cap_kernel(tc, qT, kT, vT, new_kT, new_vT, vs, offs,
 
         append(k_whole[0], new_k0[:])
         nc.vector.tensor_copy(planes[:, 0, :, 0:N], k_whole[0][:].indirect(offs_t[:]))
+        new_k1_16 = rounded("new_k1_16", new_k1[:], nc.scalar.copy)
         k16 = {t: cast(f"k16_{t}", k_half[t], HALF) for t in (1, 2)}
-        append(k16[1], rounded("new_k1_16", new_k1[:]))
-        append(k16[2], rounded("new_k2_16", new_k2))
+        append(k16[1], new_k1_16)
+        append(k16[2], rounded("new_k2_16", new_k2, nc.vector.tensor_copy))
         append(k_whole[3], new_k3[:])
         for t in (1, 2):
             nc.scalar.activation(planes[:, t, :, 0:N], k16[t][:].indirect(offs_t[:]), ACT.Copy)
@@ -110,9 +111,11 @@ def tile_attend_x_append256_cap_kernel(tc, qT, kT, vT, new_kT, new_vT, vs, offs,
             nc.vector.tensor_copy(planes[:, 3, b, 0:N], k_whole[3][:].indirect(seq_offs(b)))
 
         qx = keep.tile([P, B, NQ, PACK], BF16, name="qx", align_bytes=64)
-        for b in range(B):
-            nc.gpsimd.tensor_scalar(qx[:, b], q_raw[:, b].rearrange("p j w -> p w j"), 1.0, 0.0, ALU.mult, ALU.add)
-        new_v1 = rounded("new_v1_16", new_v[:, 1, :])
+        nc.scalar.copy(
+            qx[:].rearrange("p b (c i) j -> p b c j i", i=4),
+            q_raw[:].rearrange("p b j (c i) -> p b c j i", i=4),
+        )
+        new_v1 = rounded("new_v1_16", new_v[:, 1, :], nc.vector.tensor_copy)
 
         kx_both = keep.tile([P, B * N * PACK], BF16, name="kx", tag="after_q", align_bytes=64)
         kx = [kx_both[:, b * N * PACK : (b + 1) * N * PACK] for b in range(B)]
@@ -121,14 +124,10 @@ def tile_attend_x_append256_cap_kernel(tc, qT, kT, vT, new_kT, new_vT, vs, offs,
                 kx[b][:, 0 : SPLIT * PACK].rearrange("p (c i t) -> p c t i", i=4, t=PACK),
                 planes[:, :, b, 0:SPLIT].rearrange("p t (c i) -> p c t i", i=4),
             )
-            nc.gpsimd.tensor_scalar(
-                kx[b][:, SPLIT * PACK :].rearrange("p (s t) -> p s t", t=PACK),
-                planes[:, :, b, SPLIT:N].rearrange("p t s -> p s t"),
-                1.0,
-                0.0,
-                ALU.mult,
-                ALU.add,
-            )
+        nc.vector.tensor_copy(
+            kx_both[:].rearrange("p (b c i t) -> p b c t i", b=B, i=4, t=PACK)[:, :, SPLIT // 4 :],
+            planes[:, :, :, SPLIT:N].rearrange("p t b (c i) -> p b c t i", i=4),
+        )
 
         def quantise(name, src, width, codes=None):
             if codes is None:
@@ -156,6 +155,14 @@ def tile_attend_x_append256_cap_kernel(tc, qT, kT, vT, new_kT, new_vT, vs, offs,
             acc = psum.tile([P, N], F32, name=f"s_ps{b}", tag=f"s{b}")
             product(acc, q8, slice(b * NQ, (b + 1) * NQ), quantise(f"k{b}", kx[b], N, k_codes[:, b * N : (b + 1) * N]))
             scores.append(acc)
+        gv0 = []
+
+        def gather_v0(b, tag):
+            gv0.append(keep.tile([P, N], BF16, name=f"gv0_{b}", tag=tag, align_bytes=64))
+            nc.vector.tensor_copy(gv0[b][:].rearrange(dealt, u=2, e=2), v0[:].indirect(seq_offs(b)))
+
+        dealt = "p (u s e) -> p s u e"
+        gather_v0(0, "gv0_0")
         v16 = cast("v16", v1_half, V_CUT)
         append(v16, new_v1)
 
@@ -173,11 +180,8 @@ def tile_attend_x_append256_cap_kernel(tc, qT, kT, vT, new_kT, new_vT, vs, offs,
             nc.vector.tensor_scalar(scaled[:], capped[b][:].rearrange("q t s -> q (t s)"), -2.0, None, ALU.mult, ALU.min, accum_out=one[:])
             minus_m.append(one)
 
-        gv0 = keep.tile([P, B, N], BF16, name="gv0", tag="after_max0", align_bytes=64)
         gv1 = [keep.tile([P, N], BF16, name=f"gv1_{b}", align_bytes=64) for b in range(B)]
-        dealt = "p (u s e) -> p s u e"
-        for b in range(B):
-            nc.vector.tensor_copy(gv0[:, b, :].rearrange(dealt, u=2, e=2), v0[:].indirect(seq_offs(b)))
+        gather_v0(1, "after_max0")
 
         def gather_v1(b):
             nc.scalar.activation(gv1[b][:].rearrange(dealt, u=2, e=2), v16[:].indirect(seq_offs(b)), ACT.Copy)
@@ -210,7 +214,7 @@ def tile_attend_x_append256_cap_kernel(tc, qT, kT, vT, new_kT, new_vT, vs, offs,
         vx = []
         for b in range(B):
             turned = psum.tile([P, 2, 2, P], F32, name=f"v_ps{b}", tag=("v", "w0")[b])
-            for h, runs in ((1, gv1[b][:]), (0, gv0[:, b, :])):
+            for h, runs in ((1, gv1[b][:]), (0, gv0[b][:])):
                 for u in range(2):
                     nc.tensor.transpose(turned[:, h, u, :], runs[:, u * N // 2 : (u + 1) * N // 2].bitcast(F32), ident[:])
             values = keep.tile([P, DV * PACK], BF16, name=f"vx{b}", align_bytes=64)

@@ -19,16 +19,15 @@ ACT = mybir.ActivationFunctionType
 ALU = mybir.AluOpType
 
 PAD = 16
-SPLIT = 384
+SPLIT = 176
+SPLIT_G = 384
 HALF = T // 2
-V_CUT = 960
 
 
 def tile_attend_x_append256_cap_kernel(tc, qT, kT, vT, new_kT, new_vT, vs, offs, slots, out):
     nc = tc.nc
     with ExitStack() as ctx:
         keep = ctx.enter_context(tc.tile_pool(name="keep", bufs=1))
-        shared = ctx.enter_context(tc.tile_pool(name="shared", bufs=1))
         psum = ctx.enter_context(tc.psum_pool(name="psum", bufs=1))
 
         offs_t = keep.tile([P, B * N // 16], U16, name="offs_t")
@@ -39,13 +38,13 @@ def tile_attend_x_append256_cap_kernel(tc, qT, kT, vT, new_kT, new_vT, vs, offs,
         new_k1 = keep.tile([P, NEW], F32, name="new_k1")
         new_k2 = gk[:, B * (N + PAD) : B * (N + PAD) + N].bitcast(F32)
         new_k3 = keep.tile([P, NEW], F32, name="new_k3")
-        new_v = keep.tile([P, 2, NEW], F32, name="new_v", tag="after_v0", align_bytes=64)
-        q_raw = keep.tile([P, B, PACK, NQ], F32, name="q_raw", tag="after_q", align_bytes=64)
+        new_v = [keep.tile([P, NEW], F32, name=f"new_v{h}", tag=f"after_v{h}", align_bytes=64) for h in range(2)]
+        q_raw = keep.tile([P, B, PACK, NQ], F32, name="q_raw")
         vs_t = keep.tile([P, T], F32, name="vs_t")
         k_whole = {t: keep.tile([P, T], F32, name=f"k{t}") for t in (0, 3)}
         k_half = {t: [keep.tile([P, HALF], F32, name=f"k{t}_{a}") for a in range(2)] for t in (1, 2)}
-        v0 = keep.tile([P, T], F32, name="v0")
-        v1_half = [keep.tile([P, V_CUT], F32, name="v1_0"), shared.tile([P, T - V_CUT], F32, name="v1_1", offset=0)]
+        v0 = keep.tile([P, T], F32, name="v0", tag="after_cast")
+        v1 = keep.tile([P, T], F32, name="v1")
 
         k_hbm = kT.rearrange("(p j) w -> p j w", j=PACK)
         nk_hbm = new_kT.rearrange("(p j) w -> p j w", j=PACK)
@@ -55,19 +54,18 @@ def tile_attend_x_append256_cap_kernel(tc, qT, kT, vT, new_kT, new_vT, vs, offs,
         nc.sync.dma_start(slots_t[:], slots)
         nc.sync.dma_start(new_k0[:], nk_hbm[:, 0, :])
         nc.sync.dma_start(k_whole[0][:], k_hbm[:, 0, :])
-        nc.sync.dma_start(new_k1[:], nk_hbm[:, 1, :])
         for a in range(2):
             nc.sync.dma_start(k_half[1][a][:], k_hbm[:, 1, a * HALF : (a + 1) * HALF])
+        nc.sync.dma_start(new_k1[:], nk_hbm[:, 1, :])
         for a in range(2):
             nc.sync.dma_start(k_half[2][a][:], k_hbm[:, 2, a * HALF : (a + 1) * HALF])
         nc.sync.dma_start(new_k2, nk_hbm[:, 2, :])
         nc.sync.dma_start(new_k3[:], nk_hbm[:, 3, :])
         nc.sync.dma_start(k_whole[3][:], k_hbm[:, 3, :])
         nc.sync.dma_start(q_raw[:], qT.rearrange("b (p j) w -> p b j w", j=PACK))
-        nc.sync.dma_start(new_v[:], new_vT.rearrange("(h p) w -> p h w", h=2))
-        nc.sync.dma_start(v0[:], vT[0:P, :])
-        nc.sync.dma_start(v1_half[0][:], vT[P : 2 * P, 0:V_CUT])
-        nc.sync.dma_start(v1_half[1][:], vT[P : 2 * P, V_CUT:T])
+        for h, window in enumerate((v0, v1)):
+            nc.sync.dma_start(new_v[h][:], new_vT[h * P : (h + 1) * P, :])
+            nc.sync.dma_start(window[:], vT[h * P : (h + 1) * P, :])
 
         ident = keep.tile([P, P], F32, name="ident")
         make_identity(nc, ident[:])
@@ -78,15 +76,15 @@ def tile_attend_x_append256_cap_kernel(tc, qT, kT, vT, new_kT, new_vT, vs, offs,
         def append(window, new):
             nc.vector.tensor_copy(window[:].indirect(slots_t[:]), new)
 
-        def rounded(name, new, copy):
+        def rounded(name, new):
             tile = keep.tile([P, NEW], BF16, name=name)
-            copy(tile[:], new)
+            nc.vector.tensor_copy(tile[:], new)
             return tile[:]
 
-        def cast(name, halves, cut):
+        def cast(name, halves):
             tile = keep.tile([P, T], BF16, name=name)
-            nc.scalar.copy(tile[:, 0:cut], halves[0][:])
-            nc.scalar.copy(tile[:, cut:T], halves[1][:])
+            nc.scalar.copy(tile[:, 0:HALF], halves[0][:])
+            nc.scalar.copy(tile[:, HALF:T], halves[1][:])
             return tile
 
         vsg = keep.tile([P, B * N], F32, name="vsg")
@@ -100,10 +98,9 @@ def tile_attend_x_append256_cap_kernel(tc, qT, kT, vT, new_kT, new_vT, vs, offs,
 
         append(k_whole[0], new_k0[:])
         nc.vector.tensor_copy(planes[:, 0, :, 0:N], k_whole[0][:].indirect(offs_t[:]))
-        new_k1_16 = rounded("new_k1_16", new_k1[:], nc.scalar.copy)
-        k16 = {t: cast(f"k16_{t}", k_half[t], HALF) for t in (1, 2)}
-        append(k16[1], new_k1_16)
-        append(k16[2], rounded("new_k2_16", new_k2, nc.vector.tensor_copy))
+        k16 = {t: cast(f"k16_{t}", k_half[t]) for t in (1, 2)}
+        append(k16[1], rounded("new_k1_16", new_k1[:]))
+        append(k16[2], rounded("new_k2_16", new_k2))
         append(k_whole[3], new_k3[:])
         for t in (1, 2):
             nc.scalar.activation(planes[:, t, :, 0:N], k16[t][:].indirect(offs_t[:]), ACT.Copy)
@@ -115,9 +112,8 @@ def tile_attend_x_append256_cap_kernel(tc, qT, kT, vT, new_kT, new_vT, vs, offs,
             qx[:].rearrange("p b (c i) j -> p b c j i", i=4),
             q_raw[:].rearrange("p b j (c i) -> p b c j i", i=4),
         )
-        new_v1 = rounded("new_v1_16", new_v[:, 1, :], nc.vector.tensor_copy)
 
-        kx_both = keep.tile([P, B * N * PACK], BF16, name="kx", tag="after_q", align_bytes=64)
+        kx_both = keep.tile([P, B * N * PACK], BF16, name="kx", align_bytes=64)
         kx = [kx_both[:, b * N * PACK : (b + 1) * N * PACK] for b in range(B)]
         for b in range(B):
             nc.scalar.copy(
@@ -125,8 +121,16 @@ def tile_attend_x_append256_cap_kernel(tc, qT, kT, vT, new_kT, new_vT, vs, offs,
                 planes[:, :, b, 0:SPLIT].rearrange("p t (c i) -> p c t i", i=4),
             )
         nc.vector.tensor_copy(
-            kx_both[:].rearrange("p (b c i t) -> p b c t i", b=B, i=4, t=PACK)[:, :, SPLIT // 4 :],
-            planes[:, :, :, SPLIT:N].rearrange("p t b (c i) -> p b c t i", i=4),
+            kx_both[:].rearrange("p (b c i t) -> p b c t i", b=B, i=4, t=PACK)[:, :, SPLIT // 4 : SPLIT_G // 4],
+            planes[:, :, :, SPLIT:SPLIT_G].rearrange("p t b (c i) -> p b c t i", i=4),
+        )
+        nc.gpsimd.tensor_scalar(
+            kx_both[:].rearrange("p (b s t) -> p b s t", b=B, t=PACK)[:, :, SPLIT_G:],
+            planes[:, :, :, SPLIT_G:N].rearrange("p t b s -> p b s t"),
+            1.0,
+            0.0,
+            ALU.mult,
+            ALU.add,
         )
 
         def quantise(name, src, width, codes=None):
@@ -147,76 +151,75 @@ def tile_attend_x_append256_cap_kernel(tc, qT, kT, vT, new_kT, new_vT, vs, offs,
                 stop=True,
             )
 
-        q8 = quantise("q", qx[:].rearrange("p b w j -> p (b w j)"), B * NQ)
-        append(v0, new_v[:, 0, :])
-        k_codes = keep.tile([P, B * N], U32, name="k_codes", tag="after_v0", align_bytes=64)
+        append(v0, new_v[0][:])
+        v16 = keep.tile([P, T], BF16, name="v16")
+        nc.scalar.copy(v16[:], v0[:])
+        qk_codes = keep.tile([P, B * (NQ + N)], U32, name="qk_codes", tag="after_v0", align_bytes=64)
+        k_codes = qk_codes[:, B * NQ :]
+        q8 = quantise("q", qx[:].rearrange("p b w j -> p (b w j)"), B * NQ, qk_codes[:, 0 : B * NQ])
         scores = []
         for b in range(B):
             acc = psum.tile([P, N], F32, name=f"s_ps{b}", tag=f"s{b}")
             product(acc, q8, slice(b * NQ, (b + 1) * NQ), quantise(f"k{b}", kx[b], N, k_codes[:, b * N : (b + 1) * N]))
             scores.append(acc)
-        gv0 = []
-
-        def gather_v0(b, tag):
-            gv0.append(keep.tile([P, N], BF16, name=f"gv0_{b}", tag=tag, align_bytes=64))
-            nc.vector.tensor_copy(gv0[b][:].rearrange(dealt, u=2, e=2), v0[:].indirect(seq_offs(b)))
+        append(v1, new_v[1][:])
 
         dealt = "p (u s e) -> p s u e"
-        gather_v0(0, "gv0_0")
-        v16 = cast("v16", v1_half, V_CUT)
-        append(v16, new_v1)
+        gv = {}
 
-        capped = [shared.tile([P, PACK, P], F32, name=f"th{b}", offset=b * N * 4) for b in range(B)]
+        def gather_v(h, b, tag):
+            gv[h, b] = keep.tile([P, N], BF16, name=f"gv{h}_{b}", tag=tag, align_bytes=64)
+            runs = gv[h, b][:].rearrange(dealt, u=2, e=2)
+            if h == 0:
+                nc.scalar.activation(runs, v16[:].indirect(seq_offs(b)), ACT.Copy)
+            else:
+                nc.vector.tensor_copy(runs, v1[:].indirect(seq_offs(b)))
+
+        gather_v(1, 0, "gv1_0")
+        capped = [keep.tile([P, PACK, P], F32, name=f"th{b}", tag=("after_exp0", "th1")[b], align_bytes=64) for b in range(B)]
         for b in range(B):
             nc.scalar.activation(capped[b][:], scores[b][:].rearrange("q (s t) -> q t s", t=PACK), ACT.Tanh, scale=0.5)
-        vsT = shared.tile([P, B, 8], F32, name="vsT", offset=B * N * 4)
+        vsT = keep.tile([P, B, 8], F32, name="vsT", tag="after_cast")
         for b in range(B):
             nc.scalar.copy(vsT[:, b, 0:PACK], vs_ps[b][:, :, P - 1])
 
         minus_m = []
         for b in range(B):
-            scaled = keep.tile([P, N], F32, name=f"scaled{b}", tag=f"after_max{b}", align_bytes=64)
+            scaled = keep.tile([P, N], F32, name=f"scaled{b}", tag=("after_v1", "after_max1")[b], align_bytes=64)
             one = keep.tile([P, 1], F32, name=f"nm{b}")
             nc.vector.tensor_scalar(scaled[:], capped[b][:].rearrange("q t s -> q (t s)"), -2.0, None, ALU.mult, ALU.min, accum_out=one[:])
             minus_m.append(one)
-
-        gv1 = [keep.tile([P, N], BF16, name=f"gv1_{b}", align_bytes=64) for b in range(B)]
-        gather_v0(1, "after_max0")
-
-        def gather_v1(b):
-            nc.scalar.activation(gv1[b][:].rearrange(dealt, u=2, e=2), v16[:].indirect(seq_offs(b)), ACT.Copy)
+        gather_v(1, 1, "after_max1")
 
         total = keep.tile([P, B], F32, name="total")
-        gather_v1(0)
+        gather_v(0, 0, "gv0_0")
         prob = []
         for b in range(B):
-            p = keep.tile([P, PACK, P], F32, name=f"p{b}")
+            p = keep.tile([P, PACK, P], F32, name=f"p{b}", tag=("p0", "after_turn1")[b], align_bytes=64)
             nc.scalar.activation(p[:], capped[b][:], ACT.Exp, bias=minus_m[b][:], scale=2.0, accum_out=total[:, b : b + 1])
             prob.append(p)
-        gather_v1(1)
+        gather_v(0, 1, "after_exp0")
 
-        wx = []
+        wx = keep.tile([P, B, NQ, PACK], BF16, name="wx", align_bytes=64)
         for b in range(B):
             turned = psum.tile([P, PACK, P], F32, name=f"w_ps{b}", tag=f"w{b}")
             for t in range(PACK):
                 nc.tensor.transpose(turned[:, t, :], prob[b][:, t, :], ident[:])
-            weights = keep.tile([P, NQ, PACK], BF16, name=f"wx{b}", align_bytes=64)
             nc.vector.tensor_tensor(
-                weights[:],
+                wx[:, b],
                 turned[:].rearrange("p t q -> p q t"),
                 vsT[:, b, 0:PACK].unsqueeze(1).to_broadcast([P, NQ, PACK]),
                 ALU.mult,
             )
-            wx.append(weights)
         inv = keep.tile([P, B], F32, name="inv")
         nc.vector.reciprocal(inv[:], total[:])
 
         vx = []
         for b in range(B):
             turned = psum.tile([P, 2, 2, P], F32, name=f"v_ps{b}", tag=("v", "w0")[b])
-            for h, runs in ((1, gv1[b][:]), (0, gv0[b][:])):
+            for h in (1, 0):
                 for u in range(2):
-                    nc.tensor.transpose(turned[:, h, u, :], runs[:, u * N // 2 : (u + 1) * N // 2].bitcast(F32), ident[:])
+                    nc.tensor.transpose(turned[:, h, u, :], gv[h, b][:, u * N // 2 : (u + 1) * N // 2].bitcast(F32), ident[:])
             values = keep.tile([P, DV * PACK], BF16, name=f"vx{b}", align_bytes=64)
             nc.scalar.copy(
                 values[:].bitcast(F32).rearrange("p (h e u) -> p h e u", h=2, u=2),
@@ -224,11 +227,13 @@ def tile_attend_x_append256_cap_kernel(tc, qT, kT, vT, new_kT, new_vT, vs, offs,
             )
             vx.append(values)
 
+        v0_codes = keep.tile([P, DV], U32, name="v0_c", tag="after_turn1", align_bytes=64)
+        v8 = [quantise("v0", vx[0][:], DV, v0_codes[:])]
+        w8 = quantise("w", wx[:].rearrange("p b q t -> p (b q t)"), B * NQ)
+        v8.append(quantise("v1", vx[1][:], DV))
         for b in range(B):
-            w8 = quantise(f"w{b}", wx[b][:].rearrange("p q t -> p (q t)"), NQ)
-            v8 = quantise(f"v{b}", vx[b][:], DV)
-            y = psum.tile([P, DV], F32, name=f"y_ps{b}", tag=f"y{b}")
-            product(y, w8, slice(0, NQ), v8)
+            y = psum.tile([P, DV], F32, name=f"y_ps{b}", tag=f"s{b}")
+            product(y, w8, slice(b * NQ, (b + 1) * NQ), v8[b])
             y_sb = keep.tile([P, DV], F32, name=f"y_sb{b}")
             nc.scalar.activation(y_sb[:], y[:], ACT.Copy, scale=inv[:, b : b + 1])
             nc.sync.dma_start(out[b], y_sb[:])

@@ -19,8 +19,7 @@ ACT = mybir.ActivationFunctionType
 ALU = mybir.AluOpType
 
 PAD = 16
-SPLIT = 176
-SPLIT_G = 384
+SPLIT = 288
 HALF = T // 2
 
 
@@ -39,7 +38,7 @@ def tile_attend_x_append256_cap_kernel(tc, qT, kT, vT, new_kT, new_vT, vs, offs,
         new_k2 = gk[:, B * (N + PAD) : B * (N + PAD) + N].bitcast(F32)
         new_k3 = keep.tile([P, NEW], F32, name="new_k3")
         new_v = [keep.tile([P, NEW], F32, name=f"new_v{h}", tag=f"after_v{h}", align_bytes=64) for h in range(2)]
-        q_raw = keep.tile([P, B, PACK, NQ], F32, name="q_raw")
+        q_raw = keep.tile([P, B, PACK, NQ], F32, name="q_raw", tag="after_q", align_bytes=64)
         vs_t = keep.tile([P, T], F32, name="vs_t")
         k_whole = {t: keep.tile([P, T], F32, name=f"k{t}") for t in (0, 3)}
         k_half = {t: [keep.tile([P, HALF], F32, name=f"k{t}_{a}") for a in range(2)] for t in (1, 2)}
@@ -48,15 +47,15 @@ def tile_attend_x_append256_cap_kernel(tc, qT, kT, vT, new_kT, new_vT, vs, offs,
 
         k_hbm = kT.rearrange("(p j) w -> p j w", j=PACK)
         nk_hbm = new_kT.rearrange("(p j) w -> p j w", j=PACK)
-        nc.gpsimd.memset(vs_t[0 : P - 1, :], 0.0)
-        nc.scalar.dma_start(vs_t[P - 1 : P, :], vs[0:1, :])
+        nc.vector.memset(vs_t[0 : P - 1, :], 0.0)
+        nc.sync.dma_start(vs_t[P - 1 : P, :], vs[0:1, :])
         nc.sync.dma_start(offs_t[:], offs)
         nc.sync.dma_start(slots_t[:], slots)
         nc.sync.dma_start(new_k0[:], nk_hbm[:, 0, :])
         nc.sync.dma_start(k_whole[0][:], k_hbm[:, 0, :])
+        nc.sync.dma_start(new_k1[:], nk_hbm[:, 1, :])
         for a in range(2):
             nc.sync.dma_start(k_half[1][a][:], k_hbm[:, 1, a * HALF : (a + 1) * HALF])
-        nc.sync.dma_start(new_k1[:], nk_hbm[:, 1, :])
         for a in range(2):
             nc.sync.dma_start(k_half[2][a][:], k_hbm[:, 2, a * HALF : (a + 1) * HALF])
         nc.sync.dma_start(new_k2, nk_hbm[:, 2, :])
@@ -76,9 +75,9 @@ def tile_attend_x_append256_cap_kernel(tc, qT, kT, vT, new_kT, new_vT, vs, offs,
         def append(window, new):
             nc.vector.tensor_copy(window[:].indirect(slots_t[:]), new)
 
-        def rounded(name, new):
+        def rounded(name, new, copy):
             tile = keep.tile([P, NEW], BF16, name=name)
-            nc.vector.tensor_copy(tile[:], new)
+            copy(tile[:], new)
             return tile[:]
 
         def cast(name, halves):
@@ -98,9 +97,10 @@ def tile_attend_x_append256_cap_kernel(tc, qT, kT, vT, new_kT, new_vT, vs, offs,
 
         append(k_whole[0], new_k0[:])
         nc.vector.tensor_copy(planes[:, 0, :, 0:N], k_whole[0][:].indirect(offs_t[:]))
+        new_k1_16 = rounded("new_k1_16", new_k1[:], nc.scalar.copy)
         k16 = {t: cast(f"k16_{t}", k_half[t]) for t in (1, 2)}
-        append(k16[1], rounded("new_k1_16", new_k1[:]))
-        append(k16[2], rounded("new_k2_16", new_k2))
+        append(k16[1], new_k1_16)
+        append(k16[2], rounded("new_k2_16", new_k2, nc.vector.tensor_copy))
         append(k_whole[3], new_k3[:])
         for t in (1, 2):
             nc.scalar.activation(planes[:, t, :, 0:N], k16[t][:].indirect(offs_t[:]), ACT.Copy)
@@ -108,30 +108,27 @@ def tile_attend_x_append256_cap_kernel(tc, qT, kT, vT, new_kT, new_vT, vs, offs,
             nc.vector.tensor_copy(planes[:, 3, b, 0:N], k_whole[3][:].indirect(seq_offs(b)))
 
         qx = keep.tile([P, B, NQ, PACK], BF16, name="qx", align_bytes=64)
+        nc.gpsimd.tensor_scalar(qx[:, 0], q_raw[:, 0].rearrange("p j w -> p w j"), 1.0, 0.0, ALU.mult, ALU.add)
         nc.scalar.copy(
-            qx[:].rearrange("p b (c i) j -> p b c j i", i=4),
-            q_raw[:].rearrange("p b j (c i) -> p b c j i", i=4),
+            qx[:, 1].rearrange("p (c i) j -> p c j i", i=4),
+            q_raw[:, 1].rearrange("p j (c i) -> p c j i", i=4),
         )
 
-        kx_both = keep.tile([P, B * N * PACK], BF16, name="kx", align_bytes=64)
+        kx_both = keep.tile([P, B * N * PACK], BF16, name="kx", tag="after_q", align_bytes=64)
         kx = [kx_both[:, b * N * PACK : (b + 1) * N * PACK] for b in range(B)]
         for b in range(B):
             nc.scalar.copy(
                 kx[b][:, 0 : SPLIT * PACK].rearrange("p (c i t) -> p c t i", i=4, t=PACK),
                 planes[:, :, b, 0:SPLIT].rearrange("p t (c i) -> p c t i", i=4),
             )
-        nc.vector.tensor_copy(
-            kx_both[:].rearrange("p (b c i t) -> p b c t i", b=B, i=4, t=PACK)[:, :, SPLIT // 4 : SPLIT_G // 4],
-            planes[:, :, :, SPLIT:SPLIT_G].rearrange("p t b (c i) -> p b c t i", i=4),
-        )
-        nc.gpsimd.tensor_scalar(
-            kx_both[:].rearrange("p (b s t) -> p b s t", b=B, t=PACK)[:, :, SPLIT_G:],
-            planes[:, :, :, SPLIT_G:N].rearrange("p t b s -> p b s t"),
-            1.0,
-            0.0,
-            ALU.mult,
-            ALU.add,
-        )
+            nc.gpsimd.tensor_scalar(
+                kx[b][:, SPLIT * PACK :].rearrange("p (s t) -> p s t", t=PACK),
+                planes[:, :, b, SPLIT:N].rearrange("p t s -> p s t"),
+                1.0,
+                0.0,
+                ALU.mult,
+                ALU.add,
+            )
 
         def quantise(name, src, width, codes=None):
             if codes is None:
@@ -214,26 +211,39 @@ def tile_attend_x_append256_cap_kernel(tc, qT, kT, vT, new_kT, new_vT, vs, offs,
         inv = keep.tile([P, B], F32, name="inv")
         nc.vector.reciprocal(inv[:], total[:])
 
-        vx = []
-        for b in range(B):
-            turned = psum.tile([P, 2, 2, P], F32, name=f"v_ps{b}", tag=("v", "w0")[b])
-            for h in (1, 0):
-                for u in range(2):
-                    nc.tensor.transpose(turned[:, h, u, :], gv[h, b][:, u * N // 2 : (u + 1) * N // 2].bitcast(F32), ident[:])
-            values = keep.tile([P, DV * PACK], BF16, name=f"vx{b}", align_bytes=64)
-            nc.scalar.copy(
-                values[:].bitcast(F32).rearrange("p (h e u) -> p h e u", h=2, u=2),
-                turned[:].rearrange("p h u e -> p h e u"),
-            )
-            vx.append(values)
+        def turn_values(turned, b, h):
+            for u in range(2):
+                nc.tensor.transpose(turned[:, u, :], gv[h, b][:, u * N // 2 : (u + 1) * N // 2].bitcast(F32), ident[:])
+
+        turned = psum.tile([P, 2, 2, P], F32, name="v_ps0", tag="v")
+        for h in (1, 0):
+            turn_values(turned[:, h], 0, h)
+        vx0 = keep.tile([P, DV * PACK], BF16, name="vx0", align_bytes=64)
+        nc.scalar.copy(
+            vx0[:].bitcast(F32).rearrange("p (h e u) -> p h e u", h=2, u=2),
+            turned[:].rearrange("p h u e -> p h e u"),
+        )
+        vx1 = {}
+        for h, bank in ((1, "w0"), (0, "y1")):
+            turned = psum.tile([P, 2, P], F32, name=f"v_ps1_{h}", tag=bank)
+            turn_values(turned[:], 1, h)
+            vx1[h] = keep.tile([P, P * PACK], BF16, name=f"vx1_{h}", align_bytes=64)
+            nc.scalar.copy(vx1[h][:].bitcast(F32).rearrange("p (e u) -> p e u", u=2), turned[:].rearrange("p u e -> p e u"))
 
         v0_codes = keep.tile([P, DV], U32, name="v0_c", tag="after_turn1", align_bytes=64)
-        v8 = [quantise("v0", vx[0][:], DV, v0_codes[:])]
+        v8 = quantise("v0", vx0[:], DV, v0_codes[:])
         w8 = quantise("w", wx[:].rearrange("p b q t -> p (b q t)"), B * NQ)
-        v8.append(quantise("v1", vx[1][:], DV))
-        for b in range(B):
-            y = psum.tile([P, DV], F32, name=f"y_ps{b}", tag=f"s{b}")
-            product(y, w8, slice(b * NQ, (b + 1) * NQ), v8[b])
-            y_sb = keep.tile([P, DV], F32, name=f"y_sb{b}")
-            nc.scalar.activation(y_sb[:], y[:], ACT.Copy, scale=inv[:, b : b + 1])
-            nc.sync.dma_start(out[b], y_sb[:])
+        y = psum.tile([P, DV], F32, name="y_ps0", tag="s0")
+        product(y, w8, slice(0, NQ), v8)
+        y0_sb = keep.tile([P, DV], F32, name="y0_sb")
+        nc.scalar.activation(y0_sb[:], y[:], ACT.Copy, scale=inv[:, 0:1])
+        nc.sync.dma_start(out[0], y0_sb[:])
+
+        y1 = {}
+        for h, bank in ((1, "s1"), (0, "y0")):
+            y1[h] = psum.tile([P, P], F32, name=f"y_ps1_{h}", tag=bank)
+            product(y1[h], w8, slice(NQ, 2 * NQ), quantise(f"v1_{h}", vx1[h][:], P))
+        y1_sb = keep.tile([P, DV], F32, name="y1_sb")
+        nc.scalar.activation(y1_sb[:, P:DV], y1[1][:], ACT.Copy, scale=inv[:, 1:2])
+        nc.vector.tensor_scalar(y1_sb[:, 0:P], y1[0][:], inv[:, 1:2], None, ALU.mult)
+        nc.sync.dma_start(out[1], y1_sb[:])

@@ -6,6 +6,7 @@ from concourse.masks import make_identity
 B, N, T, D, DV, NQ, NEW = 2, 512, 2048, 512, 256, 128, 256
 P = 128
 PACK = 4
+CAP = 2.0
 FLOPS = 2 * B * NQ * N * (D + DV)
 BYTES = 4 * (B * D * NQ + D * T + DV * T + D * NEW + DV * NEW + T + B * NQ * DV) + 2 * P * (B * N + NEW) // 16
 
@@ -19,8 +20,9 @@ ACT = mybir.ActivationFunctionType
 ALU = mybir.AluOpType
 
 PAD = 16
-SPLIT = 288
-HALF = T // 2
+SPLIT = 256
+RUN = 4
+VS_ROW = P - 1
 
 
 def tile_attend_x_append256_cap_kernel(tc, qT, kT, vT, new_kT, new_vT, vs, offs, slots, out):
@@ -31,38 +33,35 @@ def tile_attend_x_append256_cap_kernel(tc, qT, kT, vT, new_kT, new_vT, vs, offs,
 
         offs_t = keep.tile([P, B * N // 16], U16, name="offs_t")
         slots_t = keep.tile([P, NEW // 16], U16, name="slots_t")
-        gk = keep.tile([P, PACK * B * (N + PAD)], BF16, name="gk", align_bytes=64)
-        planes = gk[:].rearrange("p (t b s) -> p t b s", t=PACK, b=B)
-        new_k0 = keep.tile([P, NEW], F32, name="new_k0")
-        new_k1 = keep.tile([P, NEW], F32, name="new_k1")
-        new_k2 = gk[:, B * (N + PAD) : B * (N + PAD) + N].bitcast(F32)
-        new_k3 = keep.tile([P, NEW], F32, name="new_k3")
+        gathered_k = keep.tile([P, PACK * B * (N + PAD)], BF16, name="gathered_k", align_bytes=64)
+        planes = gathered_k[:].rearrange("p (t b s) -> p t b s", t=PACK, b=B)
+        new_k0 = keep.tile([P, NEW], F32, name="new_k0", tag="after_k0")
+        new_k12 = keep.tile([P, 2, NEW], F32, name="new_k12")
+        held_run = (2 * B + 1) * (N + PAD)
+        new_k3 = gathered_k[:, held_run : held_run + N].bitcast(F32)
+        new_k = [new_k0[:], new_k12[:, 0, :], new_k12[:, 1, :], new_k3]
         new_v = [keep.tile([P, NEW], F32, name=f"new_v{h}", tag=f"after_v{h}", align_bytes=64) for h in range(2)]
         q_raw = keep.tile([P, B, PACK, NQ], F32, name="q_raw", tag="after_q", align_bytes=64)
-        vs_t = keep.tile([P, T], F32, name="vs_t")
-        k_whole = {t: keep.tile([P, T], F32, name=f"k{t}") for t in (0, 3)}
-        k_half = {t: [keep.tile([P, HALF], F32, name=f"k{t}_{a}") for a in range(2)] for t in (1, 2)}
-        v0 = keep.tile([P, T], F32, name="v0", tag="after_cast")
-        v1 = keep.tile([P, T], F32, name="v1")
+        vs_win = keep.tile([P, T], F32, name="vs_win")
+        k_win = [keep.tile([P, T], F32, name=f"k{t}") for t in range(PACK)]
+        v0_win = keep.tile([P, T], F32, name="v0_win", tag="after_cast", align_bytes=32)
+        v1_win = keep.tile([P, T], F32, name="v1_win")
 
         k_hbm = kT.rearrange("(p j) w -> p j w", j=PACK)
-        nk_hbm = new_kT.rearrange("(p j) w -> p j w", j=PACK)
-        nc.vector.memset(vs_t[0 : P - 1, :], 0.0)
-        nc.sync.dma_start(vs_t[P - 1 : P, :], vs[0:1, :])
+        new_k_hbm = new_kT.rearrange("(p j) w -> p j w", j=PACK)
+        nc.vector.memset(vs_win[0:VS_ROW, :], 0.0)
+        nc.scalar.dma_start(vs_win[VS_ROW:P, :], vs[0:1, :])
         nc.sync.dma_start(offs_t[:], offs)
         nc.sync.dma_start(slots_t[:], slots)
-        nc.sync.dma_start(new_k0[:], nk_hbm[:, 0, :])
-        nc.sync.dma_start(k_whole[0][:], k_hbm[:, 0, :])
-        nc.sync.dma_start(new_k1[:], nk_hbm[:, 1, :])
-        for a in range(2):
-            nc.sync.dma_start(k_half[1][a][:], k_hbm[:, 1, a * HALF : (a + 1) * HALF])
-        for a in range(2):
-            nc.sync.dma_start(k_half[2][a][:], k_hbm[:, 2, a * HALF : (a + 1) * HALF])
-        nc.sync.dma_start(new_k2, nk_hbm[:, 2, :])
-        nc.sync.dma_start(new_k3[:], nk_hbm[:, 3, :])
-        nc.sync.dma_start(k_whole[3][:], k_hbm[:, 3, :])
+        nc.sync.dma_start(new_k0[:], new_k_hbm[:, 0, :])
+        nc.sync.dma_start(k_win[0][:], k_hbm[:, 0, :])
+        nc.sync.dma_start(new_k12[:], new_k_hbm[:, 1:3, :])
+        for t in (1, 2):
+            nc.sync.dma_start(k_win[t][:], k_hbm[:, t, :])
+        nc.sync.dma_start(new_k3, new_k_hbm[:, 3, :])
+        nc.sync.dma_start(k_win[3][:], k_hbm[:, 3, :])
         nc.sync.dma_start(q_raw[:], qT.rearrange("b (p j) w -> p b j w", j=PACK))
-        for h, window in enumerate((v0, v1)):
+        for h, window in enumerate((v0_win, v1_win)):
             nc.sync.dma_start(new_v[h][:], new_vT[h * P : (h + 1) * P, :])
             nc.sync.dma_start(window[:], vT[h * P : (h + 1) * P, :])
 
@@ -75,51 +74,45 @@ def tile_attend_x_append256_cap_kernel(tc, qT, kT, vT, new_kT, new_vT, vs, offs,
         def append(window, new):
             nc.vector.tensor_copy(window[:].indirect(slots_t[:]), new)
 
-        def rounded(name, new, copy):
-            tile = keep.tile([P, NEW], BF16, name=name)
-            copy(tile[:], new)
-            return tile[:]
-
-        def cast(name, halves):
-            tile = keep.tile([P, T], BF16, name=name)
-            nc.scalar.copy(tile[:, 0:HALF], halves[0][:])
-            nc.scalar.copy(tile[:, HALF:T], halves[1][:])
-            return tile
-
-        vsg = keep.tile([P, B * N], F32, name="vsg")
-        nc.vector.tensor_copy(vsg[:], vs_t[:].indirect(offs_t[:]))
         vs_ps = []
-        for b in range(B):
-            turned = psum.tile([P, PACK, P], F32, name=f"vs_ps{b}", tag=f"y{b}")
+
+        def turn_scales(b, tag):
+            gathered = keep.tile([P, N], F32, name=f"gathered_vs{b}", tag=tag)
+            nc.vector.tensor_copy(gathered[:], vs_win[:].indirect(seq_offs(b)))
+            turned = psum.tile([P, PACK, P], F32, name=f"vs_ps{b}", tag=f"scales{b}")
             for t in range(PACK):
-                nc.tensor.transpose(turned[:, t, :], vsg[:, b * N + t : (b + 1) * N : PACK], ident[:])
+                nc.tensor.transpose(turned[:, t, :], gathered[:, t:N:PACK], ident[:])
             vs_ps.append(turned)
 
-        append(k_whole[0], new_k0[:])
-        nc.vector.tensor_copy(planes[:, 0, :, 0:N], k_whole[0][:].indirect(offs_t[:]))
-        new_k1_16 = rounded("new_k1_16", new_k1[:], nc.scalar.copy)
-        k16 = {t: cast(f"k16_{t}", k_half[t]) for t in (1, 2)}
-        append(k16[1], new_k1_16)
-        append(k16[2], rounded("new_k2_16", new_k2, nc.vector.tensor_copy))
-        append(k_whole[3], new_k3[:])
-        for t in (1, 2):
-            nc.scalar.activation(planes[:, t, :, 0:N], k16[t][:].indirect(offs_t[:]), ACT.Copy)
-        for b in range(B):
-            nc.vector.tensor_copy(planes[:, 3, b, 0:N], k_whole[3][:].indirect(seq_offs(b)))
+        def scalar_plane(t):
+            append(k_win[t], new_k[t])
+            k16 = keep.tile([P, T], BF16, name=f"k16_{t}")
+            nc.scalar.copy(k16[:], k_win[t][:])
+            nc.scalar.activation(planes[:, t, :, 0:N], k16[:].indirect(offs_t[:]), ACT.Copy)
+
+        turn_scales(0, "gathered_vs0")
+        scalar_plane(0)
+        turn_scales(1, "after_k0")
+        scalar_plane(1)
+        append(k_win[2], new_k[2])
+        nc.vector.tensor_copy(planes[:, 2, 0, 0:N], k_win[2][:].indirect(seq_offs(0)))
+        append(k_win[3], new_k[3])
+        for t, b in ((3, 0), (2, 1), (3, 1)):
+            nc.vector.tensor_copy(planes[:, t, b, 0:N], k_win[t][:].indirect(seq_offs(b)))
 
         qx = keep.tile([P, B, NQ, PACK], BF16, name="qx", align_bytes=64)
         nc.gpsimd.tensor_scalar(qx[:, 0], q_raw[:, 0].rearrange("p j w -> p w j"), 1.0, 0.0, ALU.mult, ALU.add)
         nc.scalar.copy(
-            qx[:, 1].rearrange("p (c i) j -> p c j i", i=4),
-            q_raw[:, 1].rearrange("p j (c i) -> p c j i", i=4),
+            qx[:, 1].rearrange("p (c i) j -> p c j i", i=RUN),
+            q_raw[:, 1].rearrange("p j (c i) -> p c j i", i=RUN),
         )
 
         kx_both = keep.tile([P, B * N * PACK], BF16, name="kx", tag="after_q", align_bytes=64)
         kx = [kx_both[:, b * N * PACK : (b + 1) * N * PACK] for b in range(B)]
         for b in range(B):
             nc.scalar.copy(
-                kx[b][:, 0 : SPLIT * PACK].rearrange("p (c i t) -> p c t i", i=4, t=PACK),
-                planes[:, :, b, 0:SPLIT].rearrange("p t (c i) -> p c t i", i=4),
+                kx[b][:, 0 : SPLIT * PACK].rearrange("p (c i t) -> p c t i", i=RUN, t=PACK),
+                planes[:, :, b, 0:SPLIT].rearrange("p t (c i) -> p c t i", i=RUN),
             )
             nc.gpsimd.tensor_scalar(
                 kx[b][:, SPLIT * PACK :].rearrange("p (s t) -> p s t", t=PACK),
@@ -130,12 +123,13 @@ def tile_attend_x_append256_cap_kernel(tc, qT, kT, vT, new_kT, new_vT, vs, offs,
                 ALU.add,
             )
 
-        def quantise(name, src, width, codes=None):
-            if codes is None:
-                codes = keep.tile([P, width], U32, name=f"{name}_c", align_bytes=64)[:]
-            scale = keep.tile([P, width], U8, name=f"{name}_s", align_bytes=64)
+        def quantise(name, src, codes):
+            scale = keep.tile([P, codes.shape[1]], U8, name=f"{name}_scale", align_bytes=64)
             nc.vector.quantize_mx(out=codes.bitcast(FP8X4), scales=scale[:], in_=src)
             return codes, scale
+
+        def code_tile(name, width, tag):
+            return keep.tile([P, width], U32, name=name, tag=tag, align_bytes=64)[:]
 
         def product(acc, lhs, cols, rhs):
             nc.tensor.matmul_mx(
@@ -148,64 +142,70 @@ def tile_attend_x_append256_cap_kernel(tc, qT, kT, vT, new_kT, new_vT, vs, offs,
                 stop=True,
             )
 
-        append(v0, new_v[0][:])
+        append(v0_win, new_v[0][:])
         v16 = keep.tile([P, T], BF16, name="v16")
-        nc.scalar.copy(v16[:], v0[:])
-        qk_codes = keep.tile([P, B * (NQ + N)], U32, name="qk_codes", tag="after_v0", align_bytes=64)
+        nc.scalar.copy(v16[:], v0_win[:])
+        qk_codes = code_tile("qk_codes", B * (NQ + N), "after_v0")
         k_codes = qk_codes[:, B * NQ :]
-        q8 = quantise("q", qx[:].rearrange("p b w j -> p (b w j)"), B * NQ, qk_codes[:, 0 : B * NQ])
+        q8 = quantise("q", qx[:].rearrange("p b w j -> p (b w j)"), qk_codes[:, 0 : B * NQ])
         scores = []
         for b in range(B):
-            acc = psum.tile([P, N], F32, name=f"s_ps{b}", tag=f"s{b}")
-            product(acc, q8, slice(b * NQ, (b + 1) * NQ), quantise(f"k{b}", kx[b], N, k_codes[:, b * N : (b + 1) * N]))
+            acc = psum.tile([P, N], F32, name=f"score_ps{b}", tag=f"score{b}")
+            product(acc, q8, slice(b * NQ, (b + 1) * NQ), quantise(f"k{b}", kx[b], k_codes[:, b * N : (b + 1) * N]))
             scores.append(acc)
-        append(v1, new_v[1][:])
+        append(v1_win, new_v[1][:])
 
-        dealt = "p (u s e) -> p s u e"
-        gv = {}
+        gathered_v = {}
 
         def gather_v(h, b, tag):
-            gv[h, b] = keep.tile([P, N], BF16, name=f"gv{h}_{b}", tag=tag, align_bytes=64)
-            runs = gv[h, b][:].rearrange(dealt, u=2, e=2)
+            gathered_v[h, b] = keep.tile([P, N], BF16, name=f"gathered_v{h}_{b}", tag=tag, align_bytes=64)
+            runs = gathered_v[h, b][:].rearrange("p (u s e) -> p s u e", u=2, e=2)
             if h == 0:
                 nc.scalar.activation(runs, v16[:].indirect(seq_offs(b)), ACT.Copy)
             else:
-                nc.vector.tensor_copy(runs, v1[:].indirect(seq_offs(b)))
+                nc.vector.tensor_copy(runs, v1_win[:].indirect(seq_offs(b)))
 
-        gather_v(1, 0, "gv1_0")
-        capped = [keep.tile([P, PACK, P], F32, name=f"th{b}", tag=("after_exp0", "th1")[b], align_bytes=64) for b in range(B)]
+        gather_v(1, 0, "gathered_v1_0")
+
+        capped = [keep.tile([P, PACK, P], F32, name=f"tanh{b}", tag=f"after_exp{b}", align_bytes=64) for b in range(B)]
         for b in range(B):
-            nc.scalar.activation(capped[b][:], scores[b][:].rearrange("q (s t) -> q t s", t=PACK), ACT.Tanh, scale=0.5)
-        vsT = keep.tile([P, B, 8], F32, name="vsT", tag="after_cast")
-        for b in range(B):
-            nc.scalar.copy(vsT[:, b, 0:PACK], vs_ps[b][:, :, P - 1])
+            nc.scalar.activation(capped[b][:], scores[b][:].rearrange("q (s t) -> q t s", t=PACK), ACT.Tanh, scale=1.0 / CAP)
+
+        scales = []
+
+        def keep_scales(b, tag, align):
+            scales.append(keep.tile([P, PACK], F32, name=f"scales{b}", tag=tag, align_bytes=align))
+            nc.scalar.copy(scales[b][:], vs_ps[b][:, :, VS_ROW])
+
+        keep_scales(0, "after_cast", 32)
 
         minus_m = []
         for b in range(B):
-            scaled = keep.tile([P, N], F32, name=f"scaled{b}", tag=("after_v1", "after_max1")[b], align_bytes=64)
-            one = keep.tile([P, 1], F32, name=f"nm{b}")
-            nc.vector.tensor_scalar(scaled[:], capped[b][:].rearrange("q t s -> q (t s)"), -2.0, None, ALU.mult, ALU.min, accum_out=one[:])
-            minus_m.append(one)
+            negated = keep.tile([P, N], F32, name=f"negated{b}", tag=("after_v1", "after_max1")[b], align_bytes=64)
+            column = keep.tile([P, 1], F32, name=f"minus_m{b}")
+            nc.vector.tensor_scalar(negated[:], capped[b][:].rearrange("q t s -> q (t s)"), -CAP, None, ALU.mult, ALU.min, accum_out=column[:])
+            minus_m.append(column)
         gather_v(1, 1, "after_max1")
 
         total = keep.tile([P, B], F32, name="total")
-        gather_v(0, 0, "gv0_0")
+        gather_v(0, 0, "gathered_v0_0")
         prob = []
         for b in range(B):
             p = keep.tile([P, PACK, P], F32, name=f"p{b}", tag=("p0", "after_turn1")[b], align_bytes=64)
-            nc.scalar.activation(p[:], capped[b][:], ACT.Exp, bias=minus_m[b][:], scale=2.0, accum_out=total[:, b : b + 1])
+            nc.scalar.activation(p[:], capped[b][:], ACT.Exp, bias=minus_m[b][:], scale=CAP, accum_out=total[:, b : b + 1])
             prob.append(p)
         gather_v(0, 1, "after_exp0")
+        keep_scales(1, "after_exp1", 64)
 
         wx = keep.tile([P, B, NQ, PACK], BF16, name="wx", align_bytes=64)
         for b in range(B):
-            turned = psum.tile([P, PACK, P], F32, name=f"w_ps{b}", tag=f"w{b}")
+            turned = psum.tile([P, PACK, P], F32, name=f"w_ps{b}", tag=f"weights{b}")
             for t in range(PACK):
                 nc.tensor.transpose(turned[:, t, :], prob[b][:, t, :], ident[:])
             nc.vector.tensor_tensor(
                 wx[:, b],
                 turned[:].rearrange("p t q -> p q t"),
-                vsT[:, b, 0:PACK].unsqueeze(1).to_broadcast([P, NQ, PACK]),
+                scales[b][:].unsqueeze(1).to_broadcast([P, NQ, PACK]),
                 ALU.mult,
             )
         inv = keep.tile([P, B], F32, name="inv")
@@ -213,9 +213,10 @@ def tile_attend_x_append256_cap_kernel(tc, qT, kT, vT, new_kT, new_vT, vs, offs,
 
         def turn_values(turned, b, h):
             for u in range(2):
-                nc.tensor.transpose(turned[:, u, :], gv[h, b][:, u * N // 2 : (u + 1) * N // 2].bitcast(F32), ident[:])
+                run = gathered_v[h, b][:, u * N // 2 : (u + 1) * N // 2]
+                nc.tensor.transpose(turned[:, u, :], run.bitcast(F32), ident[:])
 
-        turned = psum.tile([P, 2, 2, P], F32, name="v_ps0", tag="v")
+        turned = psum.tile([P, 2, 2, P], F32, name="v_ps0", tag="values0")
         for h in (1, 0):
             turn_values(turned[:, h], 0, h)
         vx0 = keep.tile([P, DV * PACK], BF16, name="vx0", align_bytes=64)
@@ -224,25 +225,26 @@ def tile_attend_x_append256_cap_kernel(tc, qT, kT, vT, new_kT, new_vT, vs, offs,
             turned[:].rearrange("p h u e -> p h e u"),
         )
         vx1 = {}
-        for h, bank in ((1, "w0"), (0, "y1")):
+        for h, bank in ((1, "scales1"), (0, "values1")):
             turned = psum.tile([P, 2, P], F32, name=f"v_ps1_{h}", tag=bank)
             turn_values(turned[:], 1, h)
             vx1[h] = keep.tile([P, P * PACK], BF16, name=f"vx1_{h}", align_bytes=64)
             nc.scalar.copy(vx1[h][:].bitcast(F32).rearrange("p (e u) -> p e u", u=2), turned[:].rearrange("p u e -> p e u"))
 
-        v0_codes = keep.tile([P, DV], U32, name="v0_c", tag="after_turn1", align_bytes=64)
-        v8 = quantise("v0", vx0[:], DV, v0_codes[:])
-        w8 = quantise("w", wx[:].rearrange("p b q t -> p (b q t)"), B * NQ)
-        y = psum.tile([P, DV], F32, name="y_ps0", tag="s0")
-        product(y, w8, slice(0, NQ), v8)
+        queries = slice(0, NQ)
+        w8 = quantise("w0", wx[:, 0].rearrange("p q t -> p (q t)"), code_tile("w0_codes", NQ, "after_turn1"))
+        v8 = quantise("v0", vx0[:], code_tile("v0_codes", DV, "v0_codes"))
+        y0 = psum.tile([P, DV], F32, name="y_ps0", tag="score0")
+        product(y0, w8, queries, v8)
         y0_sb = keep.tile([P, DV], F32, name="y0_sb")
-        nc.scalar.activation(y0_sb[:], y[:], ACT.Copy, scale=inv[:, 0:1])
+        nc.scalar.activation(y0_sb[:], y0[:], ACT.Copy, scale=inv[:, 0:1])
         nc.sync.dma_start(out[0], y0_sb[:])
 
+        w8 = quantise("w1", wx[:, 1].rearrange("p q t -> p (q t)"), code_tile("w1_codes", NQ, "w1_codes"))
         y1 = {}
-        for h, bank in ((1, "s1"), (0, "y0")):
+        for h, bank in ((1, "score1"), (0, "scales0")):
             y1[h] = psum.tile([P, P], F32, name=f"y_ps1_{h}", tag=bank)
-            product(y1[h], w8, slice(NQ, 2 * NQ), quantise(f"v1_{h}", vx1[h][:], P))
+            product(y1[h], w8, queries, quantise(f"v1_{h}", vx1[h][:], code_tile(f"v1_{h}_codes", P, f"v1_{h}_codes")))
         y1_sb = keep.tile([P, DV], F32, name="y1_sb")
         nc.scalar.activation(y1_sb[:, P:DV], y1[1][:], ACT.Copy, scale=inv[:, 1:2])
         nc.vector.tensor_scalar(y1_sb[:, 0:P], y1[0][:], inv[:, 1:2], None, ALU.mult)

@@ -20,7 +20,6 @@ ACT = mybir.ActivationFunctionType
 ALU = mybir.AluOpType
 
 PAD = 16
-SPLIT = 256
 RUN = 4
 VS_ROW = P - 1
 
@@ -33,19 +32,17 @@ def tile_attend_x_append256_cap_kernel(tc, qT, kT, vT, new_kT, new_vT, vs, offs,
 
         offs_t = keep.tile([P, B * N // 16], U16, name="offs_t")
         slots_t = keep.tile([P, NEW // 16], U16, name="slots_t")
-        gathered_k = keep.tile([P, PACK * B * (N + PAD)], BF16, name="gathered_k", align_bytes=64)
-        planes = gathered_k[:].rearrange("p (t b s) -> p t b s", t=PACK, b=B)
-        new_k0 = keep.tile([P, NEW], F32, name="new_k0", tag="after_k0")
-        new_k12 = keep.tile([P, 2, NEW], F32, name="new_k12")
-        held_run = (2 * B + 1) * (N + PAD)
-        new_k3 = gathered_k[:, held_run : held_run + N].bitcast(F32)
-        new_k = [new_k0[:], new_k12[:, 0, :], new_k12[:, 1, :], new_k3]
-        new_v = [keep.tile([P, NEW], F32, name=f"new_v{h}", tag=f"after_v{h}", align_bytes=64) for h in range(2)]
+        seq_width = PACK * (N + PAD)
+        gathered = keep.tile([P, B * seq_width], BF16, name="gathered", align_bytes=64)
+        planes = gathered[:].rearrange("p (b t s) -> p b t s", b=B, t=PACK)
+        new_k0 = keep.tile([P, NEW], F32, name="new_k0")
+        new_k123 = keep.tile([P, PACK - 1, NEW], F32, name="new_k123")
+        new_k = [new_k0[:]] + [new_k123[:, t, :] for t in range(PACK - 1)]
+        new_v = keep.tile([P, 2, NEW], F32, name="new_v")
         q_raw = keep.tile([P, B, PACK, NQ], F32, name="q_raw", tag="after_q", align_bytes=64)
         vs_win = keep.tile([P, T], F32, name="vs_win")
         k_win = [keep.tile([P, T], F32, name=f"k{t}") for t in range(PACK)]
-        v0_win = keep.tile([P, T], F32, name="v0_win", tag="after_cast", align_bytes=32)
-        v1_win = keep.tile([P, T], F32, name="v1_win")
+        v_win = [keep.tile([P, T], F32, name=f"v{h}") for h in range(2)]
 
         k_hbm = kT.rearrange("(p j) w -> p j w", j=PACK)
         new_k_hbm = new_kT.rearrange("(p j) w -> p j w", j=PACK)
@@ -55,15 +52,13 @@ def tile_attend_x_append256_cap_kernel(tc, qT, kT, vT, new_kT, new_vT, vs, offs,
         nc.sync.dma_start(slots_t[:], slots)
         nc.sync.dma_start(new_k0[:], new_k_hbm[:, 0, :])
         nc.sync.dma_start(k_win[0][:], k_hbm[:, 0, :])
-        nc.sync.dma_start(new_k12[:], new_k_hbm[:, 1:3, :])
-        for t in (1, 2):
+        nc.sync.dma_start(new_k123[:], new_k_hbm[:, 1:PACK, :])
+        for t in range(1, PACK):
             nc.sync.dma_start(k_win[t][:], k_hbm[:, t, :])
-        nc.sync.dma_start(new_k3, new_k_hbm[:, 3, :])
-        nc.sync.dma_start(k_win[3][:], k_hbm[:, 3, :])
         nc.sync.dma_start(q_raw[:], qT.rearrange("b (p j) w -> p b j w", j=PACK))
-        for h, window in enumerate((v0_win, v1_win)):
-            nc.sync.dma_start(new_v[h][:], new_vT[h * P : (h + 1) * P, :])
-            nc.sync.dma_start(window[:], vT[h * P : (h + 1) * P, :])
+        nc.sync.dma_start(new_v[:], new_vT.rearrange("(h p) w -> p h w", p=P))
+        for h in range(2):
+            nc.sync.dma_start(v_win[h][:], vT[h * P : (h + 1) * P, :])
 
         ident = keep.tile([P, P], F32, name="ident")
         make_identity(nc, ident[:])
@@ -74,178 +69,149 @@ def tile_attend_x_append256_cap_kernel(tc, qT, kT, vT, new_kT, new_vT, vs, offs,
         def append(window, new):
             nc.vector.tensor_copy(window[:].indirect(slots_t[:]), new)
 
-        vs_ps = []
-
-        def turn_scales(b, tag):
-            gathered = keep.tile([P, N], F32, name=f"gathered_vs{b}", tag=tag)
-            nc.vector.tensor_copy(gathered[:], vs_win[:].indirect(seq_offs(b)))
+        gathered_vs = keep.tile([P, B * N], F32, name="gathered_vs")
+        nc.vector.tensor_copy(gathered_vs[:], vs_win[:].indirect(offs_t[:]))
+        scales = []
+        for b in range(B):
             turned = psum.tile([P, PACK, P], F32, name=f"vs_ps{b}", tag=f"scales{b}")
             for t in range(PACK):
-                nc.tensor.transpose(turned[:, t, :], gathered[:, t:N:PACK], ident[:])
-            vs_ps.append(turned)
+                nc.tensor.transpose(turned[:, t, :], gathered_vs[:, b * N + t : (b + 1) * N : PACK], ident[:])
+            scales.append(keep.tile([P, PACK], F32, name=f"scales{b}"))
+            nc.scalar.copy(scales[b][:], turned[:, :, VS_ROW])
 
-        def scalar_plane(t):
+        for t in range(PACK):
             append(k_win[t], new_k[t])
-            k16 = keep.tile([P, T], BF16, name=f"k16_{t}")
-            nc.scalar.copy(k16[:], k_win[t][:])
-            nc.scalar.activation(planes[:, t, :, 0:N], k16[:].indirect(offs_t[:]), ACT.Copy)
-
-        turn_scales(0, "gathered_vs0")
-        scalar_plane(0)
-        turn_scales(1, "after_k0")
-        scalar_plane(1)
-        append(k_win[2], new_k[2])
-        nc.vector.tensor_copy(planes[:, 2, 0, 0:N], k_win[2][:].indirect(seq_offs(0)))
-        append(k_win[3], new_k[3])
-        for t, b in ((3, 0), (2, 1), (3, 1)):
-            nc.vector.tensor_copy(planes[:, t, b, 0:N], k_win[t][:].indirect(seq_offs(b)))
+            if t < PACK - 1:
+                nc.vector.tensor_copy(planes[:, :, t, 0:N], k_win[t][:].indirect(offs_t[:]))
+            else:
+                for b in range(B):
+                    nc.vector.tensor_copy(planes[:, b, t, 0:N], k_win[t][:].indirect(seq_offs(b)))
 
         qx = keep.tile([P, B, NQ, PACK], BF16, name="qx", align_bytes=64)
-        nc.gpsimd.tensor_scalar(qx[:, 0], q_raw[:, 0].rearrange("p j w -> p w j"), 1.0, 0.0, ALU.mult, ALU.add)
         nc.scalar.copy(
-            qx[:, 1].rearrange("p (c i) j -> p c j i", i=RUN),
-            q_raw[:, 1].rearrange("p j (c i) -> p c j i", i=RUN),
+            qx[:].rearrange("p b (c i) j -> p b c j i", i=RUN),
+            q_raw[:].rearrange("p b j (c i) -> p b c j i", i=RUN),
         )
-
         kx_both = keep.tile([P, B * N * PACK], BF16, name="kx", tag="after_q", align_bytes=64)
         kx = [kx_both[:, b * N * PACK : (b + 1) * N * PACK] for b in range(B)]
         for b in range(B):
             nc.scalar.copy(
-                kx[b][:, 0 : SPLIT * PACK].rearrange("p (c i t) -> p c t i", i=RUN, t=PACK),
-                planes[:, :, b, 0:SPLIT].rearrange("p t (c i) -> p c t i", i=RUN),
-            )
-            nc.gpsimd.tensor_scalar(
-                kx[b][:, SPLIT * PACK :].rearrange("p (s t) -> p s t", t=PACK),
-                planes[:, :, b, SPLIT:N].rearrange("p t s -> p s t"),
-                1.0,
-                0.0,
-                ALU.mult,
-                ALU.add,
+                kx[b].rearrange("p (c i t) -> p c t i", i=RUN, t=PACK),
+                planes[:, b, :, 0:N].rearrange("p t (c i) -> p c t i", i=RUN),
             )
 
-        def quantise(name, src, codes):
-            scale = keep.tile([P, codes.shape[1]], U8, name=f"{name}_scale", align_bytes=64)
-            nc.vector.quantize_mx(out=codes.bitcast(FP8X4), scales=scale[:], in_=src)
+        def quantise(name, src, width):
+            codes = keep.tile([P, width], U32, name=f"{name}_codes", align_bytes=64)
+            scale = keep.tile([P, width], U8, name=f"{name}_scale", align_bytes=64)
+            nc.vector.quantize_mx(out=codes[:].bitcast(FP8X4), scales=scale[:], in_=src)
             return codes, scale
 
-        def code_tile(name, width, tag):
-            return keep.tile([P, width], U32, name=name, tag=tag, align_bytes=64)[:]
-
-        def product(acc, lhs, cols, rhs):
+        def product(acc, lhs, lhs_cols, rhs, rhs_cols):
             nc.tensor.matmul_mx(
-                out=acc[:],
-                lhsT=lhs[0][:, cols].bitcast(FP8X4),
-                lhsT_scale=lhs[1][:, cols],
-                rhs=rhs[0].bitcast(FP8X4),
-                rhs_scale=rhs[1][:],
+                out=acc,
+                lhsT=lhs[0][:, lhs_cols].bitcast(FP8X4),
+                lhsT_scale=lhs[1][:, lhs_cols],
+                rhs=rhs[0][:, rhs_cols].bitcast(FP8X4),
+                rhs_scale=rhs[1][:, rhs_cols],
                 start=True,
                 stop=True,
             )
 
-        append(v0_win, new_v[0][:])
-        v16 = keep.tile([P, T], BF16, name="v16")
-        nc.scalar.copy(v16[:], v0_win[:])
-        qk_codes = code_tile("qk_codes", B * (NQ + N), "after_v0")
-        k_codes = qk_codes[:, B * NQ :]
-        q8 = quantise("q", qx[:].rearrange("p b w j -> p (b w j)"), qk_codes[:, 0 : B * NQ])
+        def turn_values(turned, values):
+            words = values.bitcast(F32)
+            for u in range(2):
+                nc.tensor.transpose(turned[:, u, :], words[:, u : N // 2 : 2], ident[:])
+
+        q8 = quantise("q", qx[:].rearrange("p b w j -> p (b w j)"), B * NQ)
+        append(v_win[0], new_v[:, 0, :])
         scores = []
-        for b in range(B):
+
+        def score(b):
             acc = psum.tile([P, N], F32, name=f"score_ps{b}", tag=f"score{b}")
-            product(acc, q8, slice(b * NQ, (b + 1) * NQ), quantise(f"k{b}", kx[b], k_codes[:, b * N : (b + 1) * N]))
+            product(acc[:], q8, slice(b * NQ, (b + 1) * NQ), quantise(f"k{b}", kx[b], N), slice(0, N))
             scores.append(acc)
-        append(v1_win, new_v[1][:])
 
-        gathered_v = {}
+        score(0)
+        v0_both = gathered[:, 0 : B * N]
+        nc.vector.tensor_copy(v0_both, v_win[0][:].indirect(offs_t[:]))
+        append(v_win[1], new_v[:, 1, :])
+        score(1)
 
-        def gather_v(h, b, tag):
-            gathered_v[h, b] = keep.tile([P, N], BF16, name=f"gathered_v{h}_{b}", tag=tag, align_bytes=64)
-            runs = gathered_v[h, b][:].rearrange("p (u s e) -> p s u e", u=2, e=2)
-            if h == 0:
-                nc.scalar.activation(runs, v16[:].indirect(seq_offs(b)), ACT.Copy)
-            else:
-                nc.vector.tensor_copy(runs, v1_win[:].indirect(seq_offs(b)))
+        capped, minus_m, prob = [], [], []
+        total = keep.tile([P, B], F32, name="total")
 
-        gather_v(1, 0, "gathered_v1_0")
-
-        capped = [keep.tile([P, PACK, P], F32, name=f"tanh{b}", tag=f"after_exp{b}", align_bytes=64) for b in range(B)]
-        for b in range(B):
+        def cap(b):
+            capped.append(keep.tile([P, PACK, P], F32, name=f"tanh{b}", tag=f"after_exp{b}", align_bytes=64))
             nc.scalar.activation(capped[b][:], scores[b][:].rearrange("q (s t) -> q t s", t=PACK), ACT.Tanh, scale=1.0 / CAP)
 
-        scales = []
-
-        def keep_scales(b, tag, align):
-            scales.append(keep.tile([P, PACK], F32, name=f"scales{b}", tag=tag, align_bytes=align))
-            nc.scalar.copy(scales[b][:], vs_ps[b][:, :, VS_ROW])
-
-        keep_scales(0, "after_cast", 32)
-
-        minus_m = []
-        for b in range(B):
-            negated = keep.tile([P, N], F32, name=f"negated{b}", tag=("after_v1", "after_max1")[b], align_bytes=64)
+        def row_max(b):
+            negated = keep.tile([P, N], F32, name=f"negated{b}")
             column = keep.tile([P, 1], F32, name=f"minus_m{b}")
             nc.vector.tensor_scalar(negated[:], capped[b][:].rearrange("q t s -> q (t s)"), -CAP, None, ALU.mult, ALU.min, accum_out=column[:])
             minus_m.append(column)
-        gather_v(1, 1, "after_max1")
 
-        total = keep.tile([P, B], F32, name="total")
-        gather_v(0, 0, "gathered_v0_0")
-        prob = []
+        def exp(b):
+            prob.append(keep.tile([P, PACK, P], F32, name=f"p{b}"))
+            nc.scalar.activation(prob[b][:], capped[b][:], ACT.Exp, bias=minus_m[b][:], scale=CAP, accum_out=total[:, b : b + 1])
+
+        cap(0)
+        v0_ps = psum.tile([P, B, 2, P], F32, name="v0_ps", tag="values0")
         for b in range(B):
-            p = keep.tile([P, PACK, P], F32, name=f"p{b}", tag=("p0", "after_turn1")[b], align_bytes=64)
-            nc.scalar.activation(p[:], capped[b][:], ACT.Exp, bias=minus_m[b][:], scale=CAP, accum_out=total[:, b : b + 1])
-            prob.append(p)
-        gather_v(0, 1, "after_exp0")
-        keep_scales(1, "after_exp1", 64)
+            turn_values(v0_ps[:, b], v0_both[:, b * N : (b + 1) * N])
+        vx0 = keep.tile([P, B * P * PACK], BF16, name="vx0", align_bytes=64)
+        nc.scalar.copy(vx0[:].bitcast(F32).rearrange("p (b e u) -> p b e u", b=B, u=2), v0_ps[:].rearrange("p b u e -> p b e u"))
+        cap(1)
+        row_max(0)
+        v1_seq0 = gathered[:, seq_width : seq_width + N]
+        nc.vector.tensor_copy(v1_seq0, v_win[1][:].indirect(seq_offs(0)))
+        row_max(1)
+        exp(0)
+        v1_seq1 = keep.tile([P, N], BF16, name="v1_seq1", tag="after_exp0", align_bytes=64)
+        nc.vector.tensor_copy(v1_seq1[:], v_win[1][:].indirect(seq_offs(1)))
+        v0_8 = quantise("v0", vx0[:], B * P)
 
-        wx = keep.tile([P, B, NQ, PACK], BF16, name="wx", align_bytes=64)
+        vx1 = []
+
+        def lay_v1(b, values, bank):
+            turned = psum.tile([P, 2, P], F32, name=f"v1_ps{b}", tag=bank)
+            turn_values(turned, values)
+            vx1.append(keep.tile([P, P * PACK], BF16, name=f"vx1_{b}", align_bytes=64))
+            nc.scalar.copy(vx1[b][:].bitcast(F32).rearrange("p (e u) -> p e u", u=2), turned[:].rearrange("p u e -> p e u"))
+
+        lay_v1(0, v1_seq0, "values1")
+        exp(1)
+
+        wx = []
         for b in range(B):
             turned = psum.tile([P, PACK, P], F32, name=f"w_ps{b}", tag=f"weights{b}")
             for t in range(PACK):
                 nc.tensor.transpose(turned[:, t, :], prob[b][:, t, :], ident[:])
+            wx.append(keep.tile([P, NQ, PACK], BF16, name=f"wx{b}", align_bytes=64))
             nc.vector.tensor_tensor(
-                wx[:, b],
+                wx[b][:],
                 turned[:].rearrange("p t q -> p q t"),
                 scales[b][:].unsqueeze(1).to_broadcast([P, NQ, PACK]),
                 ALU.mult,
             )
+        lay_v1(1, v1_seq1[:], "weights0")
         inv = keep.tile([P, B], F32, name="inv")
         nc.vector.reciprocal(inv[:], total[:])
 
-        def turn_values(turned, b, h):
-            for u in range(2):
-                run = gathered_v[h, b][:, u * N // 2 : (u + 1) * N // 2]
-                nc.tensor.transpose(turned[:, u, :], run.bitcast(F32), ident[:])
-
-        turned = psum.tile([P, 2, 2, P], F32, name="v_ps0", tag="values0")
-        for h in (1, 0):
-            turn_values(turned[:, h], 0, h)
-        vx0 = keep.tile([P, DV * PACK], BF16, name="vx0", align_bytes=64)
-        nc.scalar.copy(
-            vx0[:].bitcast(F32).rearrange("p (h e u) -> p h e u", h=2, u=2),
-            turned[:].rearrange("p h u e -> p h e u"),
-        )
-        vx1 = {}
-        for h, bank in ((1, "scales1"), (0, "values1")):
-            turned = psum.tile([P, 2, P], F32, name=f"v_ps1_{h}", tag=bank)
-            turn_values(turned[:], 1, h)
-            vx1[h] = keep.tile([P, P * PACK], BF16, name=f"vx1_{h}", align_bytes=64)
-            nc.scalar.copy(vx1[h][:].bitcast(F32).rearrange("p (e u) -> p e u", u=2), turned[:].rearrange("p u e -> p e u"))
-
         queries = slice(0, NQ)
-        w8 = quantise("w0", wx[:, 0].rearrange("p q t -> p (q t)"), code_tile("w0_codes", NQ, "after_turn1"))
-        v8 = quantise("v0", vx0[:], code_tile("v0_codes", DV, "v0_codes"))
+        w8 = quantise("w0", wx[0][:].rearrange("p q t -> p (q t)"), NQ)
         y0 = psum.tile([P, DV], F32, name="y_ps0", tag="score0")
-        product(y0, w8, queries, v8)
+        product(y0[:, 0:P], w8, queries, v0_8, slice(0, P))
+        product(y0[:, P:DV], w8, queries, quantise("v1_0", vx1[0][:], P), slice(0, P))
         y0_sb = keep.tile([P, DV], F32, name="y0_sb")
         nc.scalar.activation(y0_sb[:], y0[:], ACT.Copy, scale=inv[:, 0:1])
         nc.sync.dma_start(out[0], y0_sb[:])
 
-        w8 = quantise("w1", wx[:, 1].rearrange("p q t -> p (q t)"), code_tile("w1_codes", NQ, "w1_codes"))
-        y1 = {}
-        for h, bank in ((1, "score1"), (0, "scales0")):
-            y1[h] = psum.tile([P, P], F32, name=f"y_ps1_{h}", tag=bank)
-            product(y1[h], w8, queries, quantise(f"v1_{h}", vx1[h][:], code_tile(f"v1_{h}_codes", P, f"v1_{h}_codes")))
+        w8 = quantise("w1", wx[1][:].rearrange("p q t -> p (q t)"), NQ)
+        y1_lo = psum.tile([P, P], F32, name="y1_lo", tag="score1")
+        product(y1_lo[:], w8, queries, v0_8, slice(P, 2 * P))
+        y1_hi = psum.tile([P, P], F32, name="y1_hi", tag="scales0")
+        product(y1_hi[:], w8, queries, quantise("v1_1", vx1[1][:], P), slice(0, P))
         y1_sb = keep.tile([P, DV], F32, name="y1_sb")
-        nc.scalar.activation(y1_sb[:, P:DV], y1[1][:], ACT.Copy, scale=inv[:, 1:2])
-        nc.vector.tensor_scalar(y1_sb[:, 0:P], y1[0][:], inv[:, 1:2], None, ALU.mult)
+        nc.scalar.activation(y1_sb[:, 0:P], y1_lo[:], ACT.Copy, scale=inv[:, 1:2])
+        nc.vector.tensor_scalar(y1_sb[:, P:DV], y1_hi[:], inv[:, 1:2], None, ALU.mult)
         nc.sync.dma_start(out[1], y1_sb[:])

@@ -22,6 +22,8 @@ ALU = mybir.AluOpType
 PAD = 16
 RUN = 4
 VS_ROW = P - 1
+VECTOR_CAST = (1216, 1216, 1216)
+SCALAR_SLOTS = (256, 320)
 
 
 def tile_attend_x_append256_cap_kernel(tc, qT, kT, vT, new_kT, new_vT, vs, offs, slots, out):
@@ -32,17 +34,14 @@ def tile_attend_x_append256_cap_kernel(tc, qT, kT, vT, new_kT, new_vT, vs, offs,
 
         offs_t = keep.tile([P, B * N // 16], U16, name="offs_t")
         slots_t = keep.tile([P, NEW // 16], U16, name="slots_t")
-        seq_width = PACK * (N + PAD)
-        gathered = keep.tile([P, B * seq_width], BF16, name="gathered", align_bytes=64)
-        planes = gathered[:].rearrange("p (b t s) -> p b t s", b=B, t=PACK)
-        new_k0 = keep.tile([P, NEW], F32, name="new_k0")
-        new_k123 = keep.tile([P, PACK - 1, NEW], F32, name="new_k123")
-        new_k = [new_k0[:]] + [new_k123[:, t, :] for t in range(PACK - 1)]
-        new_v = keep.tile([P, 2, NEW], F32, name="new_v")
+        gathered_k = keep.tile([P, B * PACK * (N + PAD)], BF16, name="gathered_k", align_bytes=64)
+        planes = gathered_k[:].rearrange("p (b t s) -> p b t s", b=B, t=PACK)
+        new_k = [keep.tile([P, NEW], F32, name=f"new_k{t}", tag=f"after_k{t}", align_bytes=32) for t in range(PACK)]
+        new_v = [keep.tile([P, NEW], F32, name=f"new_v{h}", tag=f"after_v{h}", align_bytes=64) for h in range(2)]
         q_raw = keep.tile([P, B, PACK, NQ], F32, name="q_raw", tag="after_q", align_bytes=64)
         vs_win = keep.tile([P, T], F32, name="vs_win")
         k_win = [keep.tile([P, T], F32, name=f"k{t}") for t in range(PACK)]
-        v_win = [keep.tile([P, T], F32, name=f"v{h}") for h in range(2)]
+        v_win = [keep.tile([P, T], F32, name=f"v{h}", tag=f"v_win{h}", align_bytes=32) for h in range(2)]
 
         k_hbm = kT.rearrange("(p j) w -> p j w", j=PACK)
         new_k_hbm = new_kT.rearrange("(p j) w -> p j w", j=PACK)
@@ -50,14 +49,12 @@ def tile_attend_x_append256_cap_kernel(tc, qT, kT, vT, new_kT, new_vT, vs, offs,
         nc.scalar.dma_start(vs_win[VS_ROW:P, :], vs[0:1, :])
         nc.sync.dma_start(offs_t[:], offs)
         nc.sync.dma_start(slots_t[:], slots)
-        nc.sync.dma_start(new_k0[:], new_k_hbm[:, 0, :])
-        nc.sync.dma_start(k_win[0][:], k_hbm[:, 0, :])
-        nc.sync.dma_start(new_k123[:], new_k_hbm[:, 1:PACK, :])
-        for t in range(1, PACK):
+        for t in range(PACK):
+            nc.sync.dma_start(new_k[t][:], new_k_hbm[:, t, :])
             nc.sync.dma_start(k_win[t][:], k_hbm[:, t, :])
         nc.sync.dma_start(q_raw[:], qT.rearrange("b (p j) w -> p b j w", j=PACK))
-        nc.sync.dma_start(new_v[:], new_vT.rearrange("(h p) w -> p h w", p=P))
         for h in range(2):
+            nc.sync.dma_start(new_v[h][:], new_vT[h * P : (h + 1) * P, :])
             nc.sync.dma_start(v_win[h][:], vT[h * P : (h + 1) * P, :])
 
         ident = keep.tile([P, P], F32, name="ident")
@@ -71,116 +68,133 @@ def tile_attend_x_append256_cap_kernel(tc, qT, kT, vT, new_kT, new_vT, vs, offs,
 
         gathered_vs = keep.tile([P, B * N], F32, name="gathered_vs")
         nc.vector.tensor_copy(gathered_vs[:], vs_win[:].indirect(offs_t[:]))
-        scales = []
+        vs_ps = []
         for b in range(B):
-            turned = psum.tile([P, PACK, P], F32, name=f"vs_ps{b}", tag=f"scales{b}")
+            vs_ps.append(psum.tile([P, PACK, P], F32, name=f"vs_ps{b}", tag=f"scales{b}"))
             for t in range(PACK):
-                nc.tensor.transpose(turned[:, t, :], gathered_vs[:, b * N + t : (b + 1) * N : PACK], ident[:])
-            scales.append(keep.tile([P, PACK], F32, name=f"scales{b}"))
-            nc.scalar.copy(scales[b][:], turned[:, :, VS_ROW])
+                nc.tensor.transpose(vs_ps[b][:, t, :], gathered_vs[:, b * N + t : (b + 1) * N : PACK], ident[:])
 
-        for t in range(PACK):
-            append(k_win[t], new_k[t])
-            if t < PACK - 1:
-                nc.vector.tensor_copy(planes[:, :, t, 0:N], k_win[t][:].indirect(offs_t[:]))
+        scales = {}
+
+        def keep_scales(b, tag, align):
+            scales[b] = keep.tile([P, PACK], F32, name=f"scales{b}", tag=tag, align_bytes=align)
+            nc.scalar.copy(scales[b][:], vs_ps[b][:, :, VS_ROW])
+
+        for t in range(PACK - 1):
+            append(k_win[t], new_k[t][:])
+            k16 = keep.tile([P, T], BF16, name=f"k16_{t}")
+            cut = VECTOR_CAST[t]
+            nc.vector.tensor_copy(k16[:, 0:cut], k_win[t][:, 0:cut])
+            nc.scalar.copy(k16[:, cut:T], k_win[t][:, cut:T])
+            if t == 1:
+                keep_scales(0, "after_k1", 32)
+            if t < 2:
+                nc.scalar.activation(planes[:, :, t, 0:N], k16[:].indirect(offs_t[:]), ACT.Copy)
             else:
                 for b in range(B):
-                    nc.vector.tensor_copy(planes[:, b, t, 0:N], k_win[t][:].indirect(seq_offs(b)))
+                    nc.scalar.activation(planes[:, b, t, 0:N], k16[:].indirect(seq_offs(b)), ACT.Copy)
+        append(k_win[3], new_k[3][:])
+        for b in range(B):
+            nc.vector.tensor_copy(planes[:, b, 3, 0:N], k_win[3][:].indirect(seq_offs(b)))
 
         qx = keep.tile([P, B, NQ, PACK], BF16, name="qx", align_bytes=64)
-        nc.scalar.copy(
-            qx[:].rearrange("p b (c i) j -> p b c j i", i=RUN),
-            q_raw[:].rearrange("p b j (c i) -> p b c j i", i=RUN),
-        )
+        nc.gpsimd.tensor_scalar(qx[:], q_raw[:].rearrange("p b j w -> p b w j"), 1.0, 0.0, ALU.mult, ALU.add)
         kx_both = keep.tile([P, B * N * PACK], BF16, name="kx", tag="after_q", align_bytes=64)
         kx = [kx_both[:, b * N * PACK : (b + 1) * N * PACK] for b in range(B)]
         for b in range(B):
+            cut = SCALAR_SLOTS[b]
             nc.scalar.copy(
-                kx[b].rearrange("p (c i t) -> p c t i", i=RUN, t=PACK),
-                planes[:, b, :, 0:N].rearrange("p t (c i) -> p c t i", i=RUN),
+                kx[b][:, 0 : cut * PACK].rearrange("p (c i t) -> p c t i", i=RUN, t=PACK),
+                planes[:, b, :, 0:cut].rearrange("p t (c i) -> p c t i", i=RUN),
+            )
+            nc.gpsimd.tensor_scalar(
+                kx[b][:, cut * PACK :].rearrange("p (s t) -> p s t", t=PACK),
+                planes[:, b, :, cut:N].rearrange("p t s -> p s t"),
+                1.0,
+                0.0,
+                ALU.mult,
+                ALU.add,
             )
 
-        def quantise(name, src, width):
-            codes = keep.tile([P, width], U32, name=f"{name}_codes", align_bytes=64)
-            scale = keep.tile([P, width], U8, name=f"{name}_scale", align_bytes=64)
-            nc.vector.quantize_mx(out=codes[:].bitcast(FP8X4), scales=scale[:], in_=src)
+        def code_tile(name, width, tag):
+            return keep.tile([P, width], U32, name=name, tag=tag, align_bytes=64)[:]
+
+        def quantise(name, src, codes):
+            scale = keep.tile([P, codes.shape[1]], U8, name=f"{name}_scale", align_bytes=64)
+            nc.vector.quantize_mx(out=codes.bitcast(FP8X4), scales=scale[:], in_=src)
             return codes, scale
 
-        def product(acc, lhs, lhs_cols, rhs, rhs_cols):
+        def product(acc, lhs, cols, rhs):
             nc.tensor.matmul_mx(
                 out=acc,
-                lhsT=lhs[0][:, lhs_cols].bitcast(FP8X4),
-                lhsT_scale=lhs[1][:, lhs_cols],
-                rhs=rhs[0][:, rhs_cols].bitcast(FP8X4),
-                rhs_scale=rhs[1][:, rhs_cols],
+                lhsT=lhs[0][:, cols].bitcast(FP8X4),
+                lhsT_scale=lhs[1][:, cols],
+                rhs=rhs[0].bitcast(FP8X4),
+                rhs_scale=rhs[1][:],
                 start=True,
                 stop=True,
             )
 
-        def turn_values(turned, values):
-            words = values.bitcast(F32)
-            for u in range(2):
-                nc.tensor.transpose(turned[:, u, :], words[:, u : N // 2 : 2], ident[:])
-
-        q8 = quantise("q", qx[:].rearrange("p b w j -> p (b w j)"), B * NQ)
-        append(v_win[0], new_v[:, 0, :])
+        append(v_win[0], new_v[0][:])
+        v16 = keep.tile([P, T], BF16, name="v16")
+        nc.scalar.copy(v16[:], v_win[0][:])
+        qk_codes = code_tile("qk_codes", B * (NQ + N), "after_v0")
+        k_codes = qk_codes[:, B * NQ :]
+        q8 = quantise("q", qx[:].rearrange("p b w j -> p (b w j)"), qk_codes[:, 0 : B * NQ])
         scores = []
-
-        def score(b):
+        for b in range(B):
             acc = psum.tile([P, N], F32, name=f"score_ps{b}", tag=f"score{b}")
-            product(acc[:], q8, slice(b * NQ, (b + 1) * NQ), quantise(f"k{b}", kx[b], N), slice(0, N))
+            product(acc[:], q8, slice(b * NQ, (b + 1) * NQ), quantise(f"k{b}", kx[b], k_codes[:, b * N : (b + 1) * N]))
             scores.append(acc)
+        append(v_win[1], new_v[1][:])
 
-        score(0)
-        v0_both = gathered[:, 0 : B * N]
-        nc.vector.tensor_copy(v0_both, v_win[0][:].indirect(offs_t[:]))
-        append(v_win[1], new_v[:, 1, :])
-        score(1)
-
-        capped, minus_m, prob = [], [], []
-        total = keep.tile([P, B], F32, name="total")
-
-        def cap(b):
-            capped.append(keep.tile([P, PACK, P], F32, name=f"tanh{b}", tag=f"after_exp{b}", align_bytes=64))
+        capped = [keep.tile([P, PACK, P], F32, name=f"tanh{b}", tag=f"after_exp{b}", align_bytes=64) for b in range(B)]
+        for b in range(B):
             nc.scalar.activation(capped[b][:], scores[b][:].rearrange("q (s t) -> q t s", t=PACK), ACT.Tanh, scale=1.0 / CAP)
 
-        def row_max(b):
-            negated = keep.tile([P, N], F32, name=f"negated{b}")
+        gathered_v = {}
+
+        def gather_v(h, b, tile):
+            gathered_v[h, b] = tile
+            runs = tile.rearrange("p (u s e) -> p s u e", u=2, e=2)
+            if h == 0:
+                nc.scalar.activation(runs, v16[:].indirect(seq_offs(b)), ACT.Copy)
+            else:
+                nc.vector.tensor_copy(runs, v_win[1][:].indirect(seq_offs(b)))
+
+        minus_m = []
+        for b in range(B):
+            negated = keep.tile([P, N], F32, name=f"negated{b}", tag=f"after_max{b}", align_bytes=64)
             column = keep.tile([P, 1], F32, name=f"minus_m{b}")
             nc.vector.tensor_scalar(negated[:], capped[b][:].rearrange("q t s -> q (t s)"), -CAP, None, ALU.mult, ALU.min, accum_out=column[:])
             minus_m.append(column)
-
-        def exp(b):
-            prob.append(keep.tile([P, PACK, P], F32, name=f"p{b}"))
-            nc.scalar.activation(prob[b][:], capped[b][:], ACT.Exp, bias=minus_m[b][:], scale=CAP, accum_out=total[:, b : b + 1])
-
-        cap(0)
-        v0_ps = psum.tile([P, B, 2, P], F32, name="v0_ps", tag="values0")
+        v1_both = keep.tile([P, B * N], BF16, name="gathered_v1", tag="after_max0", align_bytes=64)
         for b in range(B):
-            turn_values(v0_ps[:, b], v0_both[:, b * N : (b + 1) * N])
-        vx0 = keep.tile([P, B * P * PACK], BF16, name="vx0", align_bytes=64)
-        nc.scalar.copy(vx0[:].bitcast(F32).rearrange("p (b e u) -> p b e u", b=B, u=2), v0_ps[:].rearrange("p b u e -> p b e u"))
-        cap(1)
-        row_max(0)
-        v1_seq0 = gathered[:, seq_width : seq_width + N]
-        nc.vector.tensor_copy(v1_seq0, v_win[1][:].indirect(seq_offs(0)))
-        row_max(1)
-        exp(0)
-        v1_seq1 = keep.tile([P, N], BF16, name="v1_seq1", tag="after_exp0", align_bytes=64)
-        nc.vector.tensor_copy(v1_seq1[:], v_win[1][:].indirect(seq_offs(1)))
-        v0_8 = quantise("v0", vx0[:], B * P)
+            gather_v(1, b, v1_both[:, b * N : (b + 1) * N])
 
-        vx1 = []
+        total = keep.tile([P, B], F32, name="total")
+        gather_v(0, 0, keep.tile([P, N], BF16, name="gathered_v0_0", align_bytes=64)[:])
+        prob = []
+        for b in range(B):
+            p = keep.tile([P, PACK, P], F32, name=f"p{b}", tag=f"after_turn{b}", align_bytes=64)
+            nc.scalar.activation(p[:], capped[b][:], ACT.Exp, bias=minus_m[b][:], scale=CAP, accum_out=total[:, b : b + 1])
+            prob.append(p)
+        keep_scales(1, "after_exp1", 64)
+        gather_v(0, 1, keep.tile([P, N], BF16, name="gathered_v0_1", tag="after_exp0", align_bytes=64)[:])
 
-        def lay_v1(b, values, bank):
-            turned = psum.tile([P, 2, P], F32, name=f"v1_ps{b}", tag=bank)
-            turn_values(turned, values)
-            vx1.append(keep.tile([P, P * PACK], BF16, name=f"vx1_{b}", align_bytes=64))
-            nc.scalar.copy(vx1[b][:].bitcast(F32).rearrange("p (e u) -> p e u", u=2), turned[:].rearrange("p u e -> p e u"))
+        def turn_values(turned, h, b):
+            for u in range(2):
+                run = gathered_v[h, b][:, u * N // 2 : (u + 1) * N // 2]
+                nc.tensor.transpose(turned[:, u, :], run.bitcast(F32), ident[:])
 
-        lay_v1(0, v1_seq0, "values1")
-        exp(1)
+        def lay_values(h, b, bank):
+            turned = psum.tile([P, 2, P], F32, name=f"v_ps{h}_{b}", tag=bank)
+            turn_values(turned, h, b)
+            vx = keep.tile([P, P * PACK], BF16, name=f"vx{h}_{b}", align_bytes=64)
+            nc.scalar.copy(vx[:].bitcast(F32).rearrange("p (e u) -> p e u", u=2), turned[:].rearrange("p u e -> p e u"))
+            return vx
 
+        vx = {(0, 0): lay_values(0, 0, "values0")}
         wx = []
         for b in range(B):
             turned = psum.tile([P, PACK, P], F32, name=f"w_ps{b}", tag=f"weights{b}")
@@ -193,25 +207,29 @@ def tile_attend_x_append256_cap_kernel(tc, qT, kT, vT, new_kT, new_vT, vs, offs,
                 scales[b][:].unsqueeze(1).to_broadcast([P, NQ, PACK]),
                 ALU.mult,
             )
-        lay_v1(1, v1_seq1[:], "weights0")
+        for h, b, bank in ((1, 0, "scales1"), (1, 1, "weights0"), (0, 1, "values1")):
+            vx[h, b] = lay_values(h, b, bank)
         inv = keep.tile([P, B], F32, name="inv")
         nc.vector.reciprocal(inv[:], total[:])
 
         queries = slice(0, NQ)
-        w8 = quantise("w0", wx[0][:].rearrange("p q t -> p (q t)"), NQ)
+        w8 = [quantise(f"w{b}", wx[b][:].rearrange("p q t -> p (q t)"), code_tile(f"w{b}_codes", NQ, ("after_turn1", "w1_codes")[b])) for b in range(B)]
+
+        def weigh(acc, h, b):
+            product(acc, w8[b], queries, quantise(f"v{h}_{b}", vx[h, b][:], code_tile(f"v{h}_{b}_codes", P, f"v{h}_{b}_codes")))
+
         y0 = psum.tile([P, DV], F32, name="y_ps0", tag="score0")
-        product(y0[:, 0:P], w8, queries, v0_8, slice(0, P))
-        product(y0[:, P:DV], w8, queries, quantise("v1_0", vx1[0][:], P), slice(0, P))
+        for h in range(2):
+            weigh(y0[:, h * P : (h + 1) * P], h, 0)
         y0_sb = keep.tile([P, DV], F32, name="y0_sb")
         nc.scalar.activation(y0_sb[:], y0[:], ACT.Copy, scale=inv[:, 0:1])
         nc.sync.dma_start(out[0], y0_sb[:])
 
-        w8 = quantise("w1", wx[1][:].rearrange("p q t -> p (q t)"), NQ)
-        y1_lo = psum.tile([P, P], F32, name="y1_lo", tag="score1")
-        product(y1_lo[:], w8, queries, v0_8, slice(P, 2 * P))
-        y1_hi = psum.tile([P, P], F32, name="y1_hi", tag="scales0")
-        product(y1_hi[:], w8, queries, quantise("v1_1", vx1[1][:], P), slice(0, P))
+        y1 = {}
+        for h, bank in ((1, "score1"), (0, "scales0")):
+            y1[h] = psum.tile([P, P], F32, name=f"y_ps1_{h}", tag=bank)
+            weigh(y1[h][:], h, 1)
         y1_sb = keep.tile([P, DV], F32, name="y1_sb")
-        nc.scalar.activation(y1_sb[:, 0:P], y1_lo[:], ACT.Copy, scale=inv[:, 1:2])
-        nc.vector.tensor_scalar(y1_sb[:, P:DV], y1_hi[:], inv[:, 1:2], None, ALU.mult)
+        nc.scalar.activation(y1_sb[:, P:DV], y1[1][:], ACT.Copy, scale=inv[:, 1:2])
+        nc.vector.tensor_scalar(y1_sb[:, 0:P], y1[0][:], inv[:, 1:2], None, ALU.mult)
         nc.sync.dma_start(out[1], y1_sb[:])

@@ -22,8 +22,8 @@ ALU = mybir.AluOpType
 PAD = 16
 RUN = 4
 VS_ROW = P - 1
-VECTOR_CAST = (1216, 1216, 1216)
-SCALAR_SLOTS = (256, 320)
+VECTOR_CAST = 1216
+SCALAR_SLOTS = (256, 288)
 
 
 def tile_attend_x_append256_cap_kernel(tc, qT, kT, vT, new_kT, new_vT, vs, offs, slots, out):
@@ -34,9 +34,11 @@ def tile_attend_x_append256_cap_kernel(tc, qT, kT, vT, new_kT, new_vT, vs, offs,
 
         offs_t = keep.tile([P, B * N // 16], U16, name="offs_t")
         slots_t = keep.tile([P, NEW // 16], U16, name="slots_t")
-        gathered_k = keep.tile([P, B * PACK * (N + PAD)], BF16, name="gathered_k", align_bytes=64)
+        gathered_k = keep.tile([P, B * PACK * (N + PAD)], BF16, name="gathered_k", tag="after_interleave", align_bytes=64)
         planes = gathered_k[:].rearrange("p (b t s) -> p b t s", b=B, t=PACK)
-        new_k = [keep.tile([P, NEW], F32, name=f"new_k{t}", tag=f"after_k{t}", align_bytes=32) for t in range(PACK)]
+        new_k = [keep.tile([P, NEW], F32, name=f"new_k{t}", tag=f"after_k{t}", align_bytes=32)[:] for t in range(PACK - 1)]
+        held_run = (PACK + 2) * (N + PAD)
+        new_k.append(gathered_k[:, held_run : held_run + N].bitcast(F32))
         new_v = [keep.tile([P, NEW], F32, name=f"new_v{h}", tag=f"after_v{h}", align_bytes=64) for h in range(2)]
         q_raw = keep.tile([P, B, PACK, NQ], F32, name="q_raw", tag="after_q", align_bytes=64)
         vs_win = keep.tile([P, T], F32, name="vs_win")
@@ -50,7 +52,7 @@ def tile_attend_x_append256_cap_kernel(tc, qT, kT, vT, new_kT, new_vT, vs, offs,
         nc.sync.dma_start(offs_t[:], offs)
         nc.sync.dma_start(slots_t[:], slots)
         for t in range(PACK):
-            nc.sync.dma_start(new_k[t][:], new_k_hbm[:, t, :])
+            nc.sync.dma_start(new_k[t], new_k_hbm[:, t, :])
             nc.sync.dma_start(k_win[t][:], k_hbm[:, t, :])
         nc.sync.dma_start(q_raw[:], qT.rearrange("b (p j) w -> p b j w", j=PACK))
         for h in range(2):
@@ -80,25 +82,25 @@ def tile_attend_x_append256_cap_kernel(tc, qT, kT, vT, new_kT, new_vT, vs, offs,
             scales[b] = keep.tile([P, PACK], F32, name=f"scales{b}", tag=tag, align_bytes=align)
             nc.scalar.copy(scales[b][:], vs_ps[b][:, :, VS_ROW])
 
-        for t in range(PACK - 1):
-            append(k_win[t], new_k[t][:])
+        for t in range(2):
+            append(k_win[t], new_k[t])
             k16 = keep.tile([P, T], BF16, name=f"k16_{t}")
-            cut = VECTOR_CAST[t]
-            nc.vector.tensor_copy(k16[:, 0:cut], k_win[t][:, 0:cut])
-            nc.scalar.copy(k16[:, cut:T], k_win[t][:, cut:T])
+            nc.vector.tensor_copy(k16[:, 0:VECTOR_CAST], k_win[t][:, 0:VECTOR_CAST])
+            nc.scalar.copy(k16[:, VECTOR_CAST:T], k_win[t][:, VECTOR_CAST:T])
             if t == 1:
                 keep_scales(0, "after_k1", 32)
-            if t < 2:
-                nc.scalar.activation(planes[:, :, t, 0:N], k16[:].indirect(offs_t[:]), ACT.Copy)
-            else:
-                for b in range(B):
-                    nc.scalar.activation(planes[:, b, t, 0:N], k16[:].indirect(seq_offs(b)), ACT.Copy)
-        append(k_win[3], new_k[3][:])
-        for b in range(B):
-            nc.vector.tensor_copy(planes[:, b, 3, 0:N], k_win[3][:].indirect(seq_offs(b)))
+            nc.scalar.activation(planes[:, :, t, 0:N], k16[:].indirect(offs_t[:]), ACT.Copy)
+        append(k_win[2], new_k[2])
+        nc.vector.tensor_copy(planes[:, 0, 2, 0:N], k_win[2][:].indirect(seq_offs(0)))
+        append(k_win[3], new_k[3])
+        for t, b in ((3, 0), (2, 1), (3, 1)):
+            nc.vector.tensor_copy(planes[:, b, t, 0:N], k_win[t][:].indirect(seq_offs(b)))
 
         qx = keep.tile([P, B, NQ, PACK], BF16, name="qx", align_bytes=64)
-        nc.gpsimd.tensor_scalar(qx[:], q_raw[:].rearrange("p b j w -> p b w j"), 1.0, 0.0, ALU.mult, ALU.add)
+        nc.scalar.copy(
+            qx[:].rearrange("p b (c i) j -> p b c j i", i=RUN),
+            q_raw[:].rearrange("p b j (c i) -> p b c j i", i=RUN),
+        )
         kx_both = keep.tile([P, B * N * PACK], BF16, name="kx", tag="after_q", align_bytes=64)
         kx = [kx_both[:, b * N * PACK : (b + 1) * N * PACK] for b in range(B)]
         for b in range(B):
@@ -138,7 +140,7 @@ def tile_attend_x_append256_cap_kernel(tc, qT, kT, vT, new_kT, new_vT, vs, offs,
         append(v_win[0], new_v[0][:])
         v16 = keep.tile([P, T], BF16, name="v16")
         nc.scalar.copy(v16[:], v_win[0][:])
-        qk_codes = code_tile("qk_codes", B * (NQ + N), "after_v0")
+        qk_codes = code_tile("qk_codes", B * (NQ + N), "after_interleave")
         k_codes = qk_codes[:, B * NQ :]
         q8 = quantise("q", qx[:].rearrange("p b w j -> p (b w j)"), qk_codes[:, 0 : B * NQ])
         scores = []
@@ -213,10 +215,18 @@ def tile_attend_x_append256_cap_kernel(tc, qT, kT, vT, new_kT, new_vT, vs, offs,
         nc.vector.reciprocal(inv[:], total[:])
 
         queries = slice(0, NQ)
-        w8 = [quantise(f"w{b}", wx[b][:].rearrange("p q t -> p (q t)"), code_tile(f"w{b}_codes", NQ, ("after_turn1", "w1_codes")[b])) for b in range(B)]
+        held_codes = code_tile("held_codes", NQ + P, "after_turn1")
+        w_codes = (held_codes[:, 0:NQ], code_tile("w1_codes", NQ, "w1_codes"))
+        v_codes = {key: code_tile(f"v{key[0]}_{key[1]}_codes", P, f"v{key[0]}_{key[1]}_codes") for key in ((1, 0), (1, 1), (0, 1))}
+        v_codes[0, 0] = held_codes[:, NQ:]
+        w8 = [quantise("w0", wx[0][:].rearrange("p q t -> p (q t)"), w_codes[0])]
+        v8 = {(0, 0): quantise("v0_0", vx[0, 0][:], v_codes[0, 0])}
+        w8.append(quantise("w1", wx[1][:].rearrange("p q t -> p (q t)"), w_codes[1]))
+        for h, b in ((1, 0), (1, 1), (0, 1)):
+            v8[h, b] = quantise(f"v{h}_{b}", vx[h, b][:], v_codes[h, b])
 
         def weigh(acc, h, b):
-            product(acc, w8[b], queries, quantise(f"v{h}_{b}", vx[h, b][:], code_tile(f"v{h}_{b}_codes", P, f"v{h}_{b}_codes")))
+            product(acc, w8[b], queries, v8[h, b])
 
         y0 = psum.tile([P, DV], F32, name="y_ps0", tag="score0")
         for h in range(2):

@@ -22,8 +22,7 @@ ALU = mybir.AluOpType
 PAD = 16
 RUN = 4
 VS_ROW = P - 1
-VECTOR_CAST = 1216
-SCALAR_SLOTS = (256, 288)
+SCALAR_SLOTS = (256, 320)
 
 
 def tile_attend_x_append256_cap_kernel(tc, qT, kT, vT, new_kT, new_vT, vs, offs, slots, out):
@@ -85,8 +84,7 @@ def tile_attend_x_append256_cap_kernel(tc, qT, kT, vT, new_kT, new_vT, vs, offs,
         for t in range(2):
             append(k_win[t], new_k[t])
             k16 = keep.tile([P, T], BF16, name=f"k16_{t}")
-            nc.vector.tensor_copy(k16[:, 0:VECTOR_CAST], k_win[t][:, 0:VECTOR_CAST])
-            nc.scalar.copy(k16[:, VECTOR_CAST:T], k_win[t][:, VECTOR_CAST:T])
+            nc.scalar.copy(k16[:], k_win[t][:])
             if t == 1:
                 keep_scales(0, "after_k1", 32)
             nc.scalar.activation(planes[:, :, t, 0:N], k16[:].indirect(offs_t[:]), ACT.Copy)
@@ -97,10 +95,7 @@ def tile_attend_x_append256_cap_kernel(tc, qT, kT, vT, new_kT, new_vT, vs, offs,
             nc.vector.tensor_copy(planes[:, b, t, 0:N], k_win[t][:].indirect(seq_offs(b)))
 
         qx = keep.tile([P, B, NQ, PACK], BF16, name="qx", align_bytes=64)
-        nc.scalar.copy(
-            qx[:].rearrange("p b (c i) j -> p b c j i", i=RUN),
-            q_raw[:].rearrange("p b j (c i) -> p b c j i", i=RUN),
-        )
+        nc.gpsimd.tensor_scalar(qx[:], q_raw[:].rearrange("p b j w -> p b w j"), 1.0, 0.0, ALU.mult, ALU.add)
         kx_both = keep.tile([P, B * N * PACK], BF16, name="kx", tag="after_q", align_bytes=64)
         kx = [kx_both[:, b * N * PACK : (b + 1) * N * PACK] for b in range(B)]
         for b in range(B):

@@ -35,7 +35,9 @@ def tile_attend_x_append256_cap_kernel(tc, qT, kT, vT, new_kT, new_vT, vs, offs,
         slots_t = keep.tile([P, NEW // 16], U16, name="slots_t")
         gathered_k = keep.tile([P, B * PACK * (N + PAD)], BF16, name="gathered_k", tag="after_interleave", align_bytes=64)
         planes = gathered_k[:].rearrange("p (b t s) -> p b t s", b=B, t=PACK)
-        new_k = [keep.tile([P, NEW], F32, name=f"new_k{t}", tag=f"after_k{t}", align_bytes=32)[:] for t in range(PACK - 1)]
+        new_k0 = keep.tile([P, NEW], F32, name="new_k0")
+        new_k12 = keep.tile([P, 2, NEW], F32, name="new_k12", tag="after_k2", align_bytes=32)
+        new_k = [new_k0[:], new_k12[:, 0, :], new_k12[:, 1, :]]
         held_run = (PACK + 2) * (N + PAD)
         new_k.append(gathered_k[:, held_run : held_run + N].bitcast(F32))
         new_v = [keep.tile([P, NEW], F32, name=f"new_v{h}", tag=f"after_v{h}", align_bytes=64) for h in range(2)]
@@ -51,7 +53,10 @@ def tile_attend_x_append256_cap_kernel(tc, qT, kT, vT, new_kT, new_vT, vs, offs,
         nc.sync.dma_start(offs_t[:], offs)
         nc.sync.dma_start(slots_t[:], slots)
         for t in range(PACK):
-            nc.sync.dma_start(new_k[t], new_k_hbm[:, t, :])
+            if t == 1:
+                nc.sync.dma_start(new_k12[:], new_k_hbm[:, 1:3, :])
+            elif t != 2:
+                nc.sync.dma_start(new_k[t], new_k_hbm[:, t, :])
             nc.sync.dma_start(k_win[t][:], k_hbm[:, t, :])
         nc.sync.dma_start(q_raw[:], qT.rearrange("b (p j) w -> p b j w", j=PACK))
         for h in range(2):
@@ -86,9 +91,9 @@ def tile_attend_x_append256_cap_kernel(tc, qT, kT, vT, new_kT, new_vT, vs, offs,
             k16 = keep.tile([P, T], BF16, name=f"k16_{t}")
             nc.scalar.copy(k16[:], k_win[t][:])
             if t == 1:
-                keep_scales(0, "after_k1", 32)
+                append(k_win[2], new_k[2])
+                keep_scales(0, "after_k2", 32)
             nc.scalar.activation(planes[:, :, t, 0:N], k16[:].indirect(offs_t[:]), ACT.Copy)
-        append(k_win[2], new_k[2])
         nc.vector.tensor_copy(planes[:, 0, 2, 0:N], k_win[2][:].indirect(seq_offs(0)))
         append(k_win[3], new_k[3])
         for t, b in ((3, 0), (2, 1), (3, 1)):
@@ -234,7 +239,8 @@ def tile_attend_x_append256_cap_kernel(tc, qT, kT, vT, new_kT, new_vT, vs, offs,
         for h, bank in ((1, "score1"), (0, "scales0")):
             y1[h] = psum.tile([P, P], F32, name=f"y_ps1_{h}", tag=bank)
             weigh(y1[h][:], h, 1)
-        y1_sb = keep.tile([P, DV], F32, name="y1_sb")
-        nc.scalar.activation(y1_sb[:, P:DV], y1[1][:], ACT.Copy, scale=inv[:, 1:2])
-        nc.vector.tensor_scalar(y1_sb[:, 0:P], y1[0][:], inv[:, 1:2], None, ALU.mult)
-        nc.sync.dma_start(out[1], y1_sb[:])
+        y1_sb = [keep.tile([P, P], F32, name=f"y1_sb{h}") for h in range(2)]
+        nc.scalar.activation(y1_sb[1][:], y1[1][:], ACT.Copy, scale=inv[:, 1:2])
+        nc.sync.dma_start(out[1, :, P:DV], y1_sb[1][:])
+        nc.vector.tensor_scalar(y1_sb[0][:], y1[0][:], inv[:, 1:2], None, ALU.mult)
+        nc.sync.dma_start(out[1, :, 0:P], y1_sb[0][:])

@@ -50,12 +50,13 @@ def tile_attend_x_append256_cap_kernel(tc, qT, kT, vT, new_kT, new_vT, vs, offs,
         new_k_hbm = new_kT.rearrange("(p j) w -> p j w", j=PACK)
         nc.vector.memset(vs_win[0:VS_ROW, :], 0.0)
         nc.scalar.dma_start(vs_win[VS_ROW:P, :], vs[0:1, :])
-        nc.sync.dma_start(offs_t[:], offs)
+        nc.sync.dma_start(k_win[0][:], k_hbm[:, 0, :])
+        nc.sync.dma_start(new_k[0], new_k_hbm[:, 0, :])
         nc.sync.dma_start(slots_t[:], slots)
-        for t in range(PACK):
-            if t == 1:
-                nc.sync.dma_start(new_k12[:], new_k_hbm[:, 1:3, :])
-            elif t != 2:
+        nc.sync.dma_start(offs_t[:], offs)
+        nc.sync.dma_start(new_k12[:], new_k_hbm[:, 1:3, :])
+        for t in range(1, PACK):
+            if t == PACK - 1:
                 nc.sync.dma_start(new_k[t], new_k_hbm[:, t, :])
             nc.sync.dma_start(k_win[t][:], k_hbm[:, t, :])
         nc.sync.dma_start(q_raw[:], qT.rearrange("b (p j) w -> p b j w", j=PACK))

@@ -20,7 +20,7 @@ ACT = mybir.ActivationFunctionType
 ALU = mybir.AluOpType
 
 PAD = 16
-RUN = 4
+RUN = 8
 VS_ROW = P - 1
 SCALAR_SLOTS = (256, 320)
 

@@ -22,7 +22,7 @@ ALU = mybir.AluOpType
 PAD = 16
 RUN = 8
 VS_ROW = P - 1
-SCALAR_SLOTS = (256, 320)
+SCALAR_SLOTS = (288, 288)
 
 
 def tile_attend_x_append256_cap_kernel(tc, qT, kT, vT, new_kT, new_vT, vs, offs, slots, out):

from contextlib import ExitStack

import concourse.mybir as mybir
from concourse.masks import make_identity

B, N, T, D, DV, NQ, NEW = 2, 512, 2048, 512, 256, 128, 256
P = 128
PACK = 4
CAP = 2.0
FLOPS = 2 * B * NQ * N * (D + DV)
BYTES = 4 * (B * D * NQ + D * T + DV * T + D * NEW + DV * NEW + T + B * NQ * DV) + 2 * P * (B * N + NEW) // 16

F32 = mybir.dt.float32
BF16 = mybir.dt.bfloat16
U32 = mybir.dt.uint32
U16 = mybir.dt.uint16
U8 = mybir.dt.uint8
FP8X4 = mybir.dt.float8_e4m3fn_x4
ACT = mybir.ActivationFunctionType
ALU = mybir.AluOpType

PAD = 16
RUN = 8
VS_ROW = P - 1
SCALAR_SLOTS = (288, 288)


def tile_attend_x_append256_cap_kernel(tc, qT, kT, vT, new_kT, new_vT, vs, offs, slots, out):
    nc = tc.nc
    with ExitStack() as ctx:
        keep = ctx.enter_context(tc.tile_pool(name="keep", bufs=1))
        psum = ctx.enter_context(tc.psum_pool(name="psum", bufs=1))

        offs_t = keep.tile([P, B * N // 16], U16, name="offs_t")
        slots_t = keep.tile([P, NEW // 16], U16, name="slots_t")
        gathered_k = keep.tile([P, B * PACK * (N + PAD)], BF16, name="gathered_k", tag="after_interleave", align_bytes=64)
        planes = gathered_k[:].rearrange("p (b t s) -> p b t s", b=B, t=PACK)
        new_k0 = keep.tile([P, NEW], F32, name="new_k0")
        new_k12 = keep.tile([P, 2, NEW], F32, name="new_k12", tag="after_k2", align_bytes=32)
        new_k = [new_k0[:], new_k12[:, 0, :], new_k12[:, 1, :]]
        held_run = (PACK + 2) * (N + PAD)
        new_k.append(gathered_k[:, held_run : held_run + N].bitcast(F32))
        new_v = [keep.tile([P, NEW], F32, name=f"new_v{h}", tag=f"after_v{h}", align_bytes=64) for h in range(2)]
        q_raw = keep.tile([P, B, PACK, NQ], F32, name="q_raw", tag="after_q", align_bytes=64)
        vs_win = keep.tile([P, T], F32, name="vs_win")
        k_win = [keep.tile([P, T], F32, name=f"k{t}") for t in range(PACK)]
        v_win = [keep.tile([P, T], F32, name=f"v{h}", tag=f"v_win{h}", align_bytes=32) for h in range(2)]

        k_hbm = kT.rearrange("(p j) w -> p j w", j=PACK)
        new_k_hbm = new_kT.rearrange("(p j) w -> p j w", j=PACK)
        nc.vector.memset(vs_win[0:VS_ROW, :], 0.0)
        nc.scalar.dma_start(vs_win[VS_ROW:P, :], vs[0:1, :])
        nc.sync.dma_start(k_win[0][:], k_hbm[:, 0, :])
        nc.sync.dma_start(new_k[0], new_k_hbm[:, 0, :])
        nc.sync.dma_start(slots_t[:], slots)
        nc.sync.dma_start(offs_t[:], offs)
        nc.sync.dma_start(new_k12[:], new_k_hbm[:, 1:3, :])
        for t in range(1, PACK):
            if t == PACK - 1:
                nc.sync.dma_start(new_k[t], new_k_hbm[:, t, :])
            nc.sync.dma_start(k_win[t][:], k_hbm[:, t, :])
        nc.sync.dma_start(q_raw[:], qT.rearrange("b (p j) w -> p b j w", j=PACK))
        for h in range(2):
            nc.sync.dma_start(new_v[h][:], new_vT[h * P : (h + 1) * P, :])
            nc.sync.dma_start(v_win[h][:], vT[h * P : (h + 1) * P, :])

        ident = keep.tile([P, P], F32, name="ident")
        make_identity(nc, ident[:])

        def seq_offs(b):
            return offs_t[:, b * N // 16 : (b + 1) * N // 16]

        def append(window, new):
            nc.vector.tensor_copy(window[:].indirect(slots_t[:]), new)

        gathered_vs = keep.tile([P, B * N], F32, name="gathered_vs")
        nc.vector.tensor_copy(gathered_vs[:], vs_win[:].indirect(offs_t[:]))
        vs_ps = []
        for b in range(B):
            vs_ps.append(psum.tile([P, PACK, P], F32, name=f"vs_ps{b}", tag=f"scales{b}"))
            for t in range(PACK):
                nc.tensor.transpose(vs_ps[b][:, t, :], gathered_vs[:, b * N + t : (b + 1) * N : PACK], ident[:])

        scales = {}

        def keep_scales(b, tag, align):
            scales[b] = keep.tile([P, PACK], F32, name=f"scales{b}", tag=tag, align_bytes=align)
            nc.scalar.copy(scales[b][:], vs_ps[b][:, :, VS_ROW])

        for t in range(2):
            append(k_win[t], new_k[t])
            k16 = keep.tile([P, T], BF16, name=f"k16_{t}")
            nc.scalar.copy(k16[:], k_win[t][:])
            if t == 1:
                append(k_win[2], new_k[2])
                keep_scales(0, "after_k2", 32)
            nc.scalar.activation(planes[:, :, t, 0:N], k16[:].indirect(offs_t[:]), ACT.Copy)
        nc.vector.tensor_copy(planes[:, 0, 2, 0:N], k_win[2][:].indirect(seq_offs(0)))
        append(k_win[3], new_k[3])
        for t, b in ((3, 0), (2, 1), (3, 1)):
            nc.vector.tensor_copy(planes[:, b, t, 0:N], k_win[t][:].indirect(seq_offs(b)))

        qx = keep.tile([P, B, NQ, PACK], BF16, name="qx", align_bytes=64)
        nc.gpsimd.tensor_scalar(qx[:], q_raw[:].rearrange("p b j w -> p b w j"), 1.0, 0.0, ALU.mult, ALU.add)
        kx_both = keep.tile([P, B * N * PACK], BF16, name="kx", tag="after_q", align_bytes=64)
        kx = [kx_both[:, b * N * PACK : (b + 1) * N * PACK] for b in range(B)]
        for b in range(B):
            cut = SCALAR_SLOTS[b]
            nc.scalar.copy(
                kx[b][:, 0 : cut * PACK].rearrange("p (c i t) -> p c t i", i=RUN, t=PACK),
                planes[:, b, :, 0:cut].rearrange("p t (c i) -> p c t i", i=RUN),
            )
            nc.gpsimd.tensor_scalar(
                kx[b][:, cut * PACK :].rearrange("p (s t) -> p s t", t=PACK),
                planes[:, b, :, cut:N].rearrange("p t s -> p s t"),
                1.0,
                0.0,
                ALU.mult,
                ALU.add,
            )

        def code_tile(name, width, tag):
            return keep.tile([P, width], U32, name=name, tag=tag, align_bytes=64)[:]

        def quantise(name, src, codes):
            scale = keep.tile([P, codes.shape[1]], U8, name=f"{name}_scale", align_bytes=64)
            nc.vector.quantize_mx(out=codes.bitcast(FP8X4), scales=scale[:], in_=src)
            return codes, scale

        def product(acc, lhs, cols, rhs):
            nc.tensor.matmul_mx(
                out=acc,
                lhsT=lhs[0][:, cols].bitcast(FP8X4),
                lhsT_scale=lhs[1][:, cols],
                rhs=rhs[0].bitcast(FP8X4),
                rhs_scale=rhs[1][:],
                start=True,
                stop=True,
            )

        append(v_win[0], new_v[0][:])
        v16 = keep.tile([P, T], BF16, name="v16")
        nc.scalar.copy(v16[:], v_win[0][:])
        qk_codes = code_tile("qk_codes", B * (NQ + N), "after_interleave")
        k_codes = qk_codes[:, B * NQ :]
        q8 = quantise("q", qx[:].rearrange("p b w j -> p (b w j)"), qk_codes[:, 0 : B * NQ])
        scores = []
        for b in range(B):
            acc = psum.tile([P, N], F32, name=f"score_ps{b}", tag=f"score{b}")
            product(acc[:], q8, slice(b * NQ, (b + 1) * NQ), quantise(f"k{b}", kx[b], k_codes[:, b * N : (b + 1) * N]))
            scores.append(acc)
        append(v_win[1], new_v[1][:])

        capped = [keep.tile([P, PACK, P], F32, name=f"tanh{b}", tag=f"after_exp{b}", align_bytes=64) for b in range(B)]
        for b in range(B):
            nc.scalar.activation(capped[b][:], scores[b][:].rearrange("q (s t) -> q t s", t=PACK), ACT.Tanh, scale=1.0 / CAP)

        gathered_v = {}

        def gather_v(h, b, tile):
            gathered_v[h, b] = tile
            runs = tile.rearrange("p (u s e) -> p s u e", u=2, e=2)
            if h == 0:
                nc.scalar.activation(runs, v16[:].indirect(seq_offs(b)), ACT.Copy)
            else:
                nc.vector.tensor_copy(runs, v_win[1][:].indirect(seq_offs(b)))

        minus_m = []
        for b in range(B):
            negated = keep.tile([P, N], F32, name=f"negated{b}", tag=f"after_max{b}", align_bytes=64)
            column = keep.tile([P, 1], F32, name=f"minus_m{b}")
            nc.vector.tensor_scalar(negated[:], capped[b][:].rearrange("q t s -> q (t s)"), -CAP, None, ALU.mult, ALU.min, accum_out=column[:])
            minus_m.append(column)
        v1_both = keep.tile([P, B * N], BF16, name="gathered_v1", tag="after_max0", align_bytes=64)
        for b in range(B):
            gather_v(1, b, v1_both[:, b * N : (b + 1) * N])

        total = keep.tile([P, B], F32, name="total")
        gather_v(0, 0, keep.tile([P, N], BF16, name="gathered_v0_0", align_bytes=64)[:])
        prob = []
        for b in range(B):
            p = keep.tile([P, PACK, P], F32, name=f"p{b}", tag=f"after_turn{b}", align_bytes=64)
            nc.scalar.activation(p[:], capped[b][:], ACT.Exp, bias=minus_m[b][:], scale=CAP, accum_out=total[:, b : b + 1])
            prob.append(p)
        keep_scales(1, "after_exp1", 64)
        gather_v(0, 1, keep.tile([P, N], BF16, name="gathered_v0_1", tag="after_exp0", align_bytes=64)[:])

        def turn_values(turned, h, b):
            for u in range(2):
                run = gathered_v[h, b][:, u * N // 2 : (u + 1) * N // 2]
                nc.tensor.transpose(turned[:, u, :], run.bitcast(F32), ident[:])

        def lay_values(h, b, bank):
            turned = psum.tile([P, 2, P], F32, name=f"v_ps{h}_{b}", tag=bank)
            turn_values(turned, h, b)
            vx = keep.tile([P, P * PACK], BF16, name=f"vx{h}_{b}", align_bytes=64)
            nc.scalar.copy(vx[:].bitcast(F32).rearrange("p (e u) -> p e u", u=2), turned[:].rearrange("p u e -> p e u"))
            return vx

        vx = {(0, 0): lay_values(0, 0, "values0")}
        wx = []
        for b in range(B):
            turned = psum.tile([P, PACK, P], F32, name=f"w_ps{b}", tag=f"weights{b}")
            for t in range(PACK):
                nc.tensor.transpose(turned[:, t, :], prob[b][:, t, :], ident[:])
            wx.append(keep.tile([P, NQ, PACK], BF16, name=f"wx{b}", align_bytes=64))
            nc.vector.tensor_tensor(
                wx[b][:],
                turned[:].rearrange("p t q -> p q t"),
                scales[b][:].unsqueeze(1).to_broadcast([P, NQ, PACK]),
                ALU.mult,
            )
        for h, b, bank in ((1, 0, "scales1"), (1, 1, "weights0"), (0, 1, "values1")):
            vx[h, b] = lay_values(h, b, bank)
        inv = keep.tile([P, B], F32, name="inv")
        nc.vector.reciprocal(inv[:], total[:])

        queries = slice(0, NQ)
        held_codes = code_tile("held_codes", NQ + P, "after_turn1")
        w_codes = (held_codes[:, 0:NQ], code_tile("w1_codes", NQ, "w1_codes"))
        v_codes = {key: code_tile(f"v{key[0]}_{key[1]}_codes", P, f"v{key[0]}_{key[1]}_codes") for key in ((1, 0), (1, 1), (0, 1))}
        v_codes[0, 0] = held_codes[:, NQ:]
        w8 = [quantise("w0", wx[0][:].rearrange("p q t -> p (q t)"), w_codes[0])]
        v8 = {(0, 0): quantise("v0_0", vx[0, 0][:], v_codes[0, 0])}
        w8.append(quantise("w1", wx[1][:].rearrange("p q t -> p (q t)"), w_codes[1]))
        for h, b in ((1, 0), (1, 1), (0, 1)):
            v8[h, b] = quantise(f"v{h}_{b}", vx[h, b][:], v_codes[h, b])

        def weigh(acc, h, b):
            product(acc, w8[b], queries, v8[h, b])

        y0 = psum.tile([P, DV], F32, name="y_ps0", tag="score0")
        for h in range(2):
            weigh(y0[:, h * P : (h + 1) * P], h, 0)
        y0_sb = keep.tile([P, DV], F32, name="y0_sb")
        nc.scalar.activation(y0_sb[:], y0[:], ACT.Copy, scale=inv[:, 0:1])
        nc.sync.dma_start(out[0], y0_sb[:])

        y1 = {}
        for h, bank in ((1, "score1"), (0, "scales0")):
            y1[h] = psum.tile([P, P], F32, name=f"y_ps1_{h}", tag=bank)
            weigh(y1[h][:], h, 1)
        y1_sb = [keep.tile([P, P], F32, name=f"y1_sb{h}") for h in range(2)]
        nc.scalar.activation(y1_sb[1][:], y1[1][:], ACT.Copy, scale=inv[:, 1:2])
        nc.sync.dma_start(out[1, :, P:DV], y1_sb[1][:])
        nc.vector.tensor_scalar(y1_sb[0][:], y1[0][:], inv[:, 1:2], None, ALU.mult)
        nc.sync.dma_start(out[1, :, 0:P], y1_sb[0][:])
